import numpy as np
import ml_dtypes


def mxq(x, axis, fmt="e4m3"):
    dtype, down = {"e4m3": (ml_dtypes.float8_e4m3fn, 7), "e5m2": (ml_dtypes.float8_e5m2, 14)}[fmt]
    v = np.moveaxis(np.asarray(x, np.float32).astype(ml_dtypes.bfloat16).astype(np.float64), axis, -1)
    blocks = v.reshape(v.shape[:-1] + (-1, 32))
    amax = np.abs(blocks).max(-1, keepdims=True)
    byte = np.maximum(np.where(amax > 0, np.frexp(amax)[1] - 1 + 127, 0) - down, 1)
    scale = np.exp2(byte - 127.0)
    codes = (blocks / scale).astype(np.float32).astype(dtype).astype(np.float64)
    return np.moveaxis((codes * scale).reshape(v.shape), -1, axis)


WIDE = False


def mx_kscale(k):
    if not WIDE:
        return np.ones(k)
    levels = np.array([10, -10, 5, -5, 0])
    if k % 512:
        return np.exp2(np.random.permutation(np.resize(levels, k // 32))).repeat(32)
    a = np.empty((k // 512, 16))
    for p in range(k // 512):
        a[p, :8] = np.random.permutation(np.resize(levels, 8))
        for g in range(8):
            far = levels[np.abs(levels - a[p, g]) >= 10]
            a[p, g + 8] = far[np.random.randint(len(far))]
    return np.exp2(a.ravel()).repeat(32)


def f64(x):
    return np.asarray(x).astype(np.float64)


def striped(idx):
    return np.tile(idx.reshape(-1, 16).T, (8, 1)).astype(np.uint16)


def unstriped(offs):
    return offs[:16].T.reshape(-1).astype(np.int64)


E2M1 = np.array([0.0, 0.5, 1.0, 1.5, 2.0, 3.0, 4.0, 6.0, -0.0, -0.5, -1.0, -1.5, -2.0, -3.0, -4.0, -6.0])


def pack_weight(w, fmt):
    k, n = w.shape
    w = f64(np.asarray(w, np.float32).astype(ml_dtypes.bfloat16)).reshape(k // 32, 32, n)
    amax = np.abs(w).max(1)
    if fmt == "e4m3":
        byte = np.frexp(amax)[1] - 1 + 127 - 7
    else:
        mant, ex = np.frexp(amax / 6.0)
        byte = np.where(mant > 0.5, ex, ex - 1) + 127
    byte = np.clip(np.where(amax > 0, byte, 1), 1, 254)
    scaled = (w * np.exp2(127.0 - byte)[:, None, :]).reshape(k, n).astype(np.float32)
    by_word = np.ascontiguousarray(scaled.reshape(k // 512, 128, 4, n).transpose(0, 1, 3, 2))
    if fmt == "e4m3":
        words = by_word.astype(ml_dtypes.float8_e4m3fn).view(np.uint8)
    else:
        c = by_word.astype(ml_dtypes.float4_e2m1fn).view(np.uint8) & 0xF
        words = (c[..., 0::2] | (c[..., 1::2] << 4)).reshape(k // 512, 128, 2 * n)
    return np.ascontiguousarray(words), np.ascontiguousarray(byte.astype(np.uint8).reshape(k // 512, 16, n))


def unpack_weight(words, scales, fmt):
    g, _, n = scales.shape
    words = np.ascontiguousarray(words).reshape(g, 128, n, -1)
    if fmt == "e4m3":
        vals = words.view(ml_dtypes.float8_e4m3fn).astype(np.float64)
    else:
        nib = np.empty((g, 128, n, 4), np.uint8)
        nib[..., 0::2] = words & 0xF
        nib[..., 1::2] = words >> 4
        vals = E2M1[nib]
    vals = vals * np.repeat(np.exp2(scales.astype(np.float64) - 127.0), 8, axis=1)[..., None]
    return vals.transpose(0, 1, 3, 2).reshape(g * 512, n)


def gelu(v):
    return 0.5 * v * (1.0 + np.tanh(np.sqrt(2.0 / np.pi) * (v + 0.044715 * v**3)))


def striped8(idx):
    return np.concatenate([v.reshape(-1, 16).T for v in idx]).astype(np.uint16)


def unstriped8(offs):
    return np.stack([offs[16 * g:16 * g + 16].T.reshape(-1) for g in range(8)]).astype(np.int64)


def put_heads(h, wgs, idx8, t2):
    r = np.arange(h.shape[0])
    page = np.zeros((h.shape[0], t2))
    page[r[:, None], idx8[r % 512 // 64]] = wgs[r // 4 % 128] * h
    return page


K, T, S, T2, H, N = 1024, 2048, 512, 1024, 1024, 384

def setup_inputs():
    n = np.random.standard_normal
    s = mx_kscale(K)[:, None]
    u = mx_kscale(H)[:, None]
    tab_words, tab_scales = pack_weight(n((K, T)) * s, "e4m3")
    w1 = (n((K, H)) / s * u.T / np.sqrt(K)).astype(np.float32)
    w2_words, w2_scales = pack_weight(n((K, H)) / s / np.sqrt(K), "e2m1")
    w3_words, w3_scales = pack_weight(n((K, H)) / s / np.sqrt(K), "e4m3")
    w4 = (n((H, N)) / u / np.sqrt(H)).astype(np.float32)
    offs = striped(np.random.permutation(T)[:S])
    offs2 = striped8(np.stack([np.random.permutation(T2)[:S] for _ in range(8)]))
    wgs = np.repeat(np.random.uniform(0.5, 2.0, (8, S)), 16, axis=0).astype(np.float32)
    offers = (n((H, T2)) * u).astype(np.float32)
    bias = (0.5 * n(N)).astype(np.float32)
    return {"tab_words": tab_words, "tab_scales": tab_scales, "offs": offs,
            "w1": w1, "w2_words": w2_words, "w2_scales": w2_scales,
            "w3_words": w3_words, "w3_scales": w3_scales,
            "wgs": wgs, "offs2": offs2, "offers": offers, "w4": w4, "bias": bias}

def reference(tab_words, tab_scales, offs, w1, w2_words, w2_scales, w3_words, w3_scales,
              wgs, offs2, offers, w4, bias):
    v = unpack_weight(tab_words, tab_scales, "e4m3")[:, unstriped(offs)]
    w2 = unpack_weight(w2_words, w2_scales, "e2m1")
    w3 = unpack_weight(w3_words, w3_scales, "e4m3")
    a1 = mxq(f64(w1), 0, "e4m3").T @ v
    a2 = w2.T @ v
    a3 = w3.T @ v
    h = a1 * a2 * a3
    page = put_heads(h, f64(wgs), unstriped8(offs2), T2)
    z = page + f64(offers)
    y = mxq(f64(w4), 0, "e4m3").T @ mxq(z, 0, "e4m3")
    return y + f64(bias)[:, None]

@@ -1,0 +1,326 @@
+from contextlib import ExitStack
+
+import concourse.mybir as mybir
+from concourse.masks import make_identity
+
+K, T, S, T2, H, N = 1024, 2048, 512, 1024, 1024, 384
+FLOPS = 3 * 2 * K * H * S + 2 * H * N * T2
+
+F32 = mybir.dt.float32
+BF16 = mybir.dt.bfloat16
+I32 = mybir.dt.int32
+U32 = mybir.dt.uint32
+U16 = mybir.dt.uint16
+U8 = mybir.dt.uint8
+FP8X4 = mybir.dt.float8_e4m3fn_x4
+FP4X4 = mybir.dt.float4_e2m1fn_x4
+MULT = mybir.AluOpType.mult
+ADD = mybir.AluOpType.add
+IDENT = mybir.ActivationFunctionType.Identity
+
+P = 128
+PACK = 4
+PASS = P * PACK
+CHUNK = 256
+CHUNKS = T2 // CHUNK
+N_TILES = N // P
+PAGES = 4
+
+
+def tile_list_bundle_offer_scores_kernel(
+    tc, tab_words, tab_scales, offs, w1, w2_words, w2_scales, w3_words, w3_scales,
+    wgs, offs2, offers, w4, bias, out,
+):
+    nc = tc.nc
+    with ExitStack() as ctx:
+        keep = ctx.enter_context(tc.tile_pool(name="keep", bufs=1))
+        psum = ctx.enter_context(tc.psum_pool(name="psum", bufs=1))
+
+        def held(name, shape, dtype):
+            return keep.tile(shape, dtype, name=name, align_bytes=64)
+
+        banks = [psum.tile([P, PASS], F32, name=f"bank{n}") for n in range(8)]
+        a1_bank, a2_bank, a3_bank = banks[0], banks[1], banks[2]
+
+        picks = keep.tile([P, S // 16], U16, name="picks")
+        cells = keep.tile([P, S // 16], U16, name="cells")
+        tab_w = [held(f"tab_w{a}", [P, T], I32) for a in range(2)]
+        tab_s = held("tab_s", [P, 2 * T], U8)
+        w23_s = held("w23_s", [P, 2 * H], U8)
+        landing = [held(f"landing{n}", [P, PACK * PASS], F32) for n in range(2)]
+        w1_raw = [tile[:].rearrange("p (j c) -> p j c", j=PACK) for tile in landing]
+        offers_sb = [tile[:].rearrange("p (e t) -> p e t", e=2) for tile in landing]
+        w3_raw = held("w3_raw", [P, 2, PASS], I32)
+        w2_raw = held("w2_raw", [P, 2, PASS // 2], I32)
+        stage = [held(f"stage{n}", [P, 2 * PASS if n < 2 else PACK * N], F32) for n in range(4)]
+        w4_raw = [tile[:].rearrange("p (i n) -> p i n", i=PACK) for tile in stage[2:]]
+        factors = [held(f"factors{n}", [P, 2 * S], F32) for n in range(2)]
+        wgs_sb = held("wgs_sb", [P, S], F32)
+        bias_sb = held("bias_sb", [P, N_TILES], F32)
+        pages = [held(f"page{n}", [P, T2], F32) for n in range(PAGES)]
+        ident = held("ident", [P, P], F32)
+
+        nc.gpsimd.memset(tab_s[:].bitcast(I32), 0)
+        nc.vector.memset(w23_s[:].bitcast(I32), 0)
+
+        def load_scale_rows(queue, plane, first_row, scales):
+            for q in range(4):
+                rows = plane[32 * q + first_row : 32 * q + first_row + 4, :]
+                queue.dma_start(
+                    out=rows.bitcast(I32).rearrange("r (a c) -> r a c", a=2),
+                    in_=scales[:, 4 * q : 4 * q + 4, :].rearrange("a r c -> r a c").bitcast(I32),
+                )
+
+        def load_w1(b, a):
+            rows = w1[PASS * a : PASS * (a + 1), PASS * b : PASS * (b + 1)]
+            nc.sync.dma_start(out=w1_raw[a], in_=rows.rearrange("(p j) c -> p j c", j=PACK))
+
+        def load_w23(b):
+            w3_view = w3_words.rearrange("a p c i -> p a (c i)")[:, :, 4 * PASS * b : 4 * PASS * (b + 1)]
+            nc.sync.dma_start(out=w3_raw[:], in_=w3_view.bitcast(I32))
+            w2_view = w2_words.rearrange("a p c -> p a c")[:, :, 2 * PASS * b : 2 * PASS * (b + 1)]
+            nc.sync.dma_start(out=w2_raw[:], in_=w2_view.bitcast(I32))
+
+        def load_tab(a):
+            nc.sync.dma_start(out=tab_w[a][:], in_=tab_words[a].rearrange("p t i -> p (t i)").bitcast(I32))
+
+        def load_offers(b, u):
+            rows = offers[PASS * b : PASS * (b + 1), :].rearrange("(p i) t -> p i t", i=PACK)
+            nc.sync.dma_start(out=offers_sb[u], in_=rows[:, 2 * u : 2 * u + 2, :])
+
+        def load_w4(b):
+            rows = w4[PASS * b : PASS * (b + 1), :].rearrange("(p i) n -> p i n", i=PACK)
+            nc.sync.dma_start(out=w4_raw[b], in_=rows)
+
+        nc.sync.dma_start(picks[:], offs)
+        nc.sync.dma_start(cells[:], offs2)
+        with nc.allow_non_contiguous_dma(reason="one bias value for each partition and output tile"):
+            nc.sync.dma_start(out=bias_sb[:], in_=bias.rearrange("(n p) -> p n", p=P))
+        nc.sync.dma_start(out=wgs_sb[:], in_=wgs)
+        load_scale_rows(nc.gpsimd, tab_s, 0, tab_scales)
+        load_scale_rows(nc.scalar, w23_s, 0, w2_scales)
+        load_scale_rows(nc.gpsimd, w23_s, 4, w3_scales)
+        load_w1(0, 0)
+        load_tab(0)
+        load_w1(0, 1)
+        load_tab(1)
+        load_w23(0)
+
+        for page in pages:
+            nc.vector.memset(page[:], 0.0)
+        make_identity(nc, ident[:])
+
+        got_w = [held(f"got_w{a}", [P, S], U32) for a in range(2)]
+        got_s = [held(f"got_s{a}", [P, S], U8) for a in range(2)]
+
+        w1_codes = [[held(f"w1_codes{b}{a}", [P, PASS], U32) for a in range(2)] for b in range(2)]
+        w1_scales = [[held(f"w1_scales{b}{a}", [P, PASS], U8) for a in range(2)] for b in range(2)]
+        w2_codes = held("w2_codes", [P, 2, 2 * PASS], U8)
+        w3_codes = held("w3_codes", [P, 2, PASS], U32)
+        w23_planes = [held(f"w23_planes{b}", [P, 2, PASS], U8) for b in range(2)]
+
+        def order_scales(b):
+            src = w23_s[:].rearrange("p (a c) -> p a c", a=2)[:, :, PASS * b : PASS * (b + 1)]
+            nc.vector.tensor_copy(
+                out=w23_planes[b][:].rearrange("p a (i m) -> p a m i", i=PACK),
+                in_=src.rearrange("p a (m i) -> p a m i", i=PACK),
+            )
+
+        def order_words(b):
+            nc.vector.tensor_copy(
+                out=w3_codes[:].rearrange("p a (i m) -> p a m i", i=PACK),
+                in_=w3_raw[:].bitcast(U32).rearrange("p a (m i) -> p a m i", i=PACK),
+            )
+            nc.vector.tensor_copy(
+                out=w2_codes[:].bitcast(U16).rearrange("p a (i m) -> p a m i", i=PACK),
+                in_=w2_raw[:].bitcast(U16).rearrange("p a (m i) -> p a m i", i=PACK),
+            )
+
+        def quantize_w1(b, a, half, interleave):
+            grouped = stage[a][:].bitcast(BF16)[:, 2 * PASS * half : 2 * PASS * (half + 1)]
+            src = w1_raw[a].rearrange("p j (m i) -> p m j i", i=PACK)[:, :, :, 2 * half : 2 * half + 2]
+            interleave(out=grouped.rearrange("p (i m j) -> p m j i", i=2, j=PACK), in_=src)
+            cols = slice(2 * P * half, 2 * P * (half + 1))
+            nc.vector.quantize_mx(out=w1_codes[b][a][:, cols].bitcast(FP8X4), scales=w1_scales[b][a][:, cols], in_=grouped)
+
+        def scalar_cast(out, in_):
+            nc.scalar.activation(out=out, in_=in_, func=IDENT)
+
+        def gather_words(a):
+            nc.vector.tensor_copy(got_w[a][:], tab_w[a][:].bitcast(U32).indirect(picks[:]))
+
+        quantize_w1(0, 0, 0, nc.vector.tensor_copy)
+        quantize_w1(0, 0, 1, scalar_cast)
+        gather_words(0)
+        for a in range(2):
+            nc.vector.tensor_copy(got_s[a][:], tab_s[:, T * a : T * (a + 1)].indirect(picks[:]))
+        quantize_w1(0, 1, 0, nc.vector.tensor_copy)
+        order_scales(0)
+        gather_words(1)
+        order_words(0)
+        quantize_w1(0, 1, 1, scalar_cast)
+
+        def place_slice(s):
+            b, i = divmod(s, PACK)
+            cols = slice(P * i, P * (i + 1))
+
+            def product(bank, stationary):
+                for a in range(2):
+                    codes, scales = stationary(a)
+                    nc.tensor.matmul_mx(
+                        out=bank[:], lhsT=codes, lhsT_scale=scales,
+                        rhs=got_w[a][:].bitcast(FP8X4), rhs_scale=got_s[a][:],
+                        start=(a == 0), stop=(a == 1),
+                    )
+
+            product(a1_bank, lambda a: (w1_codes[b][a][:, cols].bitcast(FP8X4), w1_scales[b][a][:, cols]))
+            product(a3_bank, lambda a: (w3_codes[:, a, cols].bitcast(FP8X4), w23_planes[b][4:P, a, cols]))
+            product(a2_bank, lambda a: (w2_codes[:, a, 2 * P * i : 2 * P * (i + 1)].bitcast(FP4X4), w23_planes[b][:, a, cols]))
+            if s == PACK - 1:
+                order_words(1)
+            a3_sb = stage[s % 4][:, :S]
+            nc.scalar.copy(out=a3_sb, in_=a3_bank[:])
+            both = factors[s % 2][:]
+            a1_wgs, a2_a3 = both[:, :S], both[:, S : 2 * S]
+            nc.vector.tensor_tensor(a1_wgs, a1_bank[:], wgs_sb[:], MULT)
+            nc.vector.tensor_tensor(a2_a3, a2_bank[:], a3_sb, MULT)
+            nc.vector.tensor_tensor(pages[s % PAGES][:].indirect(cells[:]), a1_wgs, a2_a3, MULT)
+
+
+        zt_words = [[held(f"zt_words{u}{c}", [P, 2, P], F32) for c in range(CHUNKS)] for u in range(2)]
+        z_codes = [[held(f"z_codes{b}{c}", [P, CHUNK], U32) for c in range(CHUNKS)] for b in range(2)]
+        z_scales = [[held(f"z_scales{b}{c}", [P, CHUNK], U8) for c in range(CHUNKS)] for b in range(2)]
+
+        def add_offers(b, u, c, bank, copy_out):
+            blocks = [(e, tt) for e in range(2) for tt in range(2)]
+            sums = bank[:].rearrange("t (tt e p) -> t tt e p", tt=2, e=2)
+            for n, (e, tt) in enumerate(blocks):
+                t0 = CHUNK * c + P * tt
+                nc.tensor.matmul(sums[:, tt, e, :], offers_sb[u][:, e, t0 : t0 + P], ident[:],
+                                 start=(n == 0), stop=False, is_transpose=True)
+            for n, (e, tt) in enumerate(blocks):
+                t0 = CHUNK * c + P * tt
+                page = pages[(PACK * b + 2 * u + e) % PAGES]
+                nc.tensor.matmul(sums[:, tt, e, :], page[:, t0 : t0 + P], ident[:],
+                                 start=False, stop=(n == len(blocks) - 1), is_transpose=True)
+            copy_out(
+                out=zt_words[u][c][:].bitcast(BF16).rearrange("t tt (p e) -> t tt p e", e=2),
+                in_=sums.rearrange("t tt e p -> t tt p e"),
+            )
+
+        z_grouped = [held(f"z_grouped{c}", [P, CHUNK * PACK], BF16) for c in range(CHUNKS)]
+
+        def turn_back(c, bank):
+            halves = bank[:].rearrange("p (u t) -> p u t", u=2)
+            for u in range(2):
+                for tt in range(2):
+                    nc.tensor.transpose(halves[:, u, P * tt : P * (tt + 1)], zt_words[u][c][:, tt, :], ident[:])
+            nc.scalar.copy(
+                out=z_grouped[c][:].bitcast(F32).rearrange("p (t u) -> p t u", u=2),
+                in_=halves.rearrange("p u t -> p t u"),
+            )
+
+        def quantize_z(b, c):
+            nc.vector.quantize_mx(out=z_codes[b][c][:].bitcast(FP8X4), scales=z_scales[b][c][:], in_=z_grouped[c][:])
+
+        def add_offers_low_half(c, bank):
+            sums = bank[:, : 2 * P].rearrange("t (tt p) -> t tt p", tt=2)
+            page = pages[6 % PAGES]
+            for tt in range(2):
+                t0 = CHUNK * c + P * tt
+                nc.tensor.matmul(sums[:, tt, :], offers_sb[1][:, 0, t0 : t0 + P], ident[:],
+                                 start=(tt == 0), stop=False, is_transpose=True)
+            for tt in range(2):
+                t0 = CHUNK * c + P * tt
+                nc.tensor.matmul(sums[:, tt, :], page[:, t0 : t0 + P], ident[:],
+                                 start=False, stop=(tt == 1), is_transpose=True)
+            nc.scalar.copy(
+                out=zt_words[1][c][:].bitcast(BF16).rearrange("t tt (p e) -> t tt p e", e=2)[:, :, :, 0],
+                in_=sums,
+            )
+
+        w4_codes = held("w4_codes", [P, 2 * N], U32)
+        w4_scales = held("w4_scales", [P, 2 * N], U8)
+
+        def quantize_w4(b):
+            grouped = stage[b][:].bitcast(BF16)[:, : PACK * N]
+            nc.scalar.copy(
+                out=grouped.rearrange("p (c n i) -> p c i n", n=4, i=PACK),
+                in_=w4_raw[b].rearrange("p i (c n) -> p c i n", n=4),
+            )
+            for lo, hi in ((0, 2 * P), (2 * P, N)):
+                cols = slice(N * b + lo, N * b + hi)
+                nc.vector.quantize_mx(out=w4_codes[:, cols].bitcast(FP8X4), scales=w4_scales[:, cols],
+                                      in_=grouped[:, PACK * lo : PACK * hi])
+
+        results = [held(f"result{c}", [P, N_TILES, CHUNK], F32) for c in range(CHUNKS)]
+
+        def score_pass(b, c, pair):
+            slots = [pair[0][:, :CHUNK], pair[0][:, CHUNK:], pair[1][:, :CHUNK]]
+            for n in range(N_TILES):
+                cols = slice(N * b + P * n, N * b + P * (n + 1))
+                nc.tensor.matmul_mx(
+                    out=slots[n], lhsT=w4_codes[:, cols].bitcast(FP8X4), lhsT_scale=w4_scales[:, cols],
+                    rhs=z_codes[b][c][:].bitcast(FP8X4), rhs_scale=z_scales[b][c][:],
+                    start=(b == 0 and n != 1), stop=(b == 1 and n != 0),
+                )
+            return slots
+
+        def store_scores(c, slots):
+            for n in range(N_TILES):
+                nc.scalar.activation(out=results[c][:, n, :], in_=slots[n], func=IDENT, bias=bias_sb[:, n : n + 1])
+            nc.sync.dma_start(
+                out=out.rearrange("(n p) t -> p n t", p=P)[:, :, CHUNK * c : CHUNK * (c + 1)], in_=results[c][:])
+
+        sum_banks, back_banks = banks[3:5], banks[5:7]
+
+        def add_pair(b, u):
+            for c in range(CHUNKS):
+                add_offers(b, u, c, sum_banks[c % 2], nc.scalar.copy)
+
+        load_w1(1, 0)
+        load_w1(1, 1)
+        load_w23(1)
+        place_slice(0)
+        order_scales(1)
+        place_slice(1)
+        quantize_w1(1, 0, 0, scalar_cast)
+        quantize_w1(1, 0, 1, scalar_cast)
+        load_offers(0, 0)
+        place_slice(2)
+        quantize_w1(1, 1, 0, scalar_cast)
+        quantize_w1(1, 1, 1, scalar_cast)
+        load_offers(0, 1)
+        load_w4(0)
+        place_slice(3)
+        load_w4(1)
+        add_pair(0, 0)
+        load_offers(1, 0)
+        place_slice(4)
+        place_slice(5)
+        add_pair(0, 1)
+        load_offers(1, 1)
+        quantize_w4(0)
+        for c in range(CHUNKS):
+            turn_back(c, back_banks[c % 2])
+            quantize_z(0, c)
+        place_slice(6)
+        quantize_w4(1)
+        place_slice(7)
+        add_pair(1, 0)
+        for c in range(CHUNKS):
+            add_offers_low_half(c, sum_banks[c % 2])
+            turn_back(c, back_banks[c % 2])
+        score_banks = [(banks[7], banks[2]), (banks[0], banks[1]), sum_banks, back_banks]
+        for c in range(CHUNKS):
+            score_pass(0, c, score_banks[c])
+        for c in range(CHUNKS):
+            cols = slice(CHUNK * c, CHUNK * (c + 1))
+            nc.vector.tensor_tensor(
+                z_grouped[c][:].rearrange("p (t i) -> p t i", i=PACK)[:, :, PACK - 1],
+                pages[7 % PAGES][:, cols], offers_sb[1][:, 1, cols], ADD)
+            if c > 0:
+                quantize_z(1, c - 1)
+                store_scores(c - 1, score_pass(1, c - 1, score_banks[c - 1]))
+        quantize_z(1, CHUNKS - 1)
+        store_scores(CHUNKS - 1, score_pass(1, CHUNKS - 1, score_banks[CHUNKS - 1]))

@@ -1,4 +1,5 @@
 from contextlib import ExitStack
+from functools import partial
 
 import concourse.mybir as mybir
 from concourse.masks import make_identity
@@ -39,28 +40,25 @@ def tile_list_bundle_offer_scores_kernel(
         def held(name, shape, dtype):
             return keep.tile(shape, dtype, name=name, align_bytes=64)
 
+        def tenant(slot, name, shape, dtype):
+            return keep.tile(shape, dtype, name=name, tag=slot, align_bytes=64)
+
         banks = [psum.tile([P, PASS], F32, name=f"bank{n}") for n in range(8)]
-        a1_bank, a2_bank, a3_bank = banks[0], banks[1], banks[2]
+        a1_banks, a2_banks, a3_bank, turn_banks = banks[0:2], banks[2:4], banks[4], banks[5:8]
 
         picks = keep.tile([P, S // 16], U16, name="picks")
         cells = keep.tile([P, S // 16], U16, name="cells")
-        tab_w = [held(f"tab_w{a}", [P, T], I32) for a in range(2)]
         tab_s = held("tab_s", [P, 2 * T], U8)
-        w23_s = held("w23_s", [P, 2 * H], U8)
-        landing = [held(f"landing{n}", [P, PACK * PASS], F32) for n in range(2)]
-        w1_raw = [tile[:].rearrange("p (j c) -> p j c", j=PACK) for tile in landing]
-        offers_sb = [tile[:].rearrange("p (e t) -> p e t", e=2) for tile in landing]
-        w3_raw = held("w3_raw", [P, 2, PASS], I32)
-        w2_raw = held("w2_raw", [P, 2, PASS // 2], I32)
+        w23_s = tenant("late_words", "w23_s", [P, 2 * H], U8)
+        tab_w, w1_raw, offers_sb, w2_raw, w3_raw = {}, {}, {}, {}, {}
         stage = [held(f"stage{n}", [P, 2 * PASS if n < 2 else PACK * N], F32) for n in range(4)]
         w4_raw = [tile[:].rearrange("p (i n) -> p i n", i=PACK) for tile in stage[2:]]
         factors = [held(f"factors{n}", [P, 2 * S], F32) for n in range(2)]
         wgs_sb = held("wgs_sb", [P, S], F32)
-        bias_sb = held("bias_sb", [P, N_TILES], F32)
         pages = [held(f"page{n}", [P, T2], F32) for n in range(PAGES)]
         ident = held("ident", [P, P], F32)
 
-        nc.gpsimd.memset(tab_s[:].bitcast(I32), 0)
+        nc.vector.memset(tab_s[:].bitcast(I32), 0)
         nc.vector.memset(w23_s[:].bitcast(I32), 0)
 
         def load_scale_rows(queue, plane, first_row, scales):
@@ -71,40 +69,43 @@ def tile_list_bundle_offer_scores_kernel(
                     in_=scales[:, 4 * q : 4 * q + 4, :].rearrange("a r c -> r a c").bitcast(I32),
                 )
 
-        def load_w1(b, a):
+        def load_w1(b, a, slot):
             rows = w1[PASS * a : PASS * (a + 1), PASS * b : PASS * (b + 1)]
-            nc.sync.dma_start(out=w1_raw[a], in_=rows.rearrange("(p j) c -> p j c", j=PACK))
+            w1_raw[b, a] = tenant(slot, f"w1_raw{b}{a}", [P, PACK, PASS], F32)
+            nc.sync.dma_start(out=w1_raw[b, a][:], in_=rows.rearrange("(p j) c -> p j c", j=PACK))
 
         def load_w23(b):
-            w3_view = w3_words.rearrange("a p c i -> p a (c i)")[:, :, 4 * PASS * b : 4 * PASS * (b + 1)]
-            nc.sync.dma_start(out=w3_raw[:], in_=w3_view.bitcast(I32))
+            raw = tenant("late_words" if b else "early_words", f"w23_raw{b}", [P, 3 * PASS], I32)
+            w2_raw[b] = raw[:, :PASS].rearrange("p (a c) -> p a c", a=2)
+            w3_raw[b] = raw[:, PASS:].rearrange("p (a c) -> p a c", a=2)
             w2_view = w2_words.rearrange("a p c -> p a c")[:, :, 2 * PASS * b : 2 * PASS * (b + 1)]
-            nc.sync.dma_start(out=w2_raw[:], in_=w2_view.bitcast(I32))
+            nc.sync.dma_start(out=w2_raw[b], in_=w2_view.bitcast(I32))
+            w3_view = w3_words.rearrange("a p c i -> p a (c i)")[:, :, 4 * PASS * b : 4 * PASS * (b + 1)]
+            nc.sync.dma_start(out=w3_raw[b], in_=w3_view.bitcast(I32))
 
-        def load_tab(a):
+        def load_tab(a, slot):
+            tab_w[a] = tenant(slot, f"tab_w{a}", [P, T], I32)
             nc.sync.dma_start(out=tab_w[a][:], in_=tab_words[a].rearrange("p t i -> p (t i)").bitcast(I32))
 
-        def load_offers(b, u):
+        def load_offers(b, u, slot):
             rows = offers[PASS * b : PASS * (b + 1), :].rearrange("(p i) t -> p i t", i=PACK)
-            nc.sync.dma_start(out=offers_sb[u], in_=rows[:, 2 * u : 2 * u + 2, :])
+            offers_sb[b, u] = tenant(slot, f"offers{b}{u}", [P, 2, T2], F32)
+            nc.sync.dma_start(out=offers_sb[b, u][:], in_=rows[:, 2 * u : 2 * u + 2, :])
 
         def load_w4(b):
             rows = w4[PASS * b : PASS * (b + 1), :].rearrange("(p i) n -> p i n", i=PACK)
             nc.sync.dma_start(out=w4_raw[b], in_=rows)
 
         nc.sync.dma_start(picks[:], offs)
-        nc.sync.dma_start(cells[:], offs2)
-        with nc.allow_non_contiguous_dma(reason="one bias value for each partition and output tile"):
-            nc.sync.dma_start(out=bias_sb[:], in_=bias.rearrange("(n p) -> p n", p=P))
+        load_tab(0, "landing0")
+        load_w23(0)
+        load_w1(0, 0, "landing1")
+        load_tab(1, "landing2")
         nc.sync.dma_start(out=wgs_sb[:], in_=wgs)
-        load_scale_rows(nc.gpsimd, tab_s, 0, tab_scales)
+        nc.sync.dma_start(cells[:], offs2)
+        load_scale_rows(nc.scalar, tab_s, 0, tab_scales)
         load_scale_rows(nc.scalar, w23_s, 0, w2_scales)
         load_scale_rows(nc.gpsimd, w23_s, 4, w3_scales)
-        load_w1(0, 0)
-        load_tab(0)
-        load_w1(0, 1)
-        load_tab(1)
-        load_w23(0)
 
         for page in pages:
             nc.vector.memset(page[:], 0.0)
@@ -122,23 +123,23 @@ def tile_list_bundle_offer_scores_kernel(
         def order_scales(b):
             src = w23_s[:].rearrange("p (a c) -> p a c", a=2)[:, :, PASS * b : PASS * (b + 1)]
             nc.vector.tensor_copy(
-                out=w23_planes[b][:].rearrange("p a (i m) -> p a m i", i=PACK),
-                in_=src.rearrange("p a (m i) -> p a m i", i=PACK),
+                out=w23_planes[b][:].rearrange("p a (i m) -> p a i m", i=PACK),
+                in_=src.rearrange("p a (m i) -> p a i m", i=PACK),
             )
 
         def order_words(b):
             nc.vector.tensor_copy(
                 out=w3_codes[:].rearrange("p a (i m) -> p a m i", i=PACK),
-                in_=w3_raw[:].bitcast(U32).rearrange("p a (m i) -> p a m i", i=PACK),
+                in_=w3_raw[b].bitcast(U32).rearrange("p a (m i) -> p a m i", i=PACK),
             )
             nc.vector.tensor_copy(
-                out=w2_codes[:].bitcast(U16).rearrange("p a (i m) -> p a m i", i=PACK),
-                in_=w2_raw[:].bitcast(U16).rearrange("p a (m i) -> p a m i", i=PACK),
+                out=w2_codes[:].bitcast(U16).rearrange("p a (i m) -> p a i m", i=PACK),
+                in_=w2_raw[b].bitcast(U16).rearrange("p a (m i) -> p a i m", i=PACK),
             )
 
         def quantize_w1(b, a, half, interleave):
             grouped = stage[a][:].bitcast(BF16)[:, 2 * PASS * half : 2 * PASS * (half + 1)]
-            src = w1_raw[a].rearrange("p j (m i) -> p m j i", i=PACK)[:, :, :, 2 * half : 2 * half + 2]
+            src = w1_raw[b, a][:].rearrange("p j (m i) -> p m j i", i=PACK)[:, :, :, 2 * half : 2 * half + 2]
             interleave(out=grouped.rearrange("p (i m j) -> p m j i", i=2, j=PACK), in_=src)
             cols = slice(2 * P * half, 2 * P * (half + 1))
             nc.vector.quantize_mx(out=w1_codes[b][a][:, cols].bitcast(FP8X4), scales=w1_scales[b][a][:, cols], in_=grouped)
@@ -149,69 +150,80 @@ def tile_list_bundle_offer_scores_kernel(
         def gather_words(a):
             nc.vector.tensor_copy(got_w[a][:], tab_w[a][:].bitcast(U32).indirect(picks[:]))
 
-        quantize_w1(0, 0, 0, nc.vector.tensor_copy)
-        quantize_w1(0, 0, 1, scalar_cast)
         gather_words(0)
+        load_w1(0, 1, "landing0")
+        order_words(0)
         for a in range(2):
             nc.vector.tensor_copy(got_s[a][:], tab_s[:, T * a : T * (a + 1)].indirect(picks[:]))
-        quantize_w1(0, 1, 0, nc.vector.tensor_copy)
-        order_scales(0)
+        quantize_w1(0, 0, 0, nc.vector.tensor_copy)
         gather_words(1)
-        order_words(0)
-        quantize_w1(0, 1, 1, scalar_cast)
+        load_w1(1, 0, "landing2")
+        order_scales(0)
+        quantize_w1(0, 1, 0, nc.vector.tensor_copy)
 
-        def place_slice(s):
+        def product(bank, stationary):
+            for a in range(2):
+                codes, scales = stationary(a)
+                nc.tensor.matmul_mx(
+                    out=bank[:], lhsT=codes, lhsT_scale=scales,
+                    rhs=got_w[a][:].bitcast(FP8X4), rhs_scale=got_s[a][:],
+                    start=(a == 0), stop=(a == 1),
+                )
+
+        def affinity1(s):
             b, i = divmod(s, PACK)
             cols = slice(P * i, P * (i + 1))
+            product(a1_banks[s % 2], lambda a: (w1_codes[b][a][:, cols].bitcast(FP8X4), w1_scales[b][a][:, cols]))
 
-            def product(bank, stationary):
-                for a in range(2):
-                    codes, scales = stationary(a)
-                    nc.tensor.matmul_mx(
-                        out=bank[:], lhsT=codes, lhsT_scale=scales,
-                        rhs=got_w[a][:].bitcast(FP8X4), rhs_scale=got_s[a][:],
-                        start=(a == 0), stop=(a == 1),
-                    )
+        def affinity2(s):
+            b, i = divmod(s, PACK)
+            cols, code_cols = slice(P * i, P * (i + 1)), slice(2 * P * i, 2 * P * (i + 1))
+            product(a2_banks[s % 2], lambda a: (w2_codes[:, a, code_cols].bitcast(FP4X4), w23_planes[b][:, a, cols]))
 
-            product(a1_bank, lambda a: (w1_codes[b][a][:, cols].bitcast(FP8X4), w1_scales[b][a][:, cols]))
+        def affinity3(s):
+            b, i = divmod(s, PACK)
+            cols = slice(P * i, P * (i + 1))
             product(a3_bank, lambda a: (w3_codes[:, a, cols].bitcast(FP8X4), w23_planes[b][4:P, a, cols]))
-            product(a2_bank, lambda a: (w2_codes[:, a, 2 * P * i : 2 * P * (i + 1)].bitcast(FP4X4), w23_planes[b][:, a, cols]))
-            if s == PACK - 1:
-                order_words(1)
-            a3_sb = stage[s % 4][:, :S]
-            nc.scalar.copy(out=a3_sb, in_=a3_bank[:])
-            both = factors[s % 2][:]
-            a1_wgs, a2_a3 = both[:, :S], both[:, S : 2 * S]
-            nc.vector.tensor_tensor(a1_wgs, a1_bank[:], wgs_sb[:], MULT)
-            nc.vector.tensor_tensor(a2_a3, a2_bank[:], a3_sb, MULT)
-            nc.vector.tensor_tensor(pages[s % PAGES][:].indirect(cells[:]), a1_wgs, a2_a3, MULT)
+            nc.scalar.copy(out=stage[s % 4][:, :S], in_=a3_bank[:])
 
+        def place(s):
+            a1_wgs, a2_a3 = factors[s % 2][:, :S], factors[s % 2][:, S:]
+            nc.vector.tensor_tensor(a2_a3, a2_banks[s % 2][:], stage[s % 4][:, :S], MULT)
+            nc.vector.tensor_tensor(a1_wgs, a1_banks[s % 2][:], wgs_sb[:], MULT)
+            nc.vector.tensor_tensor(pages[s % PAGES][:].indirect(cells[:]), a1_wgs, a2_a3, MULT)
 
         zt_words = [[held(f"zt_words{u}{c}", [P, 2, P], F32) for c in range(CHUNKS)] for u in range(2)]
         z_codes = [[held(f"z_codes{b}{c}", [P, CHUNK], U32) for c in range(CHUNKS)] for b in range(2)]
         z_scales = [[held(f"z_scales{b}{c}", [P, CHUNK], U8) for c in range(CHUNKS)] for b in range(2)]
 
-        def add_offers(b, u, c, bank, copy_out):
+        turns = []
+
+        def next_turn_bank():
+            turns.append(turn_banks[len(turns) % len(turn_banks)])
+            return turns[-1]
+
+        def add_offers(b, u, c):
+            bank = next_turn_bank()
             blocks = [(e, tt) for e in range(2) for tt in range(2)]
             sums = bank[:].rearrange("t (tt e p) -> t tt e p", tt=2, e=2)
             for n, (e, tt) in enumerate(blocks):
                 t0 = CHUNK * c + P * tt
-                nc.tensor.matmul(sums[:, tt, e, :], offers_sb[u][:, e, t0 : t0 + P], ident[:],
+                nc.tensor.matmul(sums[:, tt, e, :], offers_sb[b, u][:, e, t0 : t0 + P], ident[:],
                                  start=(n == 0), stop=False, is_transpose=True)
             for n, (e, tt) in enumerate(blocks):
                 t0 = CHUNK * c + P * tt
                 page = pages[(PACK * b + 2 * u + e) % PAGES]
                 nc.tensor.matmul(sums[:, tt, e, :], page[:, t0 : t0 + P], ident[:],
                                  start=False, stop=(n == len(blocks) - 1), is_transpose=True)
-            copy_out(
+            nc.scalar.copy(
                 out=zt_words[u][c][:].bitcast(BF16).rearrange("t tt (p e) -> t tt p e", e=2),
                 in_=sums.rearrange("t tt e p -> t tt p e"),
             )
 
         z_grouped = [held(f"z_grouped{c}", [P, CHUNK * PACK], BF16) for c in range(CHUNKS)]
 
-        def turn_back(c, bank):
-            halves = bank[:].rearrange("p (u t) -> p u t", u=2)
+        def turn_back(c):
+            halves = next_turn_bank()[:].rearrange("p (u t) -> p u t", u=2)
             for u in range(2):
                 for tt in range(2):
                     nc.tensor.transpose(halves[:, u, P * tt : P * (tt + 1)], zt_words[u][c][:, tt, :], ident[:])
@@ -223,12 +235,12 @@ def tile_list_bundle_offer_scores_kernel(
         def quantize_z(b, c):
             nc.vector.quantize_mx(out=z_codes[b][c][:].bitcast(FP8X4), scales=z_scales[b][c][:], in_=z_grouped[c][:])
 
-        def add_offers_low_half(c, bank):
-            sums = bank[:, : 2 * P].rearrange("t (tt p) -> t tt p", tt=2)
+        def add_offers_low_half(c):
+            sums = next_turn_bank()[:, : 2 * P].rearrange("t (tt p) -> t tt p", tt=2)
             page = pages[6 % PAGES]
             for tt in range(2):
                 t0 = CHUNK * c + P * tt
-                nc.tensor.matmul(sums[:, tt, :], offers_sb[1][:, 0, t0 : t0 + P], ident[:],
+                nc.tensor.matmul(sums[:, tt, :], offers_sb[1, 1][:, 0, t0 : t0 + P], ident[:],
                                  start=(tt == 0), stop=False, is_transpose=True)
             for tt in range(2):
                 t0 = CHUNK * c + P * tt
@@ -243,7 +255,7 @@ def tile_list_bundle_offer_scores_kernel(
         w4_scales = held("w4_scales", [P, 2 * N], U8)
 
         def quantize_w4(b):
-            grouped = stage[b][:].bitcast(BF16)[:, : PACK * N]
+            grouped = held(f"w4_grouped{b}", [P, PACK * N], BF16)[:]
             nc.scalar.copy(
                 out=grouped.rearrange("p (c n i) -> p c i n", n=4, i=PACK),
                 in_=w4_raw[b].rearrange("p i (c n) -> p c i n", n=4),
@@ -268,57 +280,77 @@ def tile_list_bundle_offer_scores_kernel(
 
         def store_scores(c, slots):
             for n in range(N_TILES):
-                nc.scalar.activation(out=results[c][:, n, :], in_=slots[n], func=IDENT, bias=bias_sb[:, n : n + 1])
+                if c == CHUNKS - 1 and n == N_TILES - 1:
+                    nc.vector.tensor_scalar_add(results[c][:, n, :], slots[n], bias_sb[:, n : n + 1])
+                else:
+                    nc.scalar.activation(out=results[c][:, n, :], in_=slots[n], func=IDENT, bias=bias_sb[:, n : n + 1])
             nc.sync.dma_start(
                 out=out.rearrange("(n p) t -> p n t", p=P)[:, :, CHUNK * c : CHUNK * (c + 1)], in_=results[c][:])
 
-        sum_banks, back_banks = banks[3:5], banks[5:7]
+        def step(s, turned=()):
+            jobs = list(turned)
+            half = (len(jobs) + 1) // 2
+            for job in jobs[:half]:
+                job()
+            affinity1(s)
+            for job in jobs[half:]:
+                job()
+            place(s)
+            if s + 1 < 2 * PACK:
+                affinity3(s + 1)
+                affinity2(s + 1)
 
-        def add_pair(b, u):
-            for c in range(CHUNKS):
-                add_offers(b, u, c, sum_banks[c % 2], nc.scalar.copy)
+        def back_and_quantize(c):
+            turn_back(c)
+            quantize_z(0, c)
 
-        load_w1(1, 0)
-        load_w1(1, 1)
-        load_w23(1)
-        place_slice(0)
+        affinity3(0)
+        affinity2(0)
+        step(0)
+        quantize_w1(0, 0, 1, nc.scalar.copy)
+        load_w1(1, 1, "landing1")
+        quantize_w1(0, 1, 1, nc.scalar.copy)
+        load_offers(0, 0, "landing0")
         order_scales(1)
-        place_slice(1)
+        load_w23(1)
+        step(1)
         quantize_w1(1, 0, 0, scalar_cast)
         quantize_w1(1, 0, 1, scalar_cast)
-        load_offers(0, 0)
-        place_slice(2)
+        load_offers(0, 1, "landing2")
+        step(2)
+        order_words(1)
+        bias_sb = tenant("late_words", "bias_sb", [P, N_TILES], F32)
+        with nc.allow_non_contiguous_dma(reason="one bias value for each partition and output tile"):
+            nc.sync.dma_start(out=bias_sb[:], in_=bias.rearrange("(n p) -> p n", p=P))
         quantize_w1(1, 1, 0, scalar_cast)
         quantize_w1(1, 1, 1, scalar_cast)
-        load_offers(0, 1)
+        load_offers(1, 0, "landing1")
         load_w4(0)
-        place_slice(3)
+        step(3, [partial(add_offers, 0, 0, c) for c in (0, 1)])
         load_w4(1)
-        add_pair(0, 0)
-        load_offers(1, 0)
-        place_slice(4)
-        place_slice(5)
-        add_pair(0, 1)
-        load_offers(1, 1)
         quantize_w4(0)
-        for c in range(CHUNKS):
-            turn_back(c, back_banks[c % 2])
-            quantize_z(0, c)
-        place_slice(6)
+        step(4, [partial(add_offers, 0, 0, c) for c in (2, 3)])
+        load_offers(1, 1, "landing0")
+        step(5, [partial(add_offers, 0, 1, c) for c in range(CHUNKS)])
         quantize_w4(1)
-        place_slice(7)
-        add_pair(1, 0)
+        step(6, [partial(back_and_quantize, c) for c in range(CHUNKS)])
+        step(7, [partial(add_offers, 1, 0, c) for c in range(CHUNKS)])
+        score_banks = [(a1_banks[0], a2_banks[0]), (a1_banks[1], a2_banks[1]),
+                       (a3_bank, turn_banks[1]), (turn_banks[2], turn_banks[0])]
         for c in range(CHUNKS):
-            add_offers_low_half(c, sum_banks[c % 2])
-            turn_back(c, back_banks[c % 2])
-        score_banks = [(banks[7], banks[2]), (banks[0], banks[1]), sum_banks, back_banks]
-        for c in range(CHUNKS):
+            add_offers_low_half(c)
+            if c > 0:
+                turn_back(c - 1)
+            if c < 2:
+                score_pass(0, c, score_banks[c])
+        turn_back(CHUNKS - 1)
+        for c in range(2, CHUNKS):
             score_pass(0, c, score_banks[c])
         for c in range(CHUNKS):
             cols = slice(CHUNK * c, CHUNK * (c + 1))
             nc.vector.tensor_tensor(
                 z_grouped[c][:].rearrange("p (t i) -> p t i", i=PACK)[:, :, PACK - 1],
-                pages[7 % PAGES][:, cols], offers_sb[1][:, 1, cols], ADD)
+                pages[7 % PAGES][:, cols], offers_sb[1, 1][:, 1, cols], ADD)
             if c > 0:
                 quantize_z(1, c - 1)
                 store_scores(c - 1, score_pass(1, c - 1, score_banks[c - 1]))

@@ -1,5 +1,4 @@
 from contextlib import ExitStack
-from functools import partial
 
 import concourse.mybir as mybir
 from concourse.masks import make_identity
@@ -18,14 +17,19 @@ FP4X4 = mybir.dt.float4_e2m1fn_x4
 MULT = mybir.AluOpType.mult
 ADD = mybir.AluOpType.add
 IDENT = mybir.ActivationFunctionType.Identity
+COPY = mybir.ActivationFunctionType.Copy
 
 P = 128
 PACK = 4
 PASS = P * PACK
+GROUPS = 8
+GROUP_ROWS = P // GROUPS
+J_TILES = S // P
 CHUNK = 256
 CHUNKS = T2 // CHUNK
 N_TILES = N // P
-PAGES = 4
+SLICES = 2 * PACK
+PAGES = 6
 
 
 def tile_list_bundle_offer_scores_kernel(
@@ -44,21 +48,20 @@ def tile_list_bundle_offer_scores_kernel(
             return keep.tile(shape, dtype, name=name, tag=slot, align_bytes=64)
 
         banks = [psum.tile([P, PASS], F32, name=f"bank{n}") for n in range(8)]
-        a1_banks, a2_banks, a3_bank, turn_banks = banks[0:2], banks[2:4], banks[4], banks[5:8]
 
         picks = keep.tile([P, S // 16], U16, name="picks")
         cells = keep.tile([P, S // 16], U16, name="cells")
-        tab_s = held("tab_s", [P, 2 * T], U8)
-        w23_s = tenant("late_words", "w23_s", [P, 2 * H], U8)
-        tab_w, w1_raw, offers_sb, w2_raw, w3_raw = {}, {}, {}, {}, {}
-        stage = [held(f"stage{n}", [P, 2 * PASS if n < 2 else PACK * N], F32) for n in range(4)]
-        w4_raw = [tile[:].rearrange("p (i n) -> p i n", i=PACK) for tile in stage[2:]]
-        factors = [held(f"factors{n}", [P, 2 * S], F32) for n in range(2)]
-        wgs_sb = held("wgs_sb", [P, S], F32)
-        pages = [held(f"page{n}", [P, T2], F32) for n in range(PAGES)]
+        tab_s = tenant("space_a", "tab_s", [P, 2 * T], U8)
+        w23_s = held("w23_s", [P, 2 * H], U8)
+        wgs_rows = tenant("space_w", "wgs_rows", [P, S], F32)
+        wgs_cols = held("wgs_cols", [P, J_TILES, GROUPS], F32)
+        pages = [held(f"page{s}", [P, T2], F32) for s in range(PAGES)]
         ident = held("ident", [P, P], F32)
+        tab_w, w1_raw, offers_sb, w2_w, w3_w, w4_raw = {}, {}, {}, {}, {}, {}
 
-        nc.vector.memset(tab_s[:].bitcast(I32), 0)
+        nc.gpsimd.memset(tab_s[:].bitcast(I32), 0)
+        make_identity(nc, ident[:])
+        nc.vector.memset(wgs_rows[:], 0.0)
         nc.vector.memset(w23_s[:].bitcast(I32), 0)
 
         def load_scale_rows(queue, plane, first_row, scales):
@@ -69,201 +72,185 @@ def tile_list_bundle_offer_scores_kernel(
                     in_=scales[:, 4 * q : 4 * q + 4, :].rearrange("a r c -> r a c").bitcast(I32),
                 )
 
+        def load_tab(a, slot):
+            tab_w[a] = tenant(slot, f"tab_w{a}", [P, T], I32)
+            nc.sync.dma_start(out=tab_w[a][:], in_=tab_words[a].rearrange("p t i -> p (t i)").bitcast(I32))
+
         def load_w1(b, a, slot):
             rows = w1[PASS * a : PASS * (a + 1), PASS * b : PASS * (b + 1)]
             w1_raw[b, a] = tenant(slot, f"w1_raw{b}{a}", [P, PACK, PASS], F32)
             nc.sync.dma_start(out=w1_raw[b, a][:], in_=rows.rearrange("(p j) c -> p j c", j=PACK))
 
-        def load_w23(b):
-            raw = tenant("late_words" if b else "early_words", f"w23_raw{b}", [P, 3 * PASS], I32)
-            w2_raw[b] = raw[:, :PASS].rearrange("p (a c) -> p a c", a=2)
-            w3_raw[b] = raw[:, PASS:].rearrange("p (a c) -> p a c", a=2)
-            w2_view = w2_words.rearrange("a p c -> p a c")[:, :, 2 * PASS * b : 2 * PASS * (b + 1)]
-            nc.sync.dma_start(out=w2_raw[b], in_=w2_view.bitcast(I32))
-            w3_view = w3_words.rearrange("a p c i -> p a (c i)")[:, :, 4 * PASS * b : 4 * PASS * (b + 1)]
-            nc.sync.dma_start(out=w3_raw[b], in_=w3_view.bitcast(I32))
+        def load_w2(b, dest):
+            w2_w[b] = dest.rearrange("p (a c) -> p a c", a=2)
+            view = w2_words.rearrange("a p c -> p a c")[:, :, 2 * PASS * b : 2 * PASS * (b + 1)]
+            nc.sync.dma_start(out=w2_w[b], in_=view.bitcast(I32))
 
-        def load_tab(a, slot):
-            tab_w[a] = tenant(slot, f"tab_w{a}", [P, T], I32)
-            nc.sync.dma_start(out=tab_w[a][:], in_=tab_words[a].rearrange("p t i -> p (t i)").bitcast(I32))
+        def load_w3(b, dest):
+            w3_w[b] = dest.rearrange("p (a c) -> p a c", a=2)
+            view = w3_words.rearrange("a p c i -> p a (c i)")[:, :, 4 * PASS * b : 4 * PASS * (b + 1)]
+            nc.sync.dma_start(out=w3_w[b], in_=view.bitcast(I32))
 
         def load_offers(b, u, slot):
             rows = offers[PASS * b : PASS * (b + 1), :].rearrange("(p i) t -> p i t", i=PACK)
             offers_sb[b, u] = tenant(slot, f"offers{b}{u}", [P, 2, T2], F32)
             nc.sync.dma_start(out=offers_sb[b, u][:], in_=rows[:, 2 * u : 2 * u + 2, :])
 
-        def load_w4(b):
+        def load_w4(b, slot):
             rows = w4[PASS * b : PASS * (b + 1), :].rearrange("(p i) n -> p i n", i=PACK)
-            nc.sync.dma_start(out=w4_raw[b], in_=rows)
+            w4_raw[b] = tenant(slot, f"w4_raw{b}", [P, PACK, N], F32)
+            nc.sync.dma_start(out=w4_raw[b][:], in_=rows)
 
         nc.sync.dma_start(picks[:], offs)
-        load_tab(0, "landing0")
-        load_w23(0)
-        load_w1(0, 0, "landing1")
-        load_tab(1, "landing2")
-        nc.sync.dma_start(out=wgs_sb[:], in_=wgs)
+        load_tab(0, "space_b")
+        load_tab(1, "space_c")
+        load_w3(0, tenant("space_e", "w3_w0", [P, 2 * PASS], I32)[:])
         nc.sync.dma_start(cells[:], offs2)
         load_scale_rows(nc.scalar, tab_s, 0, tab_scales)
-        load_scale_rows(nc.scalar, w23_s, 0, w2_scales)
-        load_scale_rows(nc.gpsimd, w23_s, 4, w3_scales)
-
-        for page in pages:
-            nc.vector.memset(page[:], 0.0)
-        make_identity(nc, ident[:])
+        load_scale_rows(nc.scalar, w23_s, 4, w3_scales)
+        nc.gpsimd.dma_start(out=wgs_rows[0:GROUPS, :], in_=wgs[0:P:GROUP_ROWS, :])
+        load_scale_rows(nc.gpsimd, w23_s, 0, w2_scales)
 
         got_w = [held(f"got_w{a}", [P, S], U32) for a in range(2)]
         got_s = [held(f"got_s{a}", [P, S], U8) for a in range(2)]
 
-        w1_codes = [[held(f"w1_codes{b}{a}", [P, PASS], U32) for a in range(2)] for b in range(2)]
-        w1_scales = [[held(f"w1_scales{b}{a}", [P, PASS], U8) for a in range(2)] for b in range(2)]
-        w2_codes = held("w2_codes", [P, 2, 2 * PASS], U8)
-        w3_codes = held("w3_codes", [P, 2, PASS], U32)
-        w23_planes = [held(f"w23_planes{b}", [P, 2, PASS], U8) for b in range(2)]
-
-        def order_scales(b):
-            src = w23_s[:].rearrange("p (a c) -> p a c", a=2)[:, :, PASS * b : PASS * (b + 1)]
-            nc.vector.tensor_copy(
-                out=w23_planes[b][:].rearrange("p a (i m) -> p a i m", i=PACK),
-                in_=src.rearrange("p a (m i) -> p a i m", i=PACK),
-            )
-
-        def order_words(b):
-            nc.vector.tensor_copy(
-                out=w3_codes[:].rearrange("p a (i m) -> p a m i", i=PACK),
-                in_=w3_raw[b].bitcast(U32).rearrange("p a (m i) -> p a m i", i=PACK),
-            )
-            nc.vector.tensor_copy(
-                out=w2_codes[:].bitcast(U16).rearrange("p a (i m) -> p a i m", i=PACK),
-                in_=w2_raw[b].bitcast(U16).rearrange("p a (m i) -> p a i m", i=PACK),
-            )
-
-        def quantize_w1(b, a, half, interleave):
-            grouped = stage[a][:].bitcast(BF16)[:, 2 * PASS * half : 2 * PASS * (half + 1)]
-            src = w1_raw[b, a][:].rearrange("p j (m i) -> p m j i", i=PACK)[:, :, :, 2 * half : 2 * half + 2]
-            interleave(out=grouped.rearrange("p (i m j) -> p m j i", i=2, j=PACK), in_=src)
-            cols = slice(2 * P * half, 2 * P * (half + 1))
-            nc.vector.quantize_mx(out=w1_codes[b][a][:, cols].bitcast(FP8X4), scales=w1_scales[b][a][:, cols], in_=grouped)
-
-        def scalar_cast(out, in_):
-            nc.scalar.activation(out=out, in_=in_, func=IDENT)
-
-        def gather_words(a):
-            nc.vector.tensor_copy(got_w[a][:], tab_w[a][:].bitcast(U32).indirect(picks[:]))
-
-        gather_words(0)
-        load_w1(0, 1, "landing0")
-        order_words(0)
         for a in range(2):
             nc.vector.tensor_copy(got_s[a][:], tab_s[:, T * a : T * (a + 1)].indirect(picks[:]))
-        quantize_w1(0, 0, 0, nc.vector.tensor_copy)
-        gather_words(1)
-        load_w1(1, 0, "landing2")
-        order_scales(0)
-        quantize_w1(0, 1, 0, nc.vector.tensor_copy)
+        for a in range(2):
+            nc.vector.tensor_copy(got_w[a][:], tab_w[a][:].bitcast(U32).indirect(picks[:]))
+        load_w2(0, tenant("space_b", "w2_w0", [P, PASS], I32)[:])
+        load_w1(0, 0, "space_c")
+        load_w1(0, 1, "space_a")
+        for page in pages[:4]:
+            nc.vector.memset(page[:], 0.0)
+        for page in pages[4:]:
+            nc.gpsimd.memset(page[:], 0.0)
 
-        def product(bank, stationary):
+        for jt in range(J_TILES):
+            nc.tensor.transpose(banks[7][:, P * jt : P * (jt + 1)], wgs_rows[:, P * jt : P * (jt + 1)], ident[:])
+        nc.scalar.activation(
+            out=wgs_cols[:], in_=banks[7][:].rearrange("j (jt r) -> j jt r", jt=J_TILES)[:, :, :GROUPS], func=COPY)
+
+        w1_codes = [[held(f"w1_codes{b}{a}", [P, PASS], U32) for a in range(2)] for b in range(2)]
+        w1_scales = [[held(f"w1_scales{b}{a}", [P, PASS], U8) for a in range(2)] for b in range(2)]
+        w1_grouped = {}
+
+        def cast_w1(b, a, half, cast, slot):
+            w1_grouped[b, a, half] = tenant(slot, f"w1_grouped{b}{a}{half}", [P, 2 * PASS], BF16)
+            src = w1_raw[b, a][:].rearrange("p j (m i) -> p m j i", i=PACK)[:, :, :, 2 * half : 2 * half + 2]
+            cast(out=w1_grouped[b, a, half][:].rearrange("p (i m j) -> p m j i", i=2, j=PACK), in_=src)
+            cols = slice(2 * P * half, 2 * P * (half + 1))
+            nc.vector.quantize_mx(out=w1_codes[b][a][:, cols].bitcast(FP8X4), scales=w1_scales[b][a][:, cols],
+                                  in_=w1_grouped[b, a, half][:])
+
+        a3_wgs = [held(f"a3_wgs{jt}", [P, PACK, P], F32) for jt in range(J_TILES)]
+        a23_t = [tenant("space_h", "a23_t0", [P, J_TILES, PASS], F32), held("a23_t1", [P, J_TILES, PASS], F32)]
+        a23 = [held(f"a23_{s}", [P, S], F32) for s in range(SLICES)]
+        a1 = [held(f"a1_{s}", [P, S], F32) for s in range(SLICES)]
+
+        def turned_affinity(bank, jt, moving):
+            cols = slice(P * jt, P * (jt + 1))
             for a in range(2):
-                codes, scales = stationary(a)
+                codes, scales = moving(a)
                 nc.tensor.matmul_mx(
-                    out=bank[:], lhsT=codes, lhsT_scale=scales,
-                    rhs=got_w[a][:].bitcast(FP8X4), rhs_scale=got_s[a][:],
-                    start=(a == 0), stop=(a == 1),
+                    out=bank[:], lhsT=got_w[a][:, cols].bitcast(FP8X4), lhsT_scale=got_s[a][:, cols],
+                    rhs=codes, rhs_scale=scales, start=(a == 0), stop=(a == 1),
                 )
 
-        def affinity1(s):
+        def scale_cols(b, a):
+            return slice(H * a + PASS * b, H * a + PASS * (b + 1))
+
+        def affinity3(b, jt):
+            bank = banks[jt % 2]
+            turned_affinity(bank, jt, lambda a: (w3_w[b][:, a, :].bitcast(FP8X4), w23_s[4:P, scale_cols(b, a)]))
+            rows = bank[:].rearrange("j (g m i) -> j g i m", g=GROUPS, i=PACK)
+            for g in range(GROUPS):
+                nc.scalar.activation(
+                    out=a3_wgs[jt][:, :, GROUP_ROWS * g : GROUP_ROWS * (g + 1)], in_=rows[:, g], func=COPY,
+                    scale=wgs_cols[:, jt, g : g + 1])
+
+        def affinity2(b, jt):
+            bank = banks[2 + jt % 2]
+            turned_affinity(bank, jt, lambda a: (w2_w[b][:, a, :].bitcast(FP4X4), w23_s[:, scale_cols(b, a)]))
+            nc.vector.tensor_tensor(
+                a23_t[b][:, jt, :].rearrange("j (i m) -> j i m", i=PACK),
+                bank[:].rearrange("j (m i) -> j i m", i=PACK), a3_wgs[jt][:], MULT)
+
+        def turn_a23(s, bank):
+            b, i = divmod(s, PACK)
+            for jt in range(J_TILES):
+                nc.tensor.transpose(bank[:, P * jt : P * (jt + 1)], a23_t[b][:, jt, P * i : P * (i + 1)], ident[:])
+            nc.scalar.copy(out=a23[s][:], in_=bank[:])
+
+        def affinity1(s, bank):
             b, i = divmod(s, PACK)
             cols = slice(P * i, P * (i + 1))
-            product(a1_banks[s % 2], lambda a: (w1_codes[b][a][:, cols].bitcast(FP8X4), w1_scales[b][a][:, cols]))
-
-        def affinity2(s):
-            b, i = divmod(s, PACK)
-            cols, code_cols = slice(P * i, P * (i + 1)), slice(2 * P * i, 2 * P * (i + 1))
-            product(a2_banks[s % 2], lambda a: (w2_codes[:, a, code_cols].bitcast(FP4X4), w23_planes[b][:, a, cols]))
-
-        def affinity3(s):
-            b, i = divmod(s, PACK)
-            cols = slice(P * i, P * (i + 1))
-            product(a3_bank, lambda a: (w3_codes[:, a, cols].bitcast(FP8X4), w23_planes[b][4:P, a, cols]))
-            nc.scalar.copy(out=stage[s % 4][:, :S], in_=a3_bank[:])
+            for a in range(2):
+                nc.tensor.matmul_mx(
+                    out=bank[:], lhsT=w1_codes[b][a][:, cols].bitcast(FP8X4), lhsT_scale=w1_scales[b][a][:, cols],
+                    rhs=got_w[a][:].bitcast(FP8X4), rhs_scale=got_s[a][:], start=(a == 0), stop=(a == 1),
+                )
+            nc.scalar.copy(out=a1[s][:], in_=bank[:])
 
         def place(s):
-            a1_wgs, a2_a3 = factors[s % 2][:, :S], factors[s % 2][:, S:]
-            nc.vector.tensor_tensor(a2_a3, a2_banks[s % 2][:], stage[s % 4][:, :S], MULT)
-            nc.vector.tensor_tensor(a1_wgs, a1_banks[s % 2][:], wgs_sb[:], MULT)
-            nc.vector.tensor_tensor(pages[s % PAGES][:].indirect(cells[:]), a1_wgs, a2_a3, MULT)
+            nc.vector.tensor_tensor(pages[s % PAGES][:].indirect(cells[:]), a1[s][:], a23[s][:], MULT)
+
+        def feed(s, first_bank):
+            turn_a23(s, banks[first_bank])
+            affinity1(s, banks[first_bank + 1])
+            place(s)
 
         zt_words = [[held(f"zt_words{u}{c}", [P, 2, P], F32) for c in range(CHUNKS)] for u in range(2)]
+        z_grouped = [[held(f"z_grouped{b}{c}", [P, CHUNK * PACK], BF16) for c in range(CHUNKS)] for b in range(2)]
         z_codes = [[held(f"z_codes{b}{c}", [P, CHUNK], U32) for c in range(CHUNKS)] for b in range(2)]
         z_scales = [[held(f"z_scales{b}{c}", [P, CHUNK], U8) for c in range(CHUNKS)] for b in range(2)]
 
         turns = []
 
         def next_turn_bank():
-            turns.append(turn_banks[len(turns) % len(turn_banks)])
+            turns.append(banks[len(turns) % 4])
             return turns[-1]
 
-        def add_offers(b, u, c):
-            bank = next_turn_bank()
-            blocks = [(e, tt) for e in range(2) for tt in range(2)]
-            sums = bank[:].rearrange("t (tt e p) -> t tt e p", tt=2, e=2)
+        def add_offers(b, u, c, lanes):
+            sums = next_turn_bank()[:, : 2 * lanes * P].rearrange("t (tt e p) -> t tt e p", tt=2, e=lanes)
+            blocks = [(e, tt) for e in range(lanes) for tt in range(2)]
             for n, (e, tt) in enumerate(blocks):
                 t0 = CHUNK * c + P * tt
                 nc.tensor.matmul(sums[:, tt, e, :], offers_sb[b, u][:, e, t0 : t0 + P], ident[:],
                                  start=(n == 0), stop=False, is_transpose=True)
             for n, (e, tt) in enumerate(blocks):
                 t0 = CHUNK * c + P * tt
-                page = pages[(PACK * b + 2 * u + e) % PAGES]
-                nc.tensor.matmul(sums[:, tt, e, :], page[:, t0 : t0 + P], ident[:],
+                nc.tensor.matmul(sums[:, tt, e, :], pages[(PACK * b + 2 * u + e) % PAGES][:, t0 : t0 + P], ident[:],
                                  start=False, stop=(n == len(blocks) - 1), is_transpose=True)
             nc.scalar.copy(
-                out=zt_words[u][c][:].bitcast(BF16).rearrange("t tt (p e) -> t tt p e", e=2),
+                out=zt_words[u][c][:].bitcast(BF16).rearrange("t tt (p e) -> t tt p e", e=2)[:, :, :, :lanes],
                 in_=sums.rearrange("t tt e p -> t tt p e"),
             )
 
-        z_grouped = [held(f"z_grouped{c}", [P, CHUNK * PACK], BF16) for c in range(CHUNKS)]
-
-        def turn_back(c):
+        def turn_back(b, c):
             halves = next_turn_bank()[:].rearrange("p (u t) -> p u t", u=2)
             for u in range(2):
                 for tt in range(2):
                     nc.tensor.transpose(halves[:, u, P * tt : P * (tt + 1)], zt_words[u][c][:, tt, :], ident[:])
             nc.scalar.copy(
-                out=z_grouped[c][:].bitcast(F32).rearrange("p (t u) -> p t u", u=2),
+                out=z_grouped[b][c][:].bitcast(F32).rearrange("p (t u) -> p t u", u=2),
                 in_=halves.rearrange("p u t -> p t u"),
             )
 
         def quantize_z(b, c):
-            nc.vector.quantize_mx(out=z_codes[b][c][:].bitcast(FP8X4), scales=z_scales[b][c][:], in_=z_grouped[c][:])
-
-        def add_offers_low_half(c):
-            sums = next_turn_bank()[:, : 2 * P].rearrange("t (tt p) -> t tt p", tt=2)
-            page = pages[6 % PAGES]
-            for tt in range(2):
-                t0 = CHUNK * c + P * tt
-                nc.tensor.matmul(sums[:, tt, :], offers_sb[1, 1][:, 0, t0 : t0 + P], ident[:],
-                                 start=(tt == 0), stop=False, is_transpose=True)
-            for tt in range(2):
-                t0 = CHUNK * c + P * tt
-                nc.tensor.matmul(sums[:, tt, :], page[:, t0 : t0 + P], ident[:],
-                                 start=False, stop=(tt == 1), is_transpose=True)
-            nc.scalar.copy(
-                out=zt_words[1][c][:].bitcast(BF16).rearrange("t tt (p e) -> t tt p e", e=2)[:, :, :, 0],
-                in_=sums,
-            )
+            nc.vector.quantize_mx(out=z_codes[b][c][:].bitcast(FP8X4), scales=z_scales[b][c][:], in_=z_grouped[b][c][:])
 
         w4_codes = held("w4_codes", [P, 2 * N], U32)
         w4_scales = held("w4_scales", [P, 2 * N], U8)
 
-        def quantize_w4(b):
+        def quantize_w4(b, cast):
             grouped = held(f"w4_grouped{b}", [P, PACK * N], BF16)[:]
-            nc.scalar.copy(
+            cast(
                 out=grouped.rearrange("p (c n i) -> p c i n", n=4, i=PACK),
-                in_=w4_raw[b].rearrange("p i (c n) -> p c i n", n=4),
+                in_=w4_raw[b][:].rearrange("p i (c n) -> p c i n", n=4),
             )
-            for lo, hi in ((0, 2 * P), (2 * P, N)):
-                cols = slice(N * b + lo, N * b + hi)
-                nc.vector.quantize_mx(out=w4_codes[:, cols].bitcast(FP8X4), scales=w4_scales[:, cols],
-                                      in_=grouped[:, PACK * lo : PACK * hi])
+            cols = slice(N * b, N * (b + 1))
+            nc.vector.quantize_mx(out=w4_codes[:, cols].bitcast(FP8X4), scales=w4_scales[:, cols], in_=grouped)
 
         results = [held(f"result{c}", [P, N_TILES, CHUNK], F32) for c in range(CHUNKS)]
 
@@ -287,70 +274,68 @@ def tile_list_bundle_offer_scores_kernel(
             nc.sync.dma_start(
                 out=out.rearrange("(n p) t -> p n t", p=P)[:, :, CHUNK * c : CHUNK * (c + 1)], in_=results[c][:])
 
-        def step(s, turned=()):
-            jobs = list(turned)
-            half = (len(jobs) + 1) // 2
-            for job in jobs[:half]:
-                job()
-            affinity1(s)
-            for job in jobs[half:]:
-                job()
-            place(s)
-            if s + 1 < 2 * PACK:
-                affinity3(s + 1)
-                affinity2(s + 1)
-
-        def back_and_quantize(c):
-            turn_back(c)
-            quantize_z(0, c)
-
-        affinity3(0)
-        affinity2(0)
-        step(0)
-        quantize_w1(0, 0, 1, nc.scalar.copy)
-        load_w1(1, 1, "landing1")
-        quantize_w1(0, 1, 1, nc.scalar.copy)
-        load_offers(0, 0, "landing0")
-        order_scales(1)
-        load_w23(1)
-        step(1)
-        quantize_w1(1, 0, 0, scalar_cast)
-        quantize_w1(1, 0, 1, scalar_cast)
-        load_offers(0, 1, "landing2")
-        step(2)
-        order_words(1)
-        bias_sb = tenant("late_words", "bias_sb", [P, N_TILES], F32)
+        for jt in range(J_TILES):
+            affinity3(0, jt)
+            affinity2(0, jt)
+        cast_w1(0, 0, 0, nc.vector.tensor_copy, "cast0")
+        cast_w1(0, 0, 1, nc.vector.tensor_copy, "cast1")
+        w23_late = tenant("space_c", "w23_w1", [P, 3 * PASS], I32)
+        load_w3(1, w23_late[:, PASS:])
+        load_w2(1, w23_late[:, :PASS])
+        load_w1(1, 0, "space_e")
+        load_w1(1, 1, "space_b")
+        cast_w1(0, 1, 0, nc.vector.tensor_copy, "space_f")
+        load_w4(0, "space_f")
+        feed(0, 4)
+        feed(1, 6)
+        cast_w1(0, 1, 1, nc.scalar.copy, "space_g")
+        load_w4(1, "space_g")
+        load_offers(0, 0, "space_a")
+        for jt in range(J_TILES):
+            affinity3(1, jt)
+            affinity2(1, jt)
+        load_offers(1, 0, "space_c")
+        bias_sb = tenant("space_w", "bias_sb", [P, N_TILES], F32)
         with nc.allow_non_contiguous_dma(reason="one bias value for each partition and output tile"):
             nc.sync.dma_start(out=bias_sb[:], in_=bias.rearrange("(n p) -> p n", p=P))
-        quantize_w1(1, 1, 0, scalar_cast)
-        quantize_w1(1, 1, 1, scalar_cast)
-        load_offers(1, 0, "landing1")
-        load_w4(0)
-        step(3, [partial(add_offers, 0, 0, c) for c in (0, 1)])
-        load_w4(1)
-        quantize_w4(0)
-        step(4, [partial(add_offers, 0, 0, c) for c in (2, 3)])
-        load_offers(1, 1, "landing0")
-        step(5, [partial(add_offers, 0, 1, c) for c in range(CHUNKS)])
-        quantize_w4(1)
-        step(6, [partial(back_and_quantize, c) for c in range(CHUNKS)])
-        step(7, [partial(add_offers, 1, 0, c) for c in range(CHUNKS)])
-        score_banks = [(a1_banks[0], a2_banks[0]), (a1_banks[1], a2_banks[1]),
-                       (a3_bank, turn_banks[1]), (turn_banks[2], turn_banks[0])]
+        feed(2, 0)
+        feed(3, 4)
+        load_offers(0, 1, "space_h")
+        cast_w1(1, 0, 0, nc.scalar.copy, "cast0")
+        cast_w1(1, 1, 0, nc.scalar.copy, "cast1")
+        feed(4, 6)
+        cast_w1(1, 0, 1, nc.scalar.copy, "cast2")
+        load_offers(1, 1, "space_e")
+        cast_w1(1, 1, 1, nc.scalar.copy, "cast3")
+        feed(5, 4)
         for c in range(CHUNKS):
-            add_offers_low_half(c)
+            add_offers(0, 0, c, 2)
+        feed(6, 6)
+        feed(7, 4)
+        quantize_w4(0, nc.vector.tensor_copy)
+        for c in range(CHUNKS):
+            add_offers(0, 1, c, 2)
+        for c in range(CHUNKS):
+            turn_back(0, c)
+            quantize_z(0, c)
+        quantize_w4(1, nc.vector.tensor_copy)
+        for c in range(CHUNKS):
+            add_offers(1, 0, c, 2)
+        score_banks = [(banks[4], banks[5]), (banks[6], banks[7]), (banks[0], banks[1]), (banks[2], banks[3])]
+        for c in range(CHUNKS):
+            add_offers(1, 1, c, 1)
             if c > 0:
-                turn_back(c - 1)
+                turn_back(1, c - 1)
             if c < 2:
                 score_pass(0, c, score_banks[c])
-        turn_back(CHUNKS - 1)
+        turn_back(1, CHUNKS - 1)
         for c in range(2, CHUNKS):
             score_pass(0, c, score_banks[c])
         for c in range(CHUNKS):
             cols = slice(CHUNK * c, CHUNK * (c + 1))
             nc.vector.tensor_tensor(
-                z_grouped[c][:].rearrange("p (t i) -> p t i", i=PACK)[:, :, PACK - 1],
-                pages[7 % PAGES][:, cols], offers_sb[1, 1][:, 1, cols], ADD)
+                z_grouped[1][c][:].rearrange("p (t i) -> p t i", i=PACK)[:, :, PACK - 1],
+                pages[(SLICES - 1) % PAGES][:, cols], offers_sb[1, 1][:, 1, cols], ADD)
             if c > 0:
                 quantize_z(1, c - 1)
                 store_scores(c - 1, score_pass(1, c - 1, score_banks[c - 1]))

@@ -193,7 +193,8 @@ def tile_list_bundle_offer_scores_kernel(
             nc.scalar.copy(out=a1[s][:], in_=bank[:])
 
         def place(s):
-            nc.vector.tensor_tensor(pages[s % PAGES][:].indirect(cells[:]), a1[s][:], a23[s][:], MULT)
+            nc.gpsimd.tensor_tensor(a1[s][:], a1[s][:], a23[s][:], MULT)
+            nc.vector.tensor_copy(pages[s % PAGES][:].indirect(cells[:]), a1[s][:])
 
         def feed(s, first_bank):
             turn_a23(s, banks[first_bank])

@@ -29,7 +29,8 @@ CHUNK = 256
 CHUNKS = T2 // CHUNK
 N_TILES = N // P
 SLICES = 2 * PACK
-PAGES = 6
+PAGES = 4
+KIB = 1024
 
 
 def tile_list_bundle_offer_scores_kernel(
@@ -39,6 +40,7 @@ def tile_list_bundle_offer_scores_kernel(
     nc = tc.nc
     with ExitStack() as ctx:
         keep = ctx.enter_context(tc.tile_pool(name="keep", bufs=1))
+        landing = ctx.enter_context(tc.tile_pool(name="landing", bufs=1))
         psum = ctx.enter_context(tc.psum_pool(name="psum", bufs=1))
 
         def held(name, shape, dtype):
@@ -47,54 +49,59 @@ def tile_list_bundle_offer_scores_kernel(
         def tenant(slot, name, shape, dtype):
             return keep.tile(shape, dtype, name=name, tag=slot, align_bytes=64)
 
+        def landed(kib, name, shape, dtype):
+            return landing.tile(shape, dtype, name=name, offset=kib * KIB, align_bytes=64)
+
         banks = [psum.tile([P, PASS], F32, name=f"bank{n}") for n in range(8)]
 
         picks = keep.tile([P, S // 16], U16, name="picks")
         cells = keep.tile([P, S // 16], U16, name="cells")
-        tab_s = tenant("space_a", "tab_s", [P, 2 * T], U8)
-        w23_s = held("w23_s", [P, 2 * H], U8)
+        tab_s = landed(28, "tab_s", [P, 2 * T], U8)
+        w2_s = held("w2_s", [P, 2 * H], U8)
+        w3_s = held("w3_s", [P, 2 * H], U8)
         wgs_rows = tenant("space_w", "wgs_rows", [P, S], F32)
         wgs_cols = held("wgs_cols", [P, J_TILES, GROUPS], F32)
-        pages = [held(f"page{s}", [P, T2], F32) for s in range(PAGES)]
+        pages = [held(f"page{s}", [P, T2], F32) for s in range(PAGES - 1)]
         ident = held("ident", [P, P], F32)
         tab_w, w1_raw, offers_sb, w2_w, w3_w, w4_raw = {}, {}, {}, {}, {}, {}
 
         nc.gpsimd.memset(tab_s[:].bitcast(I32), 0)
         make_identity(nc, ident[:])
         nc.vector.memset(wgs_rows[:], 0.0)
-        nc.vector.memset(w23_s[:].bitcast(I32), 0)
+        nc.vector.memset(w3_s[:].bitcast(I32), 0)
+        nc.vector.memset(w2_s[:].bitcast(I32), 0)
 
-        def load_scale_rows(queue, plane, first_row, scales):
+        def load_scale_rows(queue, plane, scales):
             for q in range(4):
-                rows = plane[32 * q + first_row : 32 * q + first_row + 4, :]
+                rows = plane[32 * q : 32 * q + 4, :]
                 queue.dma_start(
                     out=rows.bitcast(I32).rearrange("r (a c) -> r a c", a=2),
                     in_=scales[:, 4 * q : 4 * q + 4, :].rearrange("a r c -> r a c").bitcast(I32),
                 )
 
-        def load_tab(a, slot):
-            tab_w[a] = tenant(slot, f"tab_w{a}", [P, T], I32)
+        def load_tab(a, kib):
+            tab_w[a] = landed(kib, f"tab_w{a}", [P, T], I32)
             nc.sync.dma_start(out=tab_w[a][:], in_=tab_words[a].rearrange("p t i -> p (t i)").bitcast(I32))
 
-        def load_w1(b, a, slot):
+        def load_w1(b, a, kib):
             rows = w1[PASS * a : PASS * (a + 1), PASS * b : PASS * (b + 1)]
-            w1_raw[b, a] = tenant(slot, f"w1_raw{b}{a}", [P, PACK, PASS], F32)
+            w1_raw[b, a] = landed(kib, f"w1_raw{b}{a}", [P, PACK, PASS], F32)
             nc.sync.dma_start(out=w1_raw[b, a][:], in_=rows.rearrange("(p j) c -> p j c", j=PACK))
 
-        def load_w2(b, dest):
-            w2_w[b] = dest.rearrange("p (a c) -> p a c", a=2)
+        def load_w23(b, kib):
+            words = landed(kib, f"w23_w{b}", [P, 3 * PASS], I32)
+            w3_w[b] = words[:, PASS:].rearrange("p (a c) -> p a c", a=2)
+            view = w3_words.rearrange("a p c i -> p a (c i)")[:, :, 4 * PASS * b : 4 * PASS * (b + 1)]
+            nc.sync.dma_start(out=w3_w[b], in_=view.bitcast(I32))
+            w2_w[b] = words[:, :PASS].rearrange("p (a c) -> p a c", a=2)
             view = w2_words.rearrange("a p c -> p a c")[:, :, 2 * PASS * b : 2 * PASS * (b + 1)]
             nc.sync.dma_start(out=w2_w[b], in_=view.bitcast(I32))
 
-        def load_w3(b, dest):
-            w3_w[b] = dest.rearrange("p (a c) -> p a c", a=2)
-            view = w3_words.rearrange("a p c i -> p a (c i)")[:, :, 4 * PASS * b : 4 * PASS * (b + 1)]
-            nc.sync.dma_start(out=w3_w[b], in_=view.bitcast(I32))
-
-        def load_offers(b, u, slot):
+        def load_offers(b, slot):
             rows = offers[PASS * b : PASS * (b + 1), :].rearrange("(p i) t -> p i t", i=PACK)
-            offers_sb[b, u] = tenant(slot, f"offers{b}{u}", [P, 2, T2], F32)
-            nc.sync.dma_start(out=offers_sb[b, u][:], in_=rows[:, 2 * u : 2 * u + 2, :])
+            offers_sb[b] = tenant(slot, f"offers{b}", [P, PACK, T2], F32)
+            for u in range(2):
+                nc.sync.dma_start(out=offers_sb[b][:, 2 * u : 2 * u + 2, :], in_=rows[:, 2 * u : 2 * u + 2, :])
 
         def load_w4(b, slot):
             rows = w4[PASS * b : PASS * (b + 1), :].rearrange("(p i) n -> p i n", i=PACK)
@@ -102,29 +109,31 @@ def tile_list_bundle_offer_scores_kernel(
             nc.sync.dma_start(out=w4_raw[b][:], in_=rows)
 
         nc.sync.dma_start(picks[:], offs)
-        load_tab(0, "space_b")
-        load_tab(1, "space_c")
-        load_w3(0, tenant("space_e", "w3_w0", [P, 2 * PASS], I32)[:])
+        load_tab(0, 14)
+        load_w23(0, 0)
         nc.sync.dma_start(cells[:], offs2)
-        load_scale_rows(nc.scalar, tab_s, 0, tab_scales)
-        load_scale_rows(nc.scalar, w23_s, 4, w3_scales)
-        nc.gpsimd.dma_start(out=wgs_rows[0:GROUPS, :], in_=wgs[0:P:GROUP_ROWS, :])
-        load_scale_rows(nc.gpsimd, w23_s, 0, w2_scales)
+        load_scale_rows(nc.scalar, tab_s, tab_scales)
+        nc.scalar.dma_start(out=wgs_rows[0:GROUPS, :], in_=wgs[0:P:GROUP_ROWS, :])
+        load_scale_rows(nc.scalar, w3_s, w3_scales)
+        load_scale_rows(nc.gpsimd, w2_s, w2_scales)
 
         got_w = [held(f"got_w{a}", [P, S], U32) for a in range(2)]
         got_s = [held(f"got_s{a}", [P, S], U8) for a in range(2)]
 
+        def gather_words(a):
+            nc.vector.tensor_copy(got_w[a][:], tab_w[a][:].bitcast(U32).indirect(picks[:]))
+
+        gather_words(0)
+        load_tab(1, 8)
+        load_w1(0, 0, 20)
         for a in range(2):
             nc.vector.tensor_copy(got_s[a][:], tab_s[:, T * a : T * (a + 1)].indirect(picks[:]))
-        for a in range(2):
-            nc.vector.tensor_copy(got_w[a][:], tab_w[a][:].bitcast(U32).indirect(picks[:]))
-        load_w2(0, tenant("space_b", "w2_w0", [P, PASS], I32)[:])
-        load_w1(0, 0, "space_c")
-        load_w1(0, 1, "space_a")
-        for page in pages[:4]:
+        load_w1(0, 1, 28)
+        gather_words(1)
+        load_w23(1, 8)
+        pages.append(landed(14, "page3", [P, T2], F32))
+        for page in pages:
             nc.vector.memset(page[:], 0.0)
-        for page in pages[4:]:
-            nc.gpsimd.memset(page[:], 0.0)
 
         for jt in range(J_TILES):
             nc.tensor.transpose(banks[7][:, P * jt : P * (jt + 1)], wgs_rows[:, P * jt : P * (jt + 1)], ident[:])
@@ -145,33 +154,33 @@ def tile_list_bundle_offer_scores_kernel(
 
         a3_wgs = [held(f"a3_wgs{jt}", [P, PACK, P], F32) for jt in range(J_TILES)]
         a23_t = [tenant("space_h", "a23_t0", [P, J_TILES, PASS], F32), held("a23_t1", [P, J_TILES, PASS], F32)]
-        a23 = [held(f"a23_{s}", [P, S], F32) for s in range(SLICES)]
-        a1 = [held(f"a1_{s}", [P, S], F32) for s in range(SLICES)]
-
-        def turned_affinity(bank, jt, moving):
-            cols = slice(P * jt, P * (jt + 1))
-            for a in range(2):
-                codes, scales = moving(a)
-                nc.tensor.matmul_mx(
-                    out=bank[:], lhsT=got_w[a][:, cols].bitcast(FP8X4), lhsT_scale=got_s[a][:, cols],
-                    rhs=codes, rhs_scale=scales, start=(a == 0), stop=(a == 1),
-                )
+        a23 = [tenant(f"a23_{s}", f"a23_{s}", [P, S], F32) for s in range(SLICES)]
+        a1 = [tenant(f"a1_{s}", f"a1_{s}", [P, S], F32) for s in range(SLICES)]
 
         def scale_cols(b, a):
             return slice(H * a + PASS * b, H * a + PASS * (b + 1))
 
-        def affinity3(b, jt):
-            bank = banks[jt % 2]
-            turned_affinity(bank, jt, lambda a: (w3_w[b][:, a, :].bitcast(FP8X4), w23_s[4:P, scale_cols(b, a)]))
+        def turned_pass(bank, jt, a, codes, scales):
+            cols = slice(P * jt, P * (jt + 1))
+            nc.tensor.matmul_mx(
+                out=bank[:], lhsT=got_w[a][:, cols].bitcast(FP8X4), lhsT_scale=got_s[a][:, cols],
+                rhs=codes, rhs_scale=scales, start=(a == 0), stop=(a == 1),
+            )
+
+        def pass3(b, jt, a, bank):
+            turned_pass(bank, jt, a, w3_w[b][:, a, :].bitcast(FP8X4), w3_s[:, scale_cols(b, a)])
+
+        def pass2(b, jt, a, bank):
+            turned_pass(bank, jt, a, w2_w[b][:, a, :].bitcast(FP4X4), w2_s[:, scale_cols(b, a)])
+
+        def weigh_a3(jt, bank):
             rows = bank[:].rearrange("j (g m i) -> j g i m", g=GROUPS, i=PACK)
             for g in range(GROUPS):
                 nc.scalar.activation(
                     out=a3_wgs[jt][:, :, GROUP_ROWS * g : GROUP_ROWS * (g + 1)], in_=rows[:, g], func=COPY,
                     scale=wgs_cols[:, jt, g : g + 1])
 
-        def affinity2(b, jt):
-            bank = banks[2 + jt % 2]
-            turned_affinity(bank, jt, lambda a: (w2_w[b][:, a, :].bitcast(FP4X4), w23_s[:, scale_cols(b, a)]))
+        def times_a2(b, jt, bank):
             nc.vector.tensor_tensor(
                 a23_t[b][:, jt, :].rearrange("j (i m) -> j i m", i=PACK),
                 bank[:].rearrange("j (m i) -> j i m", i=PACK), a3_wgs[jt][:], MULT)
@@ -190,10 +199,13 @@ def tile_list_bundle_offer_scores_kernel(
                     out=bank[:], lhsT=w1_codes[b][a][:, cols].bitcast(FP8X4), lhsT_scale=w1_scales[b][a][:, cols],
                     rhs=got_w[a][:].bitcast(FP8X4), rhs_scale=got_s[a][:], start=(a == 0), stop=(a == 1),
                 )
-            nc.scalar.copy(out=a1[s][:], in_=bank[:])
+            if s == 0:
+                nc.vector.tensor_tensor(a1[s][:], bank[:], a23[s][:], MULT)
+            else:
+                nc.scalar.copy(out=a1[s][:], in_=bank[:])
+                nc.gpsimd.tensor_tensor(a1[s][:], a1[s][:], a23[s][:], MULT)
 
         def place(s):
-            nc.gpsimd.tensor_tensor(a1[s][:], a1[s][:], a23[s][:], MULT)
             nc.vector.tensor_copy(pages[s % PAGES][:].indirect(cells[:]), a1[s][:])
 
         def feed(s, first_bank):
@@ -201,41 +213,18 @@ def tile_list_bundle_offer_scores_kernel(
             affinity1(s, banks[first_bank + 1])
             place(s)
 
-        zt_words = [[held(f"zt_words{u}{c}", [P, 2, P], F32) for c in range(CHUNKS)] for u in range(2)]
         z_grouped = [[held(f"z_grouped{b}{c}", [P, CHUNK * PACK], BF16) for c in range(CHUNKS)] for b in range(2)]
         z_codes = [[held(f"z_codes{b}{c}", [P, CHUNK], U32) for c in range(CHUNKS)] for b in range(2)]
         z_scales = [[held(f"z_scales{b}{c}", [P, CHUNK], U8) for c in range(CHUNKS)] for b in range(2)]
 
-        turns = []
+        def add_page(s, cols=slice(0, T2)):
+            b, i = divmod(s, PACK)
+            nc.gpsimd.tensor_tensor(offers_sb[b][:, i, cols], offers_sb[b][:, i, cols], pages[s % PAGES][:, cols], ADD)
 
-        def next_turn_bank():
-            turns.append(banks[len(turns) % 4])
-            return turns[-1]
-
-        def add_offers(b, u, c, lanes):
-            sums = next_turn_bank()[:, : 2 * lanes * P].rearrange("t (tt e p) -> t tt e p", tt=2, e=lanes)
-            blocks = [(e, tt) for e in range(lanes) for tt in range(2)]
-            for n, (e, tt) in enumerate(blocks):
-                t0 = CHUNK * c + P * tt
-                nc.tensor.matmul(sums[:, tt, e, :], offers_sb[b, u][:, e, t0 : t0 + P], ident[:],
-                                 start=(n == 0), stop=False, is_transpose=True)
-            for n, (e, tt) in enumerate(blocks):
-                t0 = CHUNK * c + P * tt
-                nc.tensor.matmul(sums[:, tt, e, :], pages[(PACK * b + 2 * u + e) % PAGES][:, t0 : t0 + P], ident[:],
-                                 start=False, stop=(n == len(blocks) - 1), is_transpose=True)
-            nc.scalar.copy(
-                out=zt_words[u][c][:].bitcast(BF16).rearrange("t tt (p e) -> t tt p e", e=2)[:, :, :, :lanes],
-                in_=sums.rearrange("t tt e p -> t tt p e"),
-            )
-
-        def turn_back(b, c):
-            halves = next_turn_bank()[:].rearrange("p (u t) -> p u t", u=2)
-            for u in range(2):
-                for tt in range(2):
-                    nc.tensor.transpose(halves[:, u, P * tt : P * (tt + 1)], zt_words[u][c][:, tt, :], ident[:])
-            nc.scalar.copy(
-                out=z_grouped[b][c][:].bitcast(F32).rearrange("p (t u) -> p t u", u=2),
-                in_=halves.rearrange("p u t -> p t u"),
+        def weave_z(b, c, cast, lanes=slice(0, PACK)):
+            cast(
+                out=z_grouped[b][c][:].rearrange("p (c n i) -> p c i n", n=4, i=PACK)[:, :, lanes, :],
+                in_=offers_sb[b][:, lanes, CHUNK * c : CHUNK * (c + 1)].rearrange("p i (c n) -> p c i n", n=4),
             )
 
         def quantize_z(b, c):
@@ -268,75 +257,80 @@ def tile_list_bundle_offer_scores_kernel(
 
         def store_scores(c, slots):
             for n in range(N_TILES):
-                if c == CHUNKS - 1 and n == N_TILES - 1:
+                if c == CHUNKS - 1:
                     nc.vector.tensor_scalar_add(results[c][:, n, :], slots[n], bias_sb[:, n : n + 1])
                 else:
                     nc.scalar.activation(out=results[c][:, n, :], in_=slots[n], func=IDENT, bias=bias_sb[:, n : n + 1])
-            nc.sync.dma_start(
-                out=out.rearrange("(n p) t -> p n t", p=P)[:, :, CHUNK * c : CHUNK * (c + 1)], in_=results[c][:])
+                nc.sync.dma_start(out=out[P * n : P * (n + 1), CHUNK * c : CHUNK * (c + 1)], in_=results[c][:, n, :])
 
         for jt in range(J_TILES):
-            affinity3(0, jt)
-            affinity2(0, jt)
-        cast_w1(0, 0, 0, nc.vector.tensor_copy, "cast0")
+            pass3(0, jt, 0, banks[jt])
+        for jt in range(J_TILES):
+            pass2(0, jt, 0, banks[J_TILES + jt])
+        for jt in range(J_TILES):
+            pass3(0, jt, 1, banks[jt])
+            weigh_a3(jt, banks[jt])
+        for jt in range(J_TILES):
+            pass2(0, jt, 1, banks[J_TILES + jt])
+            times_a2(0, jt, banks[J_TILES + jt])
+        cast_w1(0, 0, 0, nc.vector.tensor_copy, "space_x")
+        load_offers(0, "space_x")
         cast_w1(0, 0, 1, nc.vector.tensor_copy, "cast1")
-        w23_late = tenant("space_c", "w23_w1", [P, 3 * PASS], I32)
-        load_w3(1, w23_late[:, PASS:])
-        load_w2(1, w23_late[:, :PASS])
-        load_w1(1, 0, "space_e")
-        load_w1(1, 1, "space_b")
+        load_w1(1, 0, 20)
+        load_w1(1, 1, 0)
         cast_w1(0, 1, 0, nc.vector.tensor_copy, "space_f")
         load_w4(0, "space_f")
-        feed(0, 4)
-        feed(1, 6)
+        feed(0, 0)
+        feed(1, 2)
         cast_w1(0, 1, 1, nc.scalar.copy, "space_g")
         load_w4(1, "space_g")
-        load_offers(0, 0, "space_a")
+        feed(2, 4)
+        add_page(0)
         for jt in range(J_TILES):
-            affinity3(1, jt)
-            affinity2(1, jt)
-        load_offers(1, 0, "space_c")
+            for a in range(2):
+                pass3(1, jt, a, banks[jt % 2])
+            weigh_a3(jt, banks[jt % 2])
+            for a in range(2):
+                pass2(1, jt, a, banks[2 + jt % 2])
+            times_a2(1, jt, banks[2 + jt % 2])
         bias_sb = tenant("space_w", "bias_sb", [P, N_TILES], F32)
         with nc.allow_non_contiguous_dma(reason="one bias value for each partition and output tile"):
             nc.sync.dma_start(out=bias_sb[:], in_=bias.rearrange("(n p) -> p n", p=P))
-        feed(2, 0)
-        feed(3, 4)
-        load_offers(0, 1, "space_h")
         cast_w1(1, 0, 0, nc.scalar.copy, "cast0")
         cast_w1(1, 1, 0, nc.scalar.copy, "cast1")
+        feed(3, 0)
+        load_offers(1, "space_h")
+        add_page(1)
         feed(4, 6)
+        add_page(2)
+        quantize_w4(0, nc.vector.tensor_copy)
         cast_w1(1, 0, 1, nc.scalar.copy, "cast2")
-        load_offers(1, 1, "space_e")
         cast_w1(1, 1, 1, nc.scalar.copy, "cast3")
         feed(5, 4)
-        for c in range(CHUNKS):
-            add_offers(0, 0, c, 2)
-        feed(6, 6)
-        feed(7, 4)
-        quantize_w4(0, nc.vector.tensor_copy)
-        for c in range(CHUNKS):
-            add_offers(0, 1, c, 2)
-        for c in range(CHUNKS):
-            turn_back(0, c)
-            quantize_z(0, c)
+        add_page(3)
         quantize_w4(1, nc.vector.tensor_copy)
+        feed(6, 6)
+        add_page(4)
+        feed(7, 4)
+        add_page(5)
+        score_banks = [(banks[0], banks[1]), (banks[2], banks[3]), (banks[6], banks[7]), (banks[4], banks[5])]
         for c in range(CHUNKS):
-            add_offers(1, 0, c, 2)
-        score_banks = [(banks[4], banks[5]), (banks[6], banks[7]), (banks[0], banks[1]), (banks[2], banks[3])]
-        for c in range(CHUNKS):
-            add_offers(1, 1, c, 1)
-            if c > 0:
-                turn_back(1, c - 1)
-            if c < 2:
-                score_pass(0, c, score_banks[c])
-        turn_back(1, CHUNKS - 1)
-        for c in range(2, CHUNKS):
+            weave_z(0, c, nc.scalar.copy)
+            quantize_z(0, c)
             score_pass(0, c, score_banks[c])
+        add_page(SLICES - 2)
         for c in range(CHUNKS):
-            cols = slice(CHUNK * c, CHUNK * (c + 1))
-            nc.vector.tensor_tensor(
-                z_grouped[1][c][:].rearrange("p (t i) -> p t i", i=PACK)[:, :, PACK - 1],
-                pages[(SLICES - 1) % PAGES][:, cols], offers_sb[1, 1][:, 1, cols], ADD)
+            weave_z(1, c, nc.scalar.copy, slice(0, 2))
+
+        def add_last_page(c):
+            sums = offers_sb[1][:, PACK - 1, CHUNK * c : CHUNK * (c + 1)]
+            nc.vector.tensor_tensor(sums, sums, pages[(SLICES - 1) % PAGES][:, CHUNK * c : CHUNK * (c + 1)], ADD)
+
+        add_last_page(0)
+        for c in range(CHUNKS):
+            if c + 1 < CHUNKS:
+                add_last_page(c + 1)
+            weave_z(1, c, nc.vector.tensor_copy, slice(2, PACK))
             if c > 0:
                 quantize_z(1, c - 1)
                 store_scores(c - 1, score_pass(1, c - 1, score_banks[c - 1]))

@@ -29,7 +29,8 @@ CHUNK = 256
 CHUNKS = T2 // CHUNK
 N_TILES = N // P
 SLICES = 2 * PACK
-PAGES = 4
+PAGES = 6
+RING = 4
 KIB = 1024
 
 
@@ -56,20 +57,20 @@ def tile_list_bundle_offer_scores_kernel(
 
         picks = keep.tile([P, S // 16], U16, name="picks")
         cells = keep.tile([P, S // 16], U16, name="cells")
-        tab_s = landed(28, "tab_s", [P, 2 * T], U8)
+        tab_s = landed(40, "tab_s", [P, 2 * T], U8)
         w2_s = held("w2_s", [P, 2 * H], U8)
         w3_s = held("w3_s", [P, 2 * H], U8)
         wgs_rows = tenant("space_w", "wgs_rows", [P, S], F32)
         wgs_cols = held("wgs_cols", [P, J_TILES, GROUPS], F32)
-        pages = [held(f"page{s}", [P, T2], F32) for s in range(PAGES - 1)]
+        pages = [held(f"page{s}", [P, T2], F32) for s in range(PACK - 1)]
         ident = held("ident", [P, P], F32)
         tab_w, w1_raw, offers_sb, w2_w, w3_w, w4_raw = {}, {}, {}, {}, {}, {}
 
         nc.gpsimd.memset(tab_s[:].bitcast(I32), 0)
         make_identity(nc, ident[:])
         nc.vector.memset(wgs_rows[:], 0.0)
-        nc.vector.memset(w3_s[:].bitcast(I32), 0)
         nc.vector.memset(w2_s[:].bitcast(I32), 0)
+        nc.vector.memset(w3_s[:].bitcast(I32), 0)
 
         def load_scale_rows(queue, plane, scales):
             for q in range(4):
@@ -99,7 +100,7 @@ def tile_list_bundle_offer_scores_kernel(
 
         def load_offers(b, slot):
             rows = offers[PASS * b : PASS * (b + 1), :].rearrange("(p i) t -> p i t", i=PACK)
-            offers_sb[b] = tenant(slot, f"offers{b}", [P, PACK, T2], F32)
+            offers_sb[b] = (tenant if b else landed)(slot, f"offers{b}", [P, PACK, T2], F32)
             for u in range(2):
                 nc.sync.dma_start(out=offers_sb[b][:, 2 * u : 2 * u + 2, :], in_=rows[:, 2 * u : 2 * u + 2, :])
 
@@ -109,13 +110,14 @@ def tile_list_bundle_offer_scores_kernel(
             nc.sync.dma_start(out=w4_raw[b][:], in_=rows)
 
         nc.sync.dma_start(picks[:], offs)
-        load_tab(0, 14)
-        load_w23(0, 0)
         nc.sync.dma_start(cells[:], offs2)
+        load_tab(0, 32)
+        load_tab(1, 12)
+        load_w23(0, 0)
         load_scale_rows(nc.scalar, tab_s, tab_scales)
         nc.scalar.dma_start(out=wgs_rows[0:GROUPS, :], in_=wgs[0:P:GROUP_ROWS, :])
-        load_scale_rows(nc.scalar, w3_s, w3_scales)
-        load_scale_rows(nc.gpsimd, w2_s, w2_scales)
+        load_scale_rows(nc.scalar, w2_s, w2_scales)
+        load_scale_rows(nc.gpsimd, w3_s, w3_scales)
 
         got_w = [held(f"got_w{a}", [P, S], U32) for a in range(2)]
         got_s = [held(f"got_s{a}", [P, S], U8) for a in range(2)]
@@ -123,15 +125,17 @@ def tile_list_bundle_offer_scores_kernel(
         def gather_words(a):
             nc.vector.tensor_copy(got_w[a][:], tab_w[a][:].bitcast(U32).indirect(picks[:]))
 
-        gather_words(0)
-        load_tab(1, 8)
-        load_w1(0, 0, 20)
-        for a in range(2):
+        def gather_scales(a):
             nc.vector.tensor_copy(got_s[a][:], tab_s[:, T * a : T * (a + 1)].indirect(picks[:]))
-        load_w1(0, 1, 28)
+
+        gather_words(0)
+        gather_scales(0)
         gather_words(1)
-        load_w23(1, 8)
-        pages.append(landed(14, "page3", [P, T2], F32))
+        load_w1(0, 0, 8)
+        load_w1(0, 1, 16)
+        gather_scales(1)
+        load_w23(1, 42)
+        pages.append(landed(38, "page3", [P, T2], F32))
         for page in pages:
             nc.vector.memset(page[:], 0.0)
 
@@ -152,7 +156,7 @@ def tile_list_bundle_offer_scores_kernel(
             nc.vector.quantize_mx(out=w1_codes[b][a][:, cols].bitcast(FP8X4), scales=w1_scales[b][a][:, cols],
                                   in_=w1_grouped[b, a, half][:])
 
-        a3_wgs = [held(f"a3_wgs{jt}", [P, PACK, P], F32) for jt in range(J_TILES)]
+        a3_wgs = {}
         a23_t = [tenant("space_h", "a23_t0", [P, J_TILES, PASS], F32), held("a23_t1", [P, J_TILES, PASS], F32)]
         a23 = [tenant(f"a23_{s}", f"a23_{s}", [P, S], F32) for s in range(SLICES)]
         a1 = [tenant(f"a1_{s}", f"a1_{s}", [P, S], F32) for s in range(SLICES)]
@@ -173,17 +177,18 @@ def tile_list_bundle_offer_scores_kernel(
         def pass2(b, jt, a, bank):
             turned_pass(bank, jt, a, w2_w[b][:, a, :].bitcast(FP4X4), w2_s[:, scale_cols(b, a)])
 
-        def weigh_a3(jt, bank):
+        def weigh_a3(b, jt, bank):
+            a3_wgs[jt] = tenant(f"weighed{jt}", f"a3_wgs{b}{jt}", [P, GROUPS, PACK, GROUP_ROWS], F32)
             rows = bank[:].rearrange("j (g m i) -> j g i m", g=GROUPS, i=PACK)
             for g in range(GROUPS):
                 nc.scalar.activation(
-                    out=a3_wgs[jt][:, :, GROUP_ROWS * g : GROUP_ROWS * (g + 1)], in_=rows[:, g], func=COPY,
-                    scale=wgs_cols[:, jt, g : g + 1])
+                    out=a3_wgs[jt][:, g], in_=rows[:, g], func=COPY, scale=wgs_cols[:, jt, g : g + 1])
 
         def times_a2(b, jt, bank):
             nc.vector.tensor_tensor(
-                a23_t[b][:, jt, :].rearrange("j (i m) -> j i m", i=PACK),
-                bank[:].rearrange("j (m i) -> j i m", i=PACK), a3_wgs[jt][:], MULT)
+                a23_t[b][:, jt, :].rearrange("j (i g m) -> j i g m", i=PACK, g=GROUPS),
+                bank[:].rearrange("j (g m i) -> j i g m", g=GROUPS, i=PACK),
+                a3_wgs[jt][:].rearrange("j g i m -> j i g m"), MULT)
 
         def turn_a23(s, bank):
             b, i = divmod(s, PACK)
@@ -199,18 +204,20 @@ def tile_list_bundle_offer_scores_kernel(
                     out=bank[:], lhsT=w1_codes[b][a][:, cols].bitcast(FP8X4), lhsT_scale=w1_scales[b][a][:, cols],
                     rhs=got_w[a][:].bitcast(FP8X4), rhs_scale=got_s[a][:], start=(a == 0), stop=(a == 1),
                 )
-            if s == 0:
-                nc.vector.tensor_tensor(a1[s][:], bank[:], a23[s][:], MULT)
-            else:
-                nc.scalar.copy(out=a1[s][:], in_=bank[:])
-                nc.gpsimd.tensor_tensor(a1[s][:], a1[s][:], a23[s][:], MULT)
+            nc.scalar.copy(out=a1[s][:], in_=bank[:])
 
         def place(s):
-            nc.vector.tensor_copy(pages[s % PAGES][:].indirect(cells[:]), a1[s][:])
+            nc.vector.tensor_tensor(pages[s % PAGES][:].indirect(cells[:]), a1[s][:], a23[s][:], MULT)
 
-        def feed(s, first_bank):
-            turn_a23(s, banks[first_bank])
-            affinity1(s, banks[first_bank + 1])
+        ring = []
+
+        def ring_bank():
+            ring.append(banks[len(ring) % RING])
+            return ring[-1]
+
+        def feed(s):
+            turn_a23(s, ring_bank())
+            affinity1(s, ring_bank())
             place(s)
 
         z_grouped = [[held(f"z_grouped{b}{c}", [P, CHUNK * PACK], BF16) for c in range(CHUNKS)] for b in range(2)]
@@ -219,7 +226,35 @@ def tile_list_bundle_offer_scores_kernel(
 
         def add_page(s, cols=slice(0, T2)):
             b, i = divmod(s, PACK)
-            nc.gpsimd.tensor_tensor(offers_sb[b][:, i, cols], offers_sb[b][:, i, cols], pages[s % PAGES][:, cols], ADD)
+            nc.vector.tensor_tensor(offers_sb[b][:, i, cols], offers_sb[b][:, i, cols], pages[s % PAGES][:, cols], ADD)
+
+        zt_words = [[held(f"zt_words{u}{c}", [P, 2, P], F32) for c in range(CHUNKS)] for u in range(2)]
+
+        def add_turned(u, c):
+            sums = ring_bank()[:].rearrange("t (tt e p) -> t tt e p", tt=2, e=2)
+            blocks = [(e, tt) for e in range(2) for tt in range(2)]
+            for n, (e, tt) in enumerate(blocks):
+                t0 = CHUNK * c + P * tt
+                nc.tensor.matmul(sums[:, tt, e, :], offers_sb[0][:, 2 * u + e, t0 : t0 + P], ident[:],
+                                 start=(n == 0), stop=False, is_transpose=True)
+            for n, (e, tt) in enumerate(blocks):
+                t0 = CHUNK * c + P * tt
+                nc.tensor.matmul(sums[:, tt, e, :], pages[2 * u + e][:, t0 : t0 + P], ident[:],
+                                 start=False, stop=(n == len(blocks) - 1), is_transpose=True)
+            nc.scalar.copy(
+                out=zt_words[u][c][:].bitcast(BF16).rearrange("t tt (p e) -> t tt p e", e=2),
+                in_=sums.rearrange("t tt e p -> t tt p e"),
+            )
+
+        def turn_back(c):
+            halves = ring_bank()[:].rearrange("p (u t) -> p u t", u=2)
+            for u in range(2):
+                for tt in range(2):
+                    nc.tensor.transpose(halves[:, u, P * tt : P * (tt + 1)], zt_words[u][c][:, tt, :], ident[:])
+            nc.scalar.copy(
+                out=z_grouped[0][c][:].bitcast(F32).rearrange("p (t u) -> p t u", u=2),
+                in_=halves.rearrange("p u t -> p t u"),
+            )
 
         def weave_z(b, c, cast, lanes=slice(0, PACK)):
             cast(
@@ -233,8 +268,8 @@ def tile_list_bundle_offer_scores_kernel(
         w4_codes = held("w4_codes", [P, 2 * N], U32)
         w4_scales = held("w4_scales", [P, 2 * N], U8)
 
-        def quantize_w4(b, cast):
-            grouped = held(f"w4_grouped{b}", [P, PACK * N], BF16)[:]
+        def quantize_w4(b, cast, slot):
+            grouped = tenant(slot, f"w4_grouped{b}", [P, PACK * N], BF16)[:]
             cast(
                 out=grouped.rearrange("p (c n i) -> p c i n", n=4, i=PACK),
                 in_=w4_raw[b][:].rearrange("p i (c n) -> p c i n", n=4),
@@ -263,60 +298,69 @@ def tile_list_bundle_offer_scores_kernel(
                     nc.scalar.activation(out=results[c][:, n, :], in_=slots[n], func=IDENT, bias=bias_sb[:, n : n + 1])
                 nc.sync.dma_start(out=out[P * n : P * (n + 1), CHUNK * c : CHUNK * (c + 1)], in_=results[c][:, n, :])
 
+        def affinity3(b, jt, bank):
+            for a in range(2):
+                pass3(b, jt, a, bank)
+            weigh_a3(b, jt, bank)
+
+        def affinity2(b, jt, bank):
+            for a in range(2):
+                pass2(b, jt, a, bank)
+            times_a2(b, jt, bank)
+
+        cast_w1(0, 0, 0, nc.vector.tensor_copy, "cast0")
+        affinity3(0, 0, banks[0])
         for jt in range(J_TILES):
-            pass3(0, jt, 0, banks[jt])
-        for jt in range(J_TILES):
-            pass2(0, jt, 0, banks[J_TILES + jt])
-        for jt in range(J_TILES):
-            pass3(0, jt, 1, banks[jt])
-            weigh_a3(jt, banks[jt])
-        for jt in range(J_TILES):
-            pass2(0, jt, 1, banks[J_TILES + jt])
-            times_a2(0, jt, banks[J_TILES + jt])
-        cast_w1(0, 0, 0, nc.vector.tensor_copy, "space_x")
-        load_offers(0, "space_x")
-        cast_w1(0, 0, 1, nc.vector.tensor_copy, "cast1")
-        load_w1(1, 0, 20)
+            if jt + 1 < J_TILES:
+                affinity3(0, jt + 1, banks[jt + 1])
+            affinity2(0, jt, banks[J_TILES + jt])
+            if jt == 1:
+                cast_w1(0, 1, 0, nc.vector.tensor_copy, "weighed1")
+        cast_w1(0, 0, 1, nc.vector.tensor_copy, "weighed2")
+        load_w1(1, 0, 8)
         load_w1(1, 1, 0)
-        cast_w1(0, 1, 0, nc.vector.tensor_copy, "space_f")
-        load_w4(0, "space_f")
-        feed(0, 0)
-        feed(1, 2)
-        cast_w1(0, 1, 1, nc.scalar.copy, "space_g")
-        load_w4(1, "space_g")
-        feed(2, 4)
-        add_page(0)
+        cast_w1(0, 1, 1, nc.vector.tensor_copy, "weighed3")
+        load_offers(0, 16)
+        for s in range(3):
+            feed(s)
+        for slot in ("a1_1", "a23_1"):
+            pages.append(tenant(slot, f"page{len(pages)}", [P, T2], F32))
+            nc.gpsimd.memset(pages[-1][:], 0.0)
         for jt in range(J_TILES):
-            for a in range(2):
-                pass3(1, jt, a, banks[jt % 2])
-            weigh_a3(jt, banks[jt % 2])
-            for a in range(2):
-                pass2(1, jt, a, banks[2 + jt % 2])
-            times_a2(1, jt, banks[2 + jt % 2])
+            affinity3(1, jt, ring_bank())
+            affinity2(1, jt, banks[RING + jt])
         bias_sb = tenant("space_w", "bias_sb", [P, N_TILES], F32)
         with nc.allow_non_contiguous_dma(reason="one bias value for each partition and output tile"):
             nc.sync.dma_start(out=bias_sb[:], in_=bias.rearrange("(n p) -> p n", p=P))
-        cast_w1(1, 0, 0, nc.scalar.copy, "cast0")
-        cast_w1(1, 1, 0, nc.scalar.copy, "cast1")
-        feed(3, 0)
+        cast_w1(1, 0, 0, nc.scalar.copy, "a1_0")
+        cast_w1(1, 1, 0, nc.scalar.copy, "a23_0")
+        load_w4(0, "a1_0")
+        load_w4(1, "a23_0")
+        feed(3)
         load_offers(1, "space_h")
-        add_page(1)
-        feed(4, 6)
-        add_page(2)
-        quantize_w4(0, nc.vector.tensor_copy)
-        cast_w1(1, 0, 1, nc.scalar.copy, "cast2")
-        cast_w1(1, 1, 1, nc.scalar.copy, "cast3")
-        feed(5, 4)
-        add_page(3)
-        quantize_w4(1, nc.vector.tensor_copy)
-        feed(6, 6)
+        add_turned(0, 0)
+        add_turned(0, 1)
+        feed(4)
+        cast_w1(1, 0, 1, nc.scalar.copy, "a1_2")
+        cast_w1(1, 1, 1, nc.scalar.copy, "a23_2")
+        feed(5)
         add_page(4)
-        feed(7, 4)
+        add_turned(0, 2)
+        add_turned(0, 3)
+        add_turned(1, 0)
+        add_turned(1, 1)
+        feed(6)
         add_page(5)
-        score_banks = [(banks[0], banks[1]), (banks[2], banks[3]), (banks[6], banks[7]), (banks[4], banks[5])]
+        feed(7)
+        add_turned(1, 2)
+        add_turned(1, 3)
+        quantize_w4(0, nc.scalar.copy, "a1_4")
         for c in range(CHUNKS):
-            weave_z(0, c, nc.scalar.copy)
+            turn_back(c)
             quantize_z(0, c)
+        quantize_w4(1, nc.scalar.copy, "a1_5")
+        score_banks = [(banks[4], banks[5]), (banks[6], banks[7]), (banks[0], banks[1]), (banks[2], banks[3])]
+        for c in range(CHUNKS):
             score_pass(0, c, score_banks[c])
         add_page(SLICES - 2)
         for c in range(CHUNKS):

@@ -31,6 +31,7 @@ N_TILES = N // P
 SLICES = 2 * PACK
 PAGES = 6
 RING = 4
+W3_ROW = 4
 KIB = 1024
 
 
@@ -69,12 +70,14 @@ def tile_list_bundle_offer_scores_kernel(
         nc.gpsimd.memset(tab_s[:].bitcast(I32), 0)
         make_identity(nc, ident[:])
         nc.vector.memset(wgs_rows[:], 0.0)
-        nc.vector.memset(w2_s[:].bitcast(I32), 0)
         nc.vector.memset(w3_s[:].bitcast(I32), 0)
+        for page in pages[:2]:
+            nc.vector.memset(page[:], 0.0)
+        nc.vector.memset(w2_s[:].bitcast(I32), 0)
 
-        def load_scale_rows(queue, plane, scales):
+        def load_scale_rows(queue, plane, scales, first_row=0):
             for q in range(4):
-                rows = plane[32 * q : 32 * q + 4, :]
+                rows = plane[32 * q + first_row : 32 * q + first_row + 4, :]
                 queue.dma_start(
                     out=rows.bitcast(I32).rearrange("r (a c) -> r a c", a=2),
                     in_=scales[:, 4 * q : 4 * q + 4, :].rearrange("a r c -> r a c").bitcast(I32),
@@ -89,8 +92,8 @@ def tile_list_bundle_offer_scores_kernel(
             w1_raw[b, a] = landed(kib, f"w1_raw{b}{a}", [P, PACK, PASS], F32)
             nc.sync.dma_start(out=w1_raw[b, a][:], in_=rows.rearrange("(p j) c -> p j c", j=PACK))
 
-        def load_w23(b, kib):
-            words = landed(kib, f"w23_w{b}", [P, 3 * PASS], I32)
+        def load_w23(b, where):
+            words = (tenant if b else landed)(where, f"w23_w{b}", [P, 3 * PASS], I32)
             w3_w[b] = words[:, PASS:].rearrange("p (a c) -> p a c", a=2)
             view = w3_words.rearrange("a p c i -> p a (c i)")[:, :, 4 * PASS * b : 4 * PASS * (b + 1)]
             nc.sync.dma_start(out=w3_w[b], in_=view.bitcast(I32))
@@ -116,8 +119,8 @@ def tile_list_bundle_offer_scores_kernel(
         load_w23(0, 0)
         load_scale_rows(nc.scalar, tab_s, tab_scales)
         nc.scalar.dma_start(out=wgs_rows[0:GROUPS, :], in_=wgs[0:P:GROUP_ROWS, :])
-        load_scale_rows(nc.scalar, w2_s, w2_scales)
-        load_scale_rows(nc.gpsimd, w3_s, w3_scales)
+        load_scale_rows(nc.sync, w2_s, w2_scales)
+        load_scale_rows(nc.gpsimd, w3_s, w3_scales, W3_ROW)
 
         got_w = [held(f"got_w{a}", [P, S], U32) for a in range(2)]
         got_s = [held(f"got_s{a}", [P, S], U8) for a in range(2)]
@@ -134,15 +137,17 @@ def tile_list_bundle_offer_scores_kernel(
         load_w1(0, 0, 8)
         load_w1(0, 1, 16)
         gather_scales(1)
-        load_w23(1, 42)
-        pages.append(landed(38, "page3", [P, T2], F32))
-        for page in pages:
+        pages.extend([landed(37, "page3", [P, T2], F32), landed(41, "page4", [P, T2], F32)])
+        for page in pages[2:]:
             nc.vector.memset(page[:], 0.0)
 
         for jt in range(J_TILES):
             nc.tensor.transpose(banks[7][:, P * jt : P * (jt + 1)], wgs_rows[:, P * jt : P * (jt + 1)], ident[:])
         nc.scalar.activation(
             out=wgs_cols[:], in_=banks[7][:].rearrange("j (jt r) -> j jt r", jt=J_TILES)[:, :, :GROUPS], func=COPY)
+
+        pages.append(tenant("space_w", "page5", [P, T2], F32))
+        nc.vector.memset(pages[-1][:], 0.0)
 
         w1_codes = [[held(f"w1_codes{b}{a}", [P, PASS], U32) for a in range(2)] for b in range(2)]
         w1_scales = [[held(f"w1_scales{b}{a}", [P, PASS], U8) for a in range(2)] for b in range(2)]
@@ -172,23 +177,23 @@ def tile_list_bundle_offer_scores_kernel(
             )
 
         def pass3(b, jt, a, bank):
-            turned_pass(bank, jt, a, w3_w[b][:, a, :].bitcast(FP8X4), w3_s[:, scale_cols(b, a)])
+            turned_pass(bank, jt, a, w3_w[b][:, a, :].bitcast(FP8X4), w3_s[W3_ROW:P, scale_cols(b, a)])
 
         def pass2(b, jt, a, bank):
             turned_pass(bank, jt, a, w2_w[b][:, a, :].bitcast(FP4X4), w2_s[:, scale_cols(b, a)])
 
         def weigh_a3(b, jt, bank):
-            a3_wgs[jt] = tenant(f"weighed{jt}", f"a3_wgs{b}{jt}", [P, GROUPS, PACK, GROUP_ROWS], F32)
+            a3_wgs[b, jt] = tenant(f"weighed{b}{jt}", f"a3_wgs{b}{jt}", [P, GROUPS, PACK, GROUP_ROWS], F32)
             rows = bank[:].rearrange("j (g m i) -> j g i m", g=GROUPS, i=PACK)
             for g in range(GROUPS):
                 nc.scalar.activation(
-                    out=a3_wgs[jt][:, g], in_=rows[:, g], func=COPY, scale=wgs_cols[:, jt, g : g + 1])
+                    out=a3_wgs[b, jt][:, g], in_=rows[:, g], func=COPY, scale=wgs_cols[:, jt, g : g + 1])
 
         def times_a2(b, jt, bank):
             nc.vector.tensor_tensor(
                 a23_t[b][:, jt, :].rearrange("j (i g m) -> j i g m", i=PACK, g=GROUPS),
                 bank[:].rearrange("j (g m i) -> j i g m", g=GROUPS, i=PACK),
-                a3_wgs[jt][:].rearrange("j g i m -> j i g m"), MULT)
+                a3_wgs[b, jt][:].rearrange("j g i m -> j i g m"), MULT)
 
         def turn_a23(s, bank):
             b, i = divmod(s, PACK)
@@ -215,9 +220,10 @@ def tile_list_bundle_offer_scores_kernel(
             ring.append(banks[len(ring) % RING])
             return ring[-1]
 
-        def feed(s):
-            turn_a23(s, ring_bank())
-            affinity1(s, ring_bank())
+        def feed(s, pair=None):
+            a23_bank, a1_bank = pair or (ring_bank(), ring_bank())
+            turn_a23(s, a23_bank)
+            affinity1(s, a1_bank)
             place(s)
 
         z_grouped = [[held(f"z_grouped{b}{c}", [P, CHUNK * PACK], BF16) for c in range(CHUNKS)] for b in range(2)]
@@ -230,29 +236,29 @@ def tile_list_bundle_offer_scores_kernel(
 
         zt_words = [[held(f"zt_words{u}{c}", [P, 2, P], F32) for c in range(CHUNKS)] for u in range(2)]
 
-        def add_turned(u, c):
+        def add_turned(b, u, c):
             sums = ring_bank()[:].rearrange("t (tt e p) -> t tt e p", tt=2, e=2)
             blocks = [(e, tt) for e in range(2) for tt in range(2)]
             for n, (e, tt) in enumerate(blocks):
                 t0 = CHUNK * c + P * tt
-                nc.tensor.matmul(sums[:, tt, e, :], offers_sb[0][:, 2 * u + e, t0 : t0 + P], ident[:],
+                nc.tensor.matmul(sums[:, tt, e, :], offers_sb[b][:, 2 * u + e, t0 : t0 + P], ident[:],
                                  start=(n == 0), stop=False, is_transpose=True)
             for n, (e, tt) in enumerate(blocks):
                 t0 = CHUNK * c + P * tt
-                nc.tensor.matmul(sums[:, tt, e, :], pages[2 * u + e][:, t0 : t0 + P], ident[:],
+                nc.tensor.matmul(sums[:, tt, e, :], pages[PACK * b + 2 * u + e][:, t0 : t0 + P], ident[:],
                                  start=False, stop=(n == len(blocks) - 1), is_transpose=True)
             nc.scalar.copy(
                 out=zt_words[u][c][:].bitcast(BF16).rearrange("t tt (p e) -> t tt p e", e=2),
                 in_=sums.rearrange("t tt e p -> t tt p e"),
             )
 
-        def turn_back(c):
-            halves = ring_bank()[:].rearrange("p (u t) -> p u t", u=2)
-            for u in range(2):
+        def turn_back(b, c, pairs):
+            halves = ring_bank()[:, : pairs * CHUNK].rearrange("p (u t) -> p u t", u=pairs)
+            for u in range(pairs):
                 for tt in range(2):
                     nc.tensor.transpose(halves[:, u, P * tt : P * (tt + 1)], zt_words[u][c][:, tt, :], ident[:])
             nc.scalar.copy(
-                out=z_grouped[0][c][:].bitcast(F32).rearrange("p (t u) -> p t u", u=2),
+                out=z_grouped[b][c][:].bitcast(F32).rearrange("p (t u) -> p t u", u=2)[:, :, :pairs],
                 in_=halves.rearrange("p u t -> p t u"),
             )
 
@@ -292,7 +298,7 @@ def tile_list_bundle_offer_scores_kernel(
 
         def store_scores(c, slots):
             for n in range(N_TILES):
-                if c == CHUNKS - 1:
+                if c == CHUNKS - 1 and n == N_TILES - 1:
                     nc.vector.tensor_scalar_add(results[c][:, n, :], slots[n], bias_sb[:, n : n + 1])
                 else:
                     nc.scalar.activation(out=results[c][:, n, :], in_=slots[n], func=IDENT, bias=bias_sb[:, n : n + 1])
@@ -309,27 +315,26 @@ def tile_list_bundle_offer_scores_kernel(
             times_a2(b, jt, bank)
 
         cast_w1(0, 0, 0, nc.vector.tensor_copy, "cast0")
+        load_w23(1, "cast0")
         affinity3(0, 0, banks[0])
         for jt in range(J_TILES):
             if jt + 1 < J_TILES:
                 affinity3(0, jt + 1, banks[jt + 1])
             affinity2(0, jt, banks[J_TILES + jt])
             if jt == 1:
-                cast_w1(0, 1, 0, nc.vector.tensor_copy, "weighed1")
-        cast_w1(0, 0, 1, nc.vector.tensor_copy, "weighed2")
+                cast_w1(0, 1, 0, nc.vector.tensor_copy, "weighed01")
+        cast_w1(0, 0, 1, nc.vector.tensor_copy, "weighed02")
         load_w1(1, 0, 8)
         load_w1(1, 1, 0)
-        cast_w1(0, 1, 1, nc.vector.tensor_copy, "weighed3")
+        cast_w1(0, 1, 1, nc.vector.tensor_copy, "weighed03")
         load_offers(0, 16)
-        for s in range(3):
-            feed(s)
-        for slot in ("a1_1", "a23_1"):
-            pages.append(tenant(slot, f"page{len(pages)}", [P, T2], F32))
-            nc.gpsimd.memset(pages[-1][:], 0.0)
+        feed(0, banks[4:6])
+        feed(1, (banks[5], banks[4]))
         for jt in range(J_TILES):
             affinity3(1, jt, ring_bank())
             affinity2(1, jt, banks[RING + jt])
-        bias_sb = tenant("space_w", "bias_sb", [P, N_TILES], F32)
+        feed(2)
+        bias_sb = tenant("weighed00", "bias_sb", [P, N_TILES], F32)
         with nc.allow_non_contiguous_dma(reason="one bias value for each partition and output tile"):
             nc.sync.dma_start(out=bias_sb[:], in_=bias.rearrange("(n p) -> p n", p=P))
         cast_w1(1, 0, 0, nc.scalar.copy, "a1_0")
@@ -338,45 +343,34 @@ def tile_list_bundle_offer_scores_kernel(
         load_w4(1, "a23_0")
         feed(3)
         load_offers(1, "space_h")
-        add_turned(0, 0)
-        add_turned(0, 1)
+        add_turned(0, 0, 0)
+        add_turned(0, 0, 1)
         feed(4)
         cast_w1(1, 0, 1, nc.scalar.copy, "a1_2")
         cast_w1(1, 1, 1, nc.scalar.copy, "a23_2")
         feed(5)
         add_page(4)
-        add_turned(0, 2)
-        add_turned(0, 3)
-        add_turned(1, 0)
-        add_turned(1, 1)
+        add_turned(0, 0, 2)
+        add_turned(0, 0, 3)
+        add_turned(0, 1, 0)
+        add_turned(0, 1, 1)
         feed(6)
         add_page(5)
         feed(7)
-        add_turned(1, 2)
-        add_turned(1, 3)
+        add_turned(0, 1, 2)
+        add_turned(0, 1, 3)
         quantize_w4(0, nc.scalar.copy, "a1_4")
-        for c in range(CHUNKS):
-            turn_back(c)
-            quantize_z(0, c)
         quantize_w4(1, nc.scalar.copy, "a1_5")
-        score_banks = [(banks[4], banks[5]), (banks[6], banks[7]), (banks[0], banks[1]), (banks[2], banks[3])]
-        for c in range(CHUNKS):
-            score_pass(0, c, score_banks[c])
         add_page(SLICES - 2)
         for c in range(CHUNKS):
-            weave_z(1, c, nc.scalar.copy, slice(0, 2))
-
-        def add_last_page(c):
-            sums = offers_sb[1][:, PACK - 1, CHUNK * c : CHUNK * (c + 1)]
-            nc.vector.tensor_tensor(sums, sums, pages[(SLICES - 1) % PAGES][:, CHUNK * c : CHUNK * (c + 1)], ADD)
-
-        add_last_page(0)
+            add_page(SLICES - 1, slice(CHUNK * c, CHUNK * (c + 1)))
         for c in range(CHUNKS):
-            if c + 1 < CHUNKS:
-                add_last_page(c + 1)
+            turn_back(0, c, 2)
+            weave_z(1, c, nc.scalar.copy, slice(0, 2))
+        score_banks = [(banks[4], banks[5]), (banks[6], banks[7]), (banks[0], banks[1]), (banks[2], banks[3])]
+        for c in range(CHUNKS):
             weave_z(1, c, nc.vector.tensor_copy, slice(2, PACK))
-            if c > 0:
-                quantize_z(1, c - 1)
-                store_scores(c - 1, score_pass(1, c - 1, score_banks[c - 1]))
-        quantize_z(1, CHUNKS - 1)
-        store_scores(CHUNKS - 1, score_pass(1, CHUNKS - 1, score_banks[CHUNKS - 1]))
+            for b in range(2):
+                quantize_z(b, c)
+                slots = score_pass(b, c, score_banks[c])
+            store_scores(c, slots)

@@ -67,20 +67,20 @@ def tile_list_bundle_offer_scores_kernel(
         ident = held("ident", [P, P], F32)
         tab_w, w1_raw, offers_sb, w2_w, w3_w, w4_raw = {}, {}, {}, {}, {}, {}
 
-        nc.gpsimd.memset(tab_s[:].bitcast(I32), 0)
         make_identity(nc, ident[:])
+        for plane in (tab_s, w3_s):
+            nc.vector.memset(plane[:].bitcast(I32), 0)
         nc.vector.memset(wgs_rows[:], 0.0)
-        nc.vector.memset(w3_s[:].bitcast(I32), 0)
-        for page in pages[:2]:
-            nc.vector.memset(page[:], 0.0)
+        nc.vector.memset(pages[0][:], 0.0)
         nc.vector.memset(w2_s[:].bitcast(I32), 0)
+        nc.vector.memset(pages[1][:], 0.0)
 
         def load_scale_rows(queue, plane, scales, first_row=0):
-            for q in range(4):
-                rows = plane[32 * q + first_row : 32 * q + first_row + 4, :]
+            for r in range(4):
+                rows = plane[first_row + r : P : 32, :]
                 queue.dma_start(
-                    out=rows.bitcast(I32).rearrange("r (a c) -> r a c", a=2),
-                    in_=scales[:, 4 * q : 4 * q + 4, :].rearrange("a r c -> r a c").bitcast(I32),
+                    out=rows.bitcast(I32).rearrange("q (a c) -> q a c", a=2),
+                    in_=scales[:, r:16:4, :].rearrange("a q c -> q a c").bitcast(I32),
                 )
 
         def load_tab(a, kib):
@@ -93,7 +93,7 @@ def tile_list_bundle_offer_scores_kernel(
             nc.sync.dma_start(out=w1_raw[b, a][:], in_=rows.rearrange("(p j) c -> p j c", j=PACK))
 
         def load_w23(b, where):
-            words = (tenant if b else landed)(where, f"w23_w{b}", [P, 3 * PASS], I32)
+            words = landed(where, f"w23_w{b}", [P, 3 * PASS], I32)
             w3_w[b] = words[:, PASS:].rearrange("p (a c) -> p a c", a=2)
             view = w3_words.rearrange("a p c i -> p a (c i)")[:, :, 4 * PASS * b : 4 * PASS * (b + 1)]
             nc.sync.dma_start(out=w3_w[b], in_=view.bitcast(I32))
@@ -114,15 +114,15 @@ def tile_list_bundle_offer_scores_kernel(
 
         nc.sync.dma_start(picks[:], offs)
         nc.sync.dma_start(cells[:], offs2)
-        load_tab(0, 32)
-        load_tab(1, 12)
+        load_tab(0, 12)
+        load_tab(1, 28)
         load_w23(0, 0)
         load_scale_rows(nc.scalar, tab_s, tab_scales)
         nc.scalar.dma_start(out=wgs_rows[0:GROUPS, :], in_=wgs[0:P:GROUP_ROWS, :])
-        load_scale_rows(nc.sync, w2_s, w2_scales)
         load_scale_rows(nc.gpsimd, w3_s, w3_scales, W3_ROW)
+        load_scale_rows(nc.sync, w2_s, w2_scales)
 
-        got_w = [held(f"got_w{a}", [P, S], U32) for a in range(2)]
+        got_w = [held("got_w0", [P, S], U32), landed(41, "got_w1", [P, S], U32)]
         got_s = [held(f"got_s{a}", [P, S], U8) for a in range(2)]
 
         def gather_words(a):
@@ -132,12 +132,12 @@ def tile_list_bundle_offer_scores_kernel(
             nc.vector.tensor_copy(got_s[a][:], tab_s[:, T * a : T * (a + 1)].indirect(picks[:]))
 
         gather_words(0)
-        gather_scales(0)
-        gather_words(1)
         load_w1(0, 0, 8)
         load_w1(0, 1, 16)
+        gather_scales(0)
         gather_scales(1)
-        pages.extend([landed(37, "page3", [P, T2], F32), landed(41, "page4", [P, T2], F32)])
+        gather_words(1)
+        pages.extend([landed(37, "page3", [P, T2], F32), landed(43, "page4", [P, T2], F32)])
         for page in pages[2:]:
             nc.vector.memset(page[:], 0.0)
 
@@ -154,7 +154,7 @@ def tile_list_bundle_offer_scores_kernel(
         w1_grouped = {}
 
         def cast_w1(b, a, half, cast, slot):
-            w1_grouped[b, a, half] = tenant(slot, f"w1_grouped{b}{a}{half}", [P, 2 * PASS], BF16)
+            w1_grouped[b, a, half] = (landed if isinstance(slot, int) else tenant)(slot, f"w1_grouped{b}{a}{half}", [P, 2 * PASS], BF16)
             src = w1_raw[b, a][:].rearrange("p j (m i) -> p m j i", i=PACK)[:, :, :, 2 * half : 2 * half + 2]
             cast(out=w1_grouped[b, a, half][:].rearrange("p (i m j) -> p m j i", i=2, j=PACK), in_=src)
             cols = slice(2 * P * half, 2 * P * (half + 1))
@@ -162,6 +162,7 @@ def tile_list_bundle_offer_scores_kernel(
                                   in_=w1_grouped[b, a, half][:])
 
         a3_wgs = {}
+        weighed_at = {(0, 0): 48, (0, J_TILES - 1): 57}
         a23_t = [tenant("space_h", "a23_t0", [P, J_TILES, PASS], F32), held("a23_t1", [P, J_TILES, PASS], F32)]
         a23 = [tenant(f"a23_{s}", f"a23_{s}", [P, S], F32) for s in range(SLICES)]
         a1 = [tenant(f"a1_{s}", f"a1_{s}", [P, S], F32) for s in range(SLICES)]
@@ -183,7 +184,11 @@ def tile_list_bundle_offer_scores_kernel(
             turned_pass(bank, jt, a, w2_w[b][:, a, :].bitcast(FP4X4), w2_s[:, scale_cols(b, a)])
 
         def weigh_a3(b, jt, bank):
-            a3_wgs[b, jt] = tenant(f"weighed{b}{jt}", f"a3_wgs{b}{jt}", [P, GROUPS, PACK, GROUP_ROWS], F32)
+            shape = [P, GROUPS, PACK, GROUP_ROWS]
+            if (b, jt) in weighed_at:
+                a3_wgs[b, jt] = landed(weighed_at[b, jt], f"a3_wgs{b}{jt}", shape, F32)
+            else:
+                a3_wgs[b, jt] = tenant(f"weighed{b}{jt}", f"a3_wgs{b}{jt}", shape, F32)
             rows = bank[:].rearrange("j (g m i) -> j g i m", g=GROUPS, i=PACK)
             for g in range(GROUPS):
                 nc.scalar.activation(
@@ -220,10 +225,9 @@ def tile_list_bundle_offer_scores_kernel(
             ring.append(banks[len(ring) % RING])
             return ring[-1]
 
-        def feed(s, pair=None):
-            a23_bank, a1_bank = pair or (ring_bank(), ring_bank())
-            turn_a23(s, a23_bank)
-            affinity1(s, a1_bank)
+        def feed(s):
+            turn_a23(s, ring_bank())
+            affinity1(s, ring_bank())
             place(s)
 
         z_grouped = [[held(f"z_grouped{b}{c}", [P, CHUNK * PACK], BF16) for c in range(CHUNKS)] for b in range(2)]
@@ -274,9 +278,8 @@ def tile_list_bundle_offer_scores_kernel(
         w4_codes = held("w4_codes", [P, 2 * N], U32)
         w4_scales = held("w4_scales", [P, 2 * N], U8)
 
-        def quantize_w4(b, cast, slot):
-            grouped = tenant(slot, f"w4_grouped{b}", [P, PACK * N], BF16)[:]
-            cast(
+        def quantize_w4(b, grouped):
+            nc.scalar.copy(
                 out=grouped.rearrange("p (c n i) -> p c i n", n=4, i=PACK),
                 in_=w4_raw[b][:].rearrange("p i (c n) -> p c i n", n=4),
             )
@@ -315,39 +318,41 @@ def tile_list_bundle_offer_scores_kernel(
             times_a2(b, jt, bank)
 
         cast_w1(0, 0, 0, nc.vector.tensor_copy, "cast0")
-        load_w23(1, "cast0")
-        affinity3(0, 0, banks[0])
         for jt in range(J_TILES):
-            if jt + 1 < J_TILES:
-                affinity3(0, jt + 1, banks[jt + 1])
-            affinity2(0, jt, banks[J_TILES + jt])
-            if jt == 1:
-                cast_w1(0, 1, 0, nc.vector.tensor_copy, "weighed01")
-        cast_w1(0, 0, 1, nc.vector.tensor_copy, "weighed02")
+            pass3(0, jt, 0, banks[jt])
+        for jt in range(J_TILES):
+            pass3(0, jt, 1, banks[jt])
+            weigh_a3(0, jt, banks[jt])
+        for jt in range(J_TILES):
+            affinity2(0, jt, banks[RING + jt])
+            if jt == 0:
+                cast_w1(0, 1, 0, nc.vector.tensor_copy, 48)
+        load_w23(1, 48)
+        cast_w1(0, 0, 1, nc.vector.tensor_copy, 56)
         load_w1(1, 0, 8)
         load_w1(1, 1, 0)
-        cast_w1(0, 1, 1, nc.vector.tensor_copy, "weighed03")
+        cast_w1(0, 1, 1, nc.vector.tensor_copy, 58)
         load_offers(0, 16)
-        feed(0, banks[4:6])
-        feed(1, (banks[5], banks[4]))
+        feed(0)
+        feed(1)
+        feed(2)
         for jt in range(J_TILES):
             affinity3(1, jt, ring_bank())
             affinity2(1, jt, banks[RING + jt])
-        feed(2)
-        bias_sb = tenant("weighed00", "bias_sb", [P, N_TILES], F32)
+        bias_sb = tenant("weighed01", "bias_sb", [P, N_TILES], F32)
         with nc.allow_non_contiguous_dma(reason="one bias value for each partition and output tile"):
             nc.sync.dma_start(out=bias_sb[:], in_=bias.rearrange("(n p) -> p n", p=P))
         cast_w1(1, 0, 0, nc.scalar.copy, "a1_0")
         cast_w1(1, 1, 0, nc.scalar.copy, "a23_0")
-        load_w4(0, "a1_0")
-        load_w4(1, "a23_0")
+        for b in range(2):
+            load_w4(b, f"weighed1{b}")
         feed(3)
         load_offers(1, "space_h")
         add_turned(0, 0, 0)
         add_turned(0, 0, 1)
         feed(4)
-        cast_w1(1, 0, 1, nc.scalar.copy, "a1_2")
-        cast_w1(1, 1, 1, nc.scalar.copy, "a23_2")
+        cast_w1(1, 0, 1, nc.scalar.copy, "a1_1")
+        cast_w1(1, 1, 1, nc.scalar.copy, "a23_1")
         feed(5)
         add_page(4)
         add_turned(0, 0, 2)
@@ -359,8 +364,8 @@ def tile_list_bundle_offer_scores_kernel(
         feed(7)
         add_turned(0, 1, 2)
         add_turned(0, 1, 3)
-        quantize_w4(0, nc.scalar.copy, "a1_4")
-        quantize_w4(1, nc.scalar.copy, "a1_5")
+        for b in range(2):
+            quantize_w4(b, tenant(f"weighed1{2 + b}", f"w4_grouped{b}", [P, PACK * N], BF16)[:])
         add_page(SLICES - 2)
         for c in range(CHUNKS):
             add_page(SLICES - 1, slice(CHUNK * c, CHUNK * (c + 1)))

@@ -162,7 +162,7 @@ def tile_list_bundle_offer_scores_kernel(
                                   in_=w1_grouped[b, a, half][:])
 
         a3_wgs = {}
-        weighed_at = {(0, 0): 48, (0, J_TILES - 1): 57}
+        weighed_at = {(0, 0): 48}
         a23_t = [tenant("space_h", "a23_t0", [P, J_TILES, PASS], F32), held("a23_t1", [P, J_TILES, PASS], F32)]
         a23 = [tenant(f"a23_{s}", f"a23_{s}", [P, S], F32) for s in range(SLICES)]
         a1 = [tenant(f"a1_{s}", f"a1_{s}", [P, S], F32) for s in range(SLICES)]
@@ -222,12 +222,13 @@ def tile_list_bundle_offer_scores_kernel(
         ring = []
 
         def ring_bank():
-            ring.append(banks[len(ring) % RING])
+            ring.append(banks[(len(ring) - 1) % RING])
             return ring[-1]
 
-        def feed(s):
-            turn_a23(s, ring_bank())
-            affinity1(s, ring_bank())
+        def feed(s, pair=None):
+            a23_bank, a1_bank = pair or (ring_bank(), ring_bank())
+            turn_a23(s, a23_bank)
+            affinity1(s, a1_bank)
             place(s)
 
         z_grouped = [[held(f"z_grouped{b}{c}", [P, CHUNK * PACK], BF16) for c in range(CHUNKS)] for b in range(2)]
@@ -266,10 +267,10 @@ def tile_list_bundle_offer_scores_kernel(
                 in_=halves.rearrange("p u t -> p t u"),
             )
 
-        def weave_z(b, c, cast, lanes=slice(0, PACK)):
-            cast(
-                out=z_grouped[b][c][:].rearrange("p (c n i) -> p c i n", n=4, i=PACK)[:, :, lanes, :],
-                in_=offers_sb[b][:, lanes, CHUNK * c : CHUNK * (c + 1)].rearrange("p i (c n) -> p c i n", n=4),
+        def weave_z(c, lanes):
+            nc.scalar.copy(
+                out=z_grouped[1][c][:].rearrange("p (t i) -> p t i", i=PACK)[:, :, lanes],
+                in_=offers_sb[1][:, lanes, CHUNK * c : CHUNK * (c + 1)].rearrange("p i t -> p t i"),
             )
 
         def quantize_z(b, c):
@@ -301,7 +302,7 @@ def tile_list_bundle_offer_scores_kernel(
 
         def store_scores(c, slots):
             for n in range(N_TILES):
-                if c == CHUNKS - 1 and n == N_TILES - 1:
+                if c % 2 == 0 or (c == CHUNKS - 1 and n == N_TILES - 1):
                     nc.vector.tensor_scalar_add(results[c][:, n, :], slots[n], bias_sb[:, n : n + 1])
                 else:
                     nc.scalar.activation(out=results[c][:, n, :], in_=slots[n], func=IDENT, bias=bias_sb[:, n : n + 1])
@@ -328,31 +329,31 @@ def tile_list_bundle_offer_scores_kernel(
             if jt == 0:
                 cast_w1(0, 1, 0, nc.vector.tensor_copy, 48)
         load_w23(1, 48)
-        cast_w1(0, 0, 1, nc.vector.tensor_copy, 56)
-        load_w1(1, 0, 8)
         load_w1(1, 1, 0)
-        cast_w1(0, 1, 1, nc.vector.tensor_copy, 58)
+        feed(0, (banks[0], banks[1]))
+        feed(1, (banks[2], banks[0]))
+        cast_w1(0, 0, 1, nc.scalar.copy, "weighed01")
+        load_w1(1, 0, 8)
+        cast_w1(0, 1, 1, nc.scalar.copy, "weighed02")
         load_offers(0, 16)
-        feed(0)
-        feed(1)
-        feed(2)
+        feed(2, (banks[1], banks[2]))
         for jt in range(J_TILES):
             affinity3(1, jt, ring_bank())
             affinity2(1, jt, banks[RING + jt])
-        bias_sb = tenant("weighed01", "bias_sb", [P, N_TILES], F32)
+        bias_sb = tenant("weighed03", "bias_sb", [P, N_TILES], F32)
         with nc.allow_non_contiguous_dma(reason="one bias value for each partition and output tile"):
             nc.sync.dma_start(out=bias_sb[:], in_=bias.rearrange("(n p) -> p n", p=P))
-        cast_w1(1, 0, 0, nc.scalar.copy, "a1_0")
-        cast_w1(1, 1, 0, nc.scalar.copy, "a23_0")
+        cast_w1(1, 0, 0, nc.scalar.copy, "cast0")
+        cast_w1(1, 1, 0, nc.scalar.copy, "cast1")
         for b in range(2):
             load_w4(b, f"weighed1{b}")
-        feed(3)
+        feed(3, ring[-2:])
         load_offers(1, "space_h")
         add_turned(0, 0, 0)
         add_turned(0, 0, 1)
+        cast_w1(1, 0, 1, nc.scalar.copy, "cast2")
+        cast_w1(1, 1, 1, nc.scalar.copy, "cast3")
         feed(4)
-        cast_w1(1, 0, 1, nc.scalar.copy, "a1_1")
-        cast_w1(1, 1, 1, nc.scalar.copy, "a23_1")
         feed(5)
         add_page(4)
         add_turned(0, 0, 2)
@@ -361,21 +362,28 @@ def tile_list_bundle_offer_scores_kernel(
         add_turned(0, 1, 1)
         feed(6)
         add_page(5)
-        feed(7)
         add_turned(0, 1, 2)
         add_turned(0, 1, 3)
         for b in range(2):
             quantize_w4(b, tenant(f"weighed1{2 + b}", f"w4_grouped{b}", [P, PACK * N], BF16)[:])
-        add_page(SLICES - 2)
-        for c in range(CHUNKS):
-            add_page(SLICES - 1, slice(CHUNK * c, CHUNK * (c + 1)))
+        add_page(6)
+        last = SLICES - 1
+        turn_a23(last, ring_bank())
         for c in range(CHUNKS):
             turn_back(0, c, 2)
-            weave_z(1, c, nc.scalar.copy, slice(0, 2))
-        score_banks = [(banks[4], banks[5]), (banks[6], banks[7]), (banks[0], banks[1]), (banks[2], banks[3])]
+            quantize_z(0, c)
+            if c == 1:
+                affinity1(last, ring_bank())
+                place(last)
         for c in range(CHUNKS):
-            weave_z(1, c, nc.vector.tensor_copy, slice(2, PACK))
-            for b in range(2):
-                quantize_z(b, c)
-                slots = score_pass(b, c, score_banks[c])
-            store_scores(c, slots)
+            weave_z(c, slice(0, 2))
+        score_banks = [banks[4:6], banks[6:8], ring[-4:-2], ring[-2:]]
+        for c in range(CHUNKS):
+            score_pass(0, c, score_banks[c])
+        for c in range(CHUNKS):
+            add_page(last, slice(CHUNK * c, CHUNK * (c + 1)))
+        for c in range(CHUNKS):
+            weave_z(c, slice(2, PACK))
+        for c in range(CHUNKS):
+            quantize_z(1, c)
+            store_scores(c, score_pass(1, c, score_banks[c]))

@@ -149,17 +149,26 @@ def tile_list_bundle_offer_scores_kernel(
         pages.append(tenant("space_w", "page5", [P, T2], F32))
         nc.vector.memset(pages[-1][:], 0.0)
 
-        w1_codes = [[held(f"w1_codes{b}{a}", [P, PASS], U32) for a in range(2)] for b in range(2)]
-        w1_scales = [[held(f"w1_scales{b}{a}", [P, PASS], U8) for a in range(2)] for b in range(2)]
-        w1_grouped = {}
+        w1_codes = [held(f"w1_codes{pair}", [P, 2, 2 * P], U32) for pair in range(4)]
+        w1_scales = [held(f"w1_scales{pair}", [P, 2, 2 * P], U8) for pair in range(4)]
+
+        def group_w1(b, a, half, cast, grouped):
+            src = w1_raw[b, a][:].rearrange("p j (m i) -> p m j i", i=PACK)[:, :, :, 2 * half : 2 * half + 2]
+            cast(out=grouped.rearrange("p (i m j) -> p m j i", i=2, j=PACK), in_=src)
 
         def cast_w1(b, a, half, cast, slot):
-            w1_grouped[b, a, half] = (landed if isinstance(slot, int) else tenant)(slot, f"w1_grouped{b}{a}{half}", [P, 2 * PASS], BF16)
-            src = w1_raw[b, a][:].rearrange("p j (m i) -> p m j i", i=PACK)[:, :, :, 2 * half : 2 * half + 2]
-            cast(out=w1_grouped[b, a, half][:].rearrange("p (i m j) -> p m j i", i=2, j=PACK), in_=src)
-            cols = slice(2 * P * half, 2 * P * (half + 1))
-            nc.vector.quantize_mx(out=w1_codes[b][a][:, cols].bitcast(FP8X4), scales=w1_scales[b][a][:, cols],
-                                  in_=w1_grouped[b, a, half][:])
+            grouped = (landed if isinstance(slot, int) else tenant)(slot, f"w1_grouped{b}{a}{half}", [P, 2 * PASS], BF16)
+            group_w1(b, a, half, cast, grouped[:])
+            nc.vector.quantize_mx(out=w1_codes[2 * b + half][:, a, :].bitcast(FP8X4),
+                                  scales=w1_scales[2 * b + half][:, a, :], in_=grouped[:])
+
+        def cast_w1_both(half):
+            grouped = held(f"w1_grouped1{half}", [P, 2, 2 * PASS], BF16)
+            for a in range(2):
+                group_w1(1, a, half, nc.scalar.copy, grouped[:, a, :])
+            nc.vector.quantize_mx(
+                out=w1_codes[2 + half][:].rearrange("p a c -> p (a c)").bitcast(FP8X4),
+                scales=w1_scales[2 + half][:].rearrange("p a c -> p (a c)"), in_=grouped[:].rearrange("p a c -> p (a c)"))
 
         a3_wgs = {}
         weighed_at = {(0, 0): 48}
@@ -207,11 +216,11 @@ def tile_list_bundle_offer_scores_kernel(
             nc.scalar.copy(out=a23[s][:], in_=bank[:])
 
         def affinity1(s, bank):
-            b, i = divmod(s, PACK)
-            cols = slice(P * i, P * (i + 1))
+            pair, e = divmod(s, 2)
+            cols = slice(P * e, P * (e + 1))
             for a in range(2):
                 nc.tensor.matmul_mx(
-                    out=bank[:], lhsT=w1_codes[b][a][:, cols].bitcast(FP8X4), lhsT_scale=w1_scales[b][a][:, cols],
+                    out=bank[:], lhsT=w1_codes[pair][:, a, cols].bitcast(FP8X4), lhsT_scale=w1_scales[pair][:, a, cols],
                     rhs=got_w[a][:].bitcast(FP8X4), rhs_scale=got_s[a][:], start=(a == 0), stop=(a == 1),
                 )
             nc.scalar.copy(out=a1[s][:], in_=bank[:])
@@ -231,13 +240,13 @@ def tile_list_bundle_offer_scores_kernel(
             affinity1(s, a1_bank)
             place(s)
 
-        z_grouped = [[held(f"z_grouped{b}{c}", [P, CHUNK * PACK], BF16) for c in range(CHUNKS)] for b in range(2)]
+        z_grouped = [[tenant(f"woven{c}", f"z_grouped0{c}", [P, CHUNK * PACK], BF16)[:] for c in range(CHUNKS)]]
         z_codes = [[held(f"z_codes{b}{c}", [P, CHUNK], U32) for c in range(CHUNKS)] for b in range(2)]
         z_scales = [[held(f"z_scales{b}{c}", [P, CHUNK], U8) for c in range(CHUNKS)] for b in range(2)]
 
-        def add_page(s, cols=slice(0, T2)):
+        def add_page(s, sums, cols=slice(0, T2)):
             b, i = divmod(s, PACK)
-            nc.vector.tensor_tensor(offers_sb[b][:, i, cols], offers_sb[b][:, i, cols], pages[s % PAGES][:, cols], ADD)
+            nc.vector.tensor_tensor(sums[:, i, cols], offers_sb[b][:, i, cols], pages[s % PAGES][:, cols], ADD)
 
         zt_words = [[held(f"zt_words{u}{c}", [P, 2, P], F32) for c in range(CHUNKS)] for u in range(2)]
 
@@ -263,18 +272,18 @@ def tile_list_bundle_offer_scores_kernel(
                 for tt in range(2):
                     nc.tensor.transpose(halves[:, u, P * tt : P * (tt + 1)], zt_words[u][c][:, tt, :], ident[:])
             nc.scalar.copy(
-                out=z_grouped[b][c][:].bitcast(F32).rearrange("p (t u) -> p t u", u=2)[:, :, :pairs],
+                out=z_grouped[b][c].bitcast(F32).rearrange("p (t u) -> p t u", u=2)[:, :, :pairs],
                 in_=halves.rearrange("p u t -> p t u"),
             )
 
-        def weave_z(c, lanes):
+        def weave_z(c, sums, lanes):
             nc.scalar.copy(
-                out=z_grouped[1][c][:].rearrange("p (t i) -> p t i", i=PACK)[:, :, lanes],
-                in_=offers_sb[1][:, lanes, CHUNK * c : CHUNK * (c + 1)].rearrange("p i t -> p t i"),
+                out=z_grouped[1][c].rearrange("p (t i) -> p t i", i=PACK)[:, :, lanes],
+                in_=sums[:, lanes, CHUNK * c : CHUNK * (c + 1)].rearrange("p i t -> p t i"),
             )
 
         def quantize_z(b, c):
-            nc.vector.quantize_mx(out=z_codes[b][c][:].bitcast(FP8X4), scales=z_scales[b][c][:], in_=z_grouped[b][c][:])
+            nc.vector.quantize_mx(out=z_codes[b][c][:].bitcast(FP8X4), scales=z_scales[b][c][:], in_=z_grouped[b][c])
 
         w4_codes = held("w4_codes", [P, 2 * N], U32)
         w4_scales = held("w4_scales", [P, 2 * N], U8)
@@ -343,30 +352,29 @@ def tile_list_bundle_offer_scores_kernel(
         bias_sb = tenant("weighed03", "bias_sb", [P, N_TILES], F32)
         with nc.allow_non_contiguous_dma(reason="one bias value for each partition and output tile"):
             nc.sync.dma_start(out=bias_sb[:], in_=bias.rearrange("(n p) -> p n", p=P))
-        cast_w1(1, 0, 0, nc.scalar.copy, "cast0")
-        cast_w1(1, 1, 0, nc.scalar.copy, "cast1")
+        cast_w1_both(0)
         for b in range(2):
             load_w4(b, f"weighed1{b}")
         feed(3, ring[-2:])
         load_offers(1, "space_h")
         add_turned(0, 0, 0)
         add_turned(0, 0, 1)
-        cast_w1(1, 0, 1, nc.scalar.copy, "cast2")
-        cast_w1(1, 1, 1, nc.scalar.copy, "cast3")
+        cast_w1_both(1)
         feed(4)
         feed(5)
-        add_page(4)
+        low_sums = tenant("a1_5", "low_sums", [P, 2, T2], F32)
+        add_page(4, low_sums)
+        add_page(5, low_sums)
         add_turned(0, 0, 2)
         add_turned(0, 0, 3)
         add_turned(0, 1, 0)
         add_turned(0, 1, 1)
         feed(6)
-        add_page(5)
         add_turned(0, 1, 2)
         add_turned(0, 1, 3)
         for b in range(2):
             quantize_w4(b, tenant(f"weighed1{2 + b}", f"w4_grouped{b}", [P, PACK * N], BF16)[:])
-        add_page(6)
+        add_page(6, offers_sb[1])
         last = SLICES - 1
         turn_a23(last, ring_bank())
         for c in range(CHUNKS):
@@ -375,15 +383,17 @@ def tile_list_bundle_offer_scores_kernel(
             if c == 1:
                 affinity1(last, ring_bank())
                 place(last)
+        late_grouped = tenant("woven1", "z_grouped1", [P, CHUNKS, CHUNK * PACK], BF16)
+        z_grouped.append([late_grouped[:, c, :] for c in range(CHUNKS)])
         for c in range(CHUNKS):
-            weave_z(c, slice(0, 2))
+            weave_z(c, low_sums, slice(0, 2))
         score_banks = [banks[4:6], banks[6:8], ring[-4:-2], ring[-2:]]
         for c in range(CHUNKS):
             score_pass(0, c, score_banks[c])
         for c in range(CHUNKS):
-            add_page(last, slice(CHUNK * c, CHUNK * (c + 1)))
+            add_page(last, offers_sb[1], slice(CHUNK * c, CHUNK * (c + 1)))
         for c in range(CHUNKS):
-            weave_z(c, slice(2, PACK))
+            weave_z(c, offers_sb[1], slice(2, PACK))
         for c in range(CHUNKS):
             quantize_z(1, c)
             store_scores(c, score_pass(1, c, score_banks[c]))

@@ -68,12 +68,11 @@ def tile_list_bundle_offer_scores_kernel(
         tab_w, w1_raw, offers_sb, w2_w, w3_w, w4_raw = {}, {}, {}, {}, {}, {}
 
         make_identity(nc, ident[:])
-        for plane in (tab_s, w3_s):
+        for plane in (tab_s, w3_s, w2_s):
             nc.vector.memset(plane[:].bitcast(I32), 0)
         nc.vector.memset(wgs_rows[:], 0.0)
-        nc.vector.memset(pages[0][:], 0.0)
-        nc.vector.memset(w2_s[:].bitcast(I32), 0)
-        nc.vector.memset(pages[1][:], 0.0)
+        for page in pages[:2]:
+            nc.vector.memset(page[:], 0.0)
 
         def load_scale_rows(queue, plane, scales, first_row=0):
             for r in range(4):
@@ -120,7 +119,7 @@ def tile_list_bundle_offer_scores_kernel(
         load_scale_rows(nc.scalar, tab_s, tab_scales)
         nc.scalar.dma_start(out=wgs_rows[0:GROUPS, :], in_=wgs[0:P:GROUP_ROWS, :])
         load_scale_rows(nc.gpsimd, w3_s, w3_scales, W3_ROW)
-        load_scale_rows(nc.sync, w2_s, w2_scales)
+        load_scale_rows(nc.gpsimd, w2_s, w2_scales)
 
         got_w = [held("got_w0", [P, S], U32), landed(41, "got_w1", [P, S], U32)]
         got_s = [held(f"got_s{a}", [P, S], U8) for a in range(2)]
@@ -343,13 +342,13 @@ def tile_list_bundle_offer_scores_kernel(
         feed(1, (banks[2], banks[0]))
         cast_w1(0, 0, 1, nc.scalar.copy, "weighed01")
         load_w1(1, 0, 8)
-        cast_w1(0, 1, 1, nc.scalar.copy, "weighed02")
+        cast_w1(0, 1, 1, nc.vector.tensor_copy, "weighed03")
         load_offers(0, 16)
         feed(2, (banks[1], banks[2]))
         for jt in range(J_TILES):
             affinity3(1, jt, ring_bank())
             affinity2(1, jt, banks[RING + jt])
-        bias_sb = tenant("weighed03", "bias_sb", [P, N_TILES], F32)
+        bias_sb = tenant("weighed02", "bias_sb", [P, N_TILES], F32)
         with nc.allow_non_contiguous_dma(reason="one bias value for each partition and output tile"):
             nc.sync.dma_start(out=bias_sb[:], in_=bias.rearrange("(n p) -> p n", p=P))
         cast_w1_both(0)

@@ -31,7 +31,7 @@ N_TILES = N // P
 SLICES = 2 * PACK
 PAGES = 6
 RING = 4
-W3_ROW = 4
+W3_ROW = 0
 KIB = 1024
 
 
@@ -58,7 +58,8 @@ def tile_list_bundle_offer_scores_kernel(
 
         picks = keep.tile([P, S // 16], U16, name="picks")
         cells = keep.tile([P, S // 16], U16, name="cells")
-        tab_s = landed(40, "tab_s", [P, 2 * T], U8)
+        tab_s = landed(40, "tab_s", [P, T], U8)
+        low_s = held("low_s", [P, S], U8)
         w2_s = held("w2_s", [P, 2 * H], U8)
         w3_s = held("w3_s", [P, 2 * H], U8)
         wgs_rows = tenant("space_w", "wgs_rows", [P, S], F32)
@@ -68,7 +69,7 @@ def tile_list_bundle_offer_scores_kernel(
         tab_w, w1_raw, offers_sb, w2_w, w3_w, w4_raw = {}, {}, {}, {}, {}, {}
 
         make_identity(nc, ident[:])
-        for plane in (tab_s, w3_s, w2_s):
+        for plane in (tab_s, w3_s, w2_s, low_s):
             nc.vector.memset(plane[:].bitcast(I32), 0)
         nc.vector.memset(wgs_rows[:], 0.0)
         for page in pages[:2]:
@@ -86,9 +87,9 @@ def tile_list_bundle_offer_scores_kernel(
             tab_w[a] = landed(kib, f"tab_w{a}", [P, T], I32)
             nc.sync.dma_start(out=tab_w[a][:], in_=tab_words[a].rearrange("p t i -> p (t i)").bitcast(I32))
 
-        def load_w1(b, a, kib):
+        def load_w1(b, a, where):
             rows = w1[PASS * a : PASS * (a + 1), PASS * b : PASS * (b + 1)]
-            w1_raw[b, a] = landed(kib, f"w1_raw{b}{a}", [P, PACK, PASS], F32)
+            w1_raw[b, a] = (landed if isinstance(where, int) else tenant)(where, f"w1_raw{b}{a}", [P, PACK, PASS], F32)
             nc.sync.dma_start(out=w1_raw[b, a][:], in_=rows.rearrange("(p j) c -> p j c", j=PACK))
 
         def load_w23(b, where):
@@ -116,27 +117,29 @@ def tile_list_bundle_offer_scores_kernel(
         load_tab(0, 12)
         load_tab(1, 28)
         load_w23(0, 0)
-        load_scale_rows(nc.scalar, tab_s, tab_scales)
+        for q in range(4):
+            nc.scalar.dma_start(
+                out=tab_s[32 * q : 32 * q + 8, :].bitcast(I32),
+                in_=tab_scales[:, 4 * q : 4 * q + 4, :].bitcast(I32))
         nc.scalar.dma_start(out=wgs_rows[0:GROUPS, :], in_=wgs[0:P:GROUP_ROWS, :])
         load_scale_rows(nc.gpsimd, w3_s, w3_scales, W3_ROW)
         load_scale_rows(nc.gpsimd, w2_s, w2_scales)
 
-        got_w = [held("got_w0", [P, S], U32), landed(41, "got_w1", [P, S], U32)]
-        got_s = [held(f"got_s{a}", [P, S], U8) for a in range(2)]
+        got_w = [held("got_w0", [P, S], U32), landed(39, "got_w1", [P, S], U32)]
+        got_both = held("got_both", [P, S], U8)
+        got_s = [got_both[0:P, :], got_both[4:P, :]]
 
         def gather_words(a):
             nc.vector.tensor_copy(got_w[a][:], tab_w[a][:].bitcast(U32).indirect(picks[:]))
 
-        def gather_scales(a):
-            nc.vector.tensor_copy(got_s[a][:], tab_s[:, T * a : T * (a + 1)].indirect(picks[:]))
-
         gather_words(0)
         load_w1(0, 0, 8)
         load_w1(0, 1, 16)
-        gather_scales(0)
-        gather_scales(1)
+        nc.vector.tensor_copy(got_both[:], tab_s[:].indirect(picks[:]))
+        for r in range(4):
+            nc.scalar.dma_start(out=low_s[r:P:32, :].bitcast(I32), in_=got_both[4 + r : P : 32, :].bitcast(I32))
         gather_words(1)
-        pages.extend([landed(37, "page3", [P, T2], F32), landed(43, "page4", [P, T2], F32)])
+        pages.extend([landed(41, "page3", [P, T2], F32), landed(32, "page4", [P, T2], F32)])
         for page in pages[2:]:
             nc.vector.memset(page[:], 0.0)
 
@@ -170,7 +173,7 @@ def tile_list_bundle_offer_scores_kernel(
                 scales=w1_scales[2 + half][:].rearrange("p a c -> p (a c)"), in_=grouped[:].rearrange("p a c -> p (a c)"))
 
         a3_wgs = {}
-        weighed_at = {(0, 0): 48}
+        weighed_at = {(0, 0): 46}
         a23_t = [tenant("space_h", "a23_t0", [P, J_TILES, PASS], F32), held("a23_t1", [P, J_TILES, PASS], F32)]
         a23 = [tenant(f"a23_{s}", f"a23_{s}", [P, S], F32) for s in range(SLICES)]
         a1 = [tenant(f"a1_{s}", f"a1_{s}", [P, S], F32) for s in range(SLICES)]
@@ -178,18 +181,18 @@ def tile_list_bundle_offer_scores_kernel(
         def scale_cols(b, a):
             return slice(H * a + PASS * b, H * a + PASS * (b + 1))
 
-        def turned_pass(bank, jt, a, codes, scales):
+        def turned_pass(bank, jt, a, table_scales, codes, scales):
             cols = slice(P * jt, P * (jt + 1))
             nc.tensor.matmul_mx(
-                out=bank[:], lhsT=got_w[a][:, cols].bitcast(FP8X4), lhsT_scale=got_s[a][:, cols],
+                out=bank[:], lhsT=got_w[a][:, cols].bitcast(FP8X4), lhsT_scale=table_scales[:, cols],
                 rhs=codes, rhs_scale=scales, start=(a == 0), stop=(a == 1),
             )
 
         def pass3(b, jt, a, bank):
-            turned_pass(bank, jt, a, w3_w[b][:, a, :].bitcast(FP8X4), w3_s[W3_ROW:P, scale_cols(b, a)])
+            turned_pass(bank, jt, a, got_s[a], w3_w[b][:, a, :].bitcast(FP8X4), w3_s[W3_ROW:P, scale_cols(b, a)])
 
         def pass2(b, jt, a, bank):
-            turned_pass(bank, jt, a, w2_w[b][:, a, :].bitcast(FP4X4), w2_s[:, scale_cols(b, a)])
+            turned_pass(bank, jt, a, low_s if a else got_both, w2_w[b][:, a, :].bitcast(FP4X4), w2_s[:, scale_cols(b, a)])
 
         def weigh_a3(b, jt, bank):
             shape = [P, GROUPS, PACK, GROUP_ROWS]
@@ -220,7 +223,7 @@ def tile_list_bundle_offer_scores_kernel(
             for a in range(2):
                 nc.tensor.matmul_mx(
                     out=bank[:], lhsT=w1_codes[pair][:, a, cols].bitcast(FP8X4), lhsT_scale=w1_scales[pair][:, a, cols],
-                    rhs=got_w[a][:].bitcast(FP8X4), rhs_scale=got_s[a][:], start=(a == 0), stop=(a == 1),
+                    rhs=got_w[a][:].bitcast(FP8X4), rhs_scale=got_s[a], start=(a == 0), stop=(a == 1),
                 )
             nc.scalar.copy(out=a1[s][:], in_=bank[:])
 
@@ -327,28 +330,29 @@ def tile_list_bundle_offer_scores_kernel(
             times_a2(b, jt, bank)
 
         cast_w1(0, 0, 0, nc.vector.tensor_copy, "cast0")
-        for jt in range(J_TILES):
-            pass3(0, jt, 0, banks[jt])
-        for jt in range(J_TILES):
-            pass3(0, jt, 1, banks[jt])
-            weigh_a3(0, jt, banks[jt])
+        for first in range(0, J_TILES, 2):
+            for a in range(2):
+                for jt in (first, first + 1):
+                    pass3(0, jt, a, banks[jt])
+            for jt in (first, first + 1):
+                weigh_a3(0, jt, banks[jt])
         for jt in range(J_TILES):
             affinity2(0, jt, banks[RING + jt])
             if jt == 0:
-                cast_w1(0, 1, 0, nc.vector.tensor_copy, 48)
-        load_w23(1, 48)
+                cast_w1(0, 1, 0, nc.vector.tensor_copy, 47)
+        load_w23(1, 47)
         load_w1(1, 1, 0)
-        feed(0, (banks[0], banks[1]))
+        feed(0, (banks[0], banks[5]))
         feed(1, (banks[2], banks[0]))
-        cast_w1(0, 0, 1, nc.scalar.copy, "weighed01")
-        load_w1(1, 0, 8)
-        cast_w1(0, 1, 1, nc.vector.tensor_copy, "weighed03")
+        cast_w1(0, 0, 1, nc.scalar.copy, 45)
+        load_w1(1, 0, "weighed02")
+        cast_w1(0, 1, 1, nc.scalar.copy, "weighed01")
         load_offers(0, 16)
-        feed(2, (banks[1], banks[2]))
+        feed(2, (banks[5], banks[2]))
         for jt in range(J_TILES):
             affinity3(1, jt, ring_bank())
             affinity2(1, jt, banks[RING + jt])
-        bias_sb = tenant("weighed02", "bias_sb", [P, N_TILES], F32)
+        bias_sb = tenant("weighed03", "bias_sb", [P, N_TILES], F32)
         with nc.allow_non_contiguous_dma(reason="one bias value for each partition and output tile"):
             nc.sync.dma_start(out=bias_sb[:], in_=bias.rearrange("(n p) -> p n", p=P))
         cast_w1_both(0)

@@ -29,9 +29,10 @@ CHUNK = 256
 CHUNKS = T2 // CHUNK
 N_TILES = N // P
 SLICES = 2 * PACK
-PAGES = 6
+PAGES = 4
 RING = 4
-W3_ROW = 0
+TAB_ROWS = (0, 4)
+W3_ROW = 12
 KIB = 1024
 
 
@@ -52,120 +53,116 @@ def tile_list_bundle_offer_scores_kernel(
             return keep.tile(shape, dtype, name=name, tag=slot, align_bytes=64)
 
         def landed(kib, name, shape, dtype):
-            return landing.tile(shape, dtype, name=name, offset=kib * KIB, align_bytes=64)
+            return landing.tile(shape, dtype, name=name, offset=int(kib * KIB), align_bytes=64)
+
+        def placed(where, name, shape, dtype):
+            return (tenant if isinstance(where, str) else landed)(where, name, shape, dtype)
 
         banks = [psum.tile([P, PASS], F32, name=f"bank{n}") for n in range(8)]
 
         picks = keep.tile([P, S // 16], U16, name="picks")
         cells = keep.tile([P, S // 16], U16, name="cells")
-        tab_s = landed(40, "tab_s", [P, T], U8)
+        tab_s = tenant("tab_s", "tab_s", [P, T], U8)
         low_s = held("low_s", [P, S], U8)
-        w2_s = held("w2_s", [P, 2 * H], U8)
         w3_s = held("w3_s", [P, 2 * H], U8)
-        wgs_rows = tenant("space_w", "wgs_rows", [P, S], F32)
-        wgs_cols = held("wgs_cols", [P, J_TILES, GROUPS], F32)
-        pages = [held(f"page{s}", [P, T2], F32) for s in range(PACK - 1)]
+        w2_s = held("w2_s", [P, 2 * H], U8)
+        pages = [held(f"page{s}", [P, T2], F32) for s in range(PAGES)]
         ident = held("ident", [P, P], F32)
         tab_w, w1_raw, offers_sb, w2_w, w3_w, w4_raw = {}, {}, {}, {}, {}, {}
 
-        make_identity(nc, ident[:])
         for plane in (tab_s, w3_s, w2_s, low_s):
             nc.vector.memset(plane[:].bitcast(I32), 0)
-        nc.vector.memset(wgs_rows[:], 0.0)
-        for page in pages[:2]:
-            nc.vector.memset(page[:], 0.0)
+        for page in pages:
+            nc.vector.memset(page[:, 1:], 0.0)
+            nc.vector.memset(page[:, :1], 0.0)
 
-        def load_scale_rows(queue, plane, scales, first_row=0):
+        def load_scale_rows(queue, plane, first_row, scales):
             for r in range(4):
-                rows = plane[first_row + r : P : 32, :]
+                rows = scales[:, r:16:4, :].rearrange("a q c -> q a c")
                 queue.dma_start(
-                    out=rows.bitcast(I32).rearrange("q (a c) -> q a c", a=2),
-                    in_=scales[:, r:16:4, :].rearrange("a q c -> q a c").bitcast(I32),
-                )
+                    out=plane[first_row + r : P : 32, :].bitcast(I32).rearrange("q (a c) -> q a c", a=2),
+                    in_=rows.bitcast(I32))
 
         def load_tab(a, kib):
             tab_w[a] = landed(kib, f"tab_w{a}", [P, T], I32)
             nc.sync.dma_start(out=tab_w[a][:], in_=tab_words[a].rearrange("p t i -> p (t i)").bitcast(I32))
 
-        def load_w1(b, a, where):
+        def load_w1(b, a, kib):
             rows = w1[PASS * a : PASS * (a + 1), PASS * b : PASS * (b + 1)]
-            w1_raw[b, a] = (landed if isinstance(where, int) else tenant)(where, f"w1_raw{b}{a}", [P, PACK, PASS], F32)
+            w1_raw[b, a] = landed(kib, f"w1_raw{b}{a}", [P, PACK, PASS], F32)
             nc.sync.dma_start(out=w1_raw[b, a][:], in_=rows.rearrange("(p j) c -> p j c", j=PACK))
 
-        def load_w23(b, where):
-            words = landed(where, f"w23_w{b}", [P, 3 * PASS], I32)
-            w3_w[b] = words[:, PASS:].rearrange("p (a c) -> p a c", a=2)
+        def load_w3(b, words):
+            w3_w[b] = words.rearrange("p (a c) -> p a c", a=2)
             view = w3_words.rearrange("a p c i -> p a (c i)")[:, :, 4 * PASS * b : 4 * PASS * (b + 1)]
             nc.sync.dma_start(out=w3_w[b], in_=view.bitcast(I32))
-            w2_w[b] = words[:, :PASS].rearrange("p (a c) -> p a c", a=2)
+
+        def load_w2(b, words):
+            w2_w[b] = words.rearrange("p (a c) -> p a c", a=2)
             view = w2_words.rearrange("a p c -> p a c")[:, :, 2 * PASS * b : 2 * PASS * (b + 1)]
             nc.sync.dma_start(out=w2_w[b], in_=view.bitcast(I32))
 
-        def load_offers(b, slot):
+        def load_offers(b, u, kib):
             rows = offers[PASS * b : PASS * (b + 1), :].rearrange("(p i) t -> p i t", i=PACK)
-            offers_sb[b] = (tenant if b else landed)(slot, f"offers{b}", [P, PACK, T2], F32)
-            for u in range(2):
-                nc.sync.dma_start(out=offers_sb[b][:, 2 * u : 2 * u + 2, :], in_=rows[:, 2 * u : 2 * u + 2, :])
+            offers_sb[b, u] = landed(kib, f"offers{b}{u}", [P, 2, T2], F32)
+            nc.sync.dma_start(out=offers_sb[b, u][:], in_=rows[:, 2 * u : 2 * u + 2, :])
 
-        def load_w4(b, slot):
+        def load_w4(b, kib):
             rows = w4[PASS * b : PASS * (b + 1), :].rearrange("(p i) n -> p i n", i=PACK)
-            w4_raw[b] = tenant(slot, f"w4_raw{b}", [P, PACK, N], F32)
+            w4_raw[b] = landed(kib, f"w4_raw{b}", [P, PACK, N], F32)
             nc.sync.dma_start(out=w4_raw[b][:], in_=rows)
 
         nc.sync.dma_start(picks[:], offs)
         nc.sync.dma_start(cells[:], offs2)
-        load_tab(0, 12)
-        load_tab(1, 28)
-        load_w23(0, 0)
+        load_tab(0, 7)
+        load_w3(0, landed(56, "w3_w0", [P, 2 * PASS], I32)[:])
+        load_tab(1, 29)
+        load_scale_rows(nc.scalar, w3_s, W3_ROW, w3_scales)
         for q in range(4):
-            nc.scalar.dma_start(
-                out=tab_s[32 * q : 32 * q + 8, :].bitcast(I32),
-                in_=tab_scales[:, 4 * q : 4 * q + 4, :].bitcast(I32))
-        nc.scalar.dma_start(out=wgs_rows[0:GROUPS, :], in_=wgs[0:P:GROUP_ROWS, :])
-        load_scale_rows(nc.gpsimd, w3_s, w3_scales, W3_ROW)
-        load_scale_rows(nc.gpsimd, w2_s, w2_scales)
+            nc.gpsimd.dma_start(out=tab_s[32 * q : 32 * q + 8, :].bitcast(I32),
+                                in_=tab_scales[:, 4 * q : 4 * q + 4, :].bitcast(I32))
+        make_identity(nc, ident[:])
+        load_scale_rows(nc.gpsimd, w2_s, 0, w2_scales)
 
-        got_w = [held("got_w0", [P, S], U32), landed(39, "got_w1", [P, S], U32)]
+        got_w = [held("got_w0", [P, S], U32)]
         got_both = held("got_both", [P, S], U8)
-        got_s = [got_both[0:P, :], got_both[4:P, :]]
+        got_s = [got_both[row:P, :] for row in TAB_ROWS]
 
         def gather_words(a):
             nc.vector.tensor_copy(got_w[a][:], tab_w[a][:].bitcast(U32).indirect(picks[:]))
 
         gather_words(0)
-        load_w1(0, 0, 8)
-        load_w1(0, 1, 16)
+        load_w2(0, landed(8, "w2_w0", [P, PASS], I32)[:])
+        wgs_rows = landed(10, "wgs_rows", [P, P], F32)
+        nc.sync.dma_start(out=wgs_rows[:], in_=wgs[0:P:J_TILES, :].rearrange("m (jt c) -> m jt c", jt=J_TILES))
+        load_w1(0, 0, 0)
+        load_w1(0, 1, 14)
         nc.vector.tensor_copy(got_both[:], tab_s[:].indirect(picks[:]))
         for r in range(4):
             nc.scalar.dma_start(out=low_s[r:P:32, :].bitcast(I32), in_=got_both[4 + r : P : 32, :].bitcast(I32))
+        got_w.append(tenant("tab_s", "got_w1", [P, S], U32))
         gather_words(1)
-        pages.extend([landed(41, "page3", [P, T2], F32), landed(32, "page4", [P, T2], F32)])
-        for page in pages[2:]:
-            nc.vector.memset(page[:], 0.0)
 
-        for jt in range(J_TILES):
-            nc.tensor.transpose(banks[7][:, P * jt : P * (jt + 1)], wgs_rows[:, P * jt : P * (jt + 1)], ident[:])
+        wgs_cols = held("wgs_cols", [P, GROUPS, J_TILES], F32)
+        nc.tensor.transpose(banks[7][:, :P], wgs_rows[:], ident[:])
         nc.scalar.activation(
-            out=wgs_cols[:], in_=banks[7][:].rearrange("j (jt r) -> j jt r", jt=J_TILES)[:, :, :GROUPS], func=COPY)
+            out=wgs_cols[:], in_=banks[7][:, :P].rearrange("j (g m) -> j g m", g=GROUPS)[:, :, :J_TILES], func=COPY)
 
-        pages.append(tenant("space_w", "page5", [P, T2], F32))
-        nc.vector.memset(pages[-1][:], 0.0)
-
-        w1_codes = [held(f"w1_codes{pair}", [P, 2, 2 * P], U32) for pair in range(4)]
-        w1_scales = [held(f"w1_scales{pair}", [P, 2, 2 * P], U8) for pair in range(4)]
+        w1_codes = [tenant(f"w1_codes{pair}", f"w1_codes{pair}", [P, 2, 2 * P], U32) for pair in range(4)]
+        w1_scales = [tenant(f"w1_scales{pair}", f"w1_scales{pair}", [P, 2, 2 * P], U8) for pair in range(4)]
 
         def group_w1(b, a, half, cast, grouped):
             src = w1_raw[b, a][:].rearrange("p j (m i) -> p m j i", i=PACK)[:, :, :, 2 * half : 2 * half + 2]
             cast(out=grouped.rearrange("p (i m j) -> p m j i", i=2, j=PACK), in_=src)
 
         def cast_w1(b, a, half, cast, slot):
-            grouped = (landed if isinstance(slot, int) else tenant)(slot, f"w1_grouped{b}{a}{half}", [P, 2 * PASS], BF16)
+            grouped = placed(slot, f"w1_grouped{b}{a}{half}", [P, 2 * PASS], BF16)
             group_w1(b, a, half, cast, grouped[:])
             nc.vector.quantize_mx(out=w1_codes[2 * b + half][:, a, :].bitcast(FP8X4),
                                   scales=w1_scales[2 * b + half][:, a, :], in_=grouped[:])
 
-        def cast_w1_both(half):
-            grouped = held(f"w1_grouped1{half}", [P, 2, 2 * PASS], BF16)
+        def cast_w1_both(half, slot):
+            grouped = placed(slot, f"w1_grouped1{half}", [P, 2, 2 * PASS], BF16)
             for a in range(2):
                 group_w1(1, a, half, nc.scalar.copy, grouped[:, a, :])
             nc.vector.quantize_mx(
@@ -173,13 +170,9 @@ def tile_list_bundle_offer_scores_kernel(
                 scales=w1_scales[2 + half][:].rearrange("p a c -> p (a c)"), in_=grouped[:].rearrange("p a c -> p (a c)"))
 
         a3_wgs = {}
-        weighed_at = {(0, 0): 46}
-        a23_t = [tenant("space_h", "a23_t0", [P, J_TILES, PASS], F32), held("a23_t1", [P, J_TILES, PASS], F32)]
-        a23 = [tenant(f"a23_{s}", f"a23_{s}", [P, S], F32) for s in range(SLICES)]
-        a1 = [tenant(f"a1_{s}", f"a1_{s}", [P, S], F32) for s in range(SLICES)]
-
-        def scale_cols(b, a):
-            return slice(H * a + PASS * b, H * a + PASS * (b + 1))
+        a23_t = [held(f"a23_t{b}", [P, J_TILES, PASS], F32) for b in range(2)]
+        a23 = [landed(66, "a23_0", [P, S], F32)] + [held(f"a23_{s}", [P, S], F32) for s in range(1, SLICES)]
+        a1 = [landed(74, "a1_0", [P, S], F32)] + [held(f"a1_{s}", [P, S], F32) for s in range(1, SLICES)]
 
         def turned_pass(bank, jt, a, table_scales, codes, scales):
             cols = slice(P * jt, P * (jt + 1))
@@ -189,21 +182,18 @@ def tile_list_bundle_offer_scores_kernel(
             )
 
         def pass3(b, jt, a, bank):
-            turned_pass(bank, jt, a, got_s[a], w3_w[b][:, a, :].bitcast(FP8X4), w3_s[W3_ROW:P, scale_cols(b, a)])
+            turned_pass(bank, jt, a, got_s[a], w3_w[b][:, a, :].bitcast(FP8X4),
+                        w3_s[W3_ROW:P, H * a + PASS * b : H * a + PASS * (b + 1)])
 
         def pass2(b, jt, a, bank):
-            turned_pass(bank, jt, a, low_s if a else got_both, w2_w[b][:, a, :].bitcast(FP4X4), w2_s[:, scale_cols(b, a)])
+            turned_pass(bank, jt, a, low_s if a else got_both, w2_w[b][:, a, :].bitcast(FP4X4), w2_s[:, H * a + PASS * b : H * a + PASS * (b + 1)])
 
         def weigh_a3(b, jt, bank):
-            shape = [P, GROUPS, PACK, GROUP_ROWS]
-            if (b, jt) in weighed_at:
-                a3_wgs[b, jt] = landed(weighed_at[b, jt], f"a3_wgs{b}{jt}", shape, F32)
-            else:
-                a3_wgs[b, jt] = tenant(f"weighed{b}{jt}", f"a3_wgs{b}{jt}", shape, F32)
+            a3_wgs[b, jt] = placed({(0, 0): 37, (0, 2): 49}.get((b, jt), f"weighed{b}{jt}"), f"a3_wgs{b}{jt}", [P, GROUPS, PACK, GROUP_ROWS], F32)
             rows = bank[:].rearrange("j (g m i) -> j g i m", g=GROUPS, i=PACK)
             for g in range(GROUPS):
                 nc.scalar.activation(
-                    out=a3_wgs[b, jt][:, g], in_=rows[:, g], func=COPY, scale=wgs_cols[:, jt, g : g + 1])
+                    out=a3_wgs[b, jt][:, g], in_=rows[:, g], func=COPY, scale=wgs_cols[:, g, jt : jt + 1])
 
         def times_a2(b, jt, bank):
             nc.vector.tensor_tensor(
@@ -233,70 +223,78 @@ def tile_list_bundle_offer_scores_kernel(
         ring = []
 
         def ring_bank():
-            ring.append(banks[(len(ring) - 1) % RING])
+            ring.append(banks[(len(ring) + 1) % RING])
             return ring[-1]
 
-        def feed(s, pair=None):
-            a23_bank, a1_bank = pair or (ring_bank(), ring_bank())
-            turn_a23(s, a23_bank)
-            affinity1(s, a1_bank)
-            place(s)
+        def feed(s):
+            turn_a23(s, ring_bank())
+            affinity1(s, ring_bank())
 
-        z_grouped = [[tenant(f"woven{c}", f"z_grouped0{c}", [P, CHUNK * PACK], BF16)[:] for c in range(CHUNKS)]]
-        z_codes = [[held(f"z_codes{b}{c}", [P, CHUNK], U32) for c in range(CHUNKS)] for b in range(2)]
+        z_grouped = [[tenant(f"z_grouped{b}{c}", f"z_grouped{b}{c}", [P, CHUNK * PACK], BF16) for c in range(CHUNKS)] for b in range(2)]
+        z_codes = {}
         z_scales = [[held(f"z_scales{b}{c}", [P, CHUNK], U8) for c in range(CHUNKS)] for b in range(2)]
-
-        def add_page(s, sums, cols=slice(0, T2)):
-            b, i = divmod(s, PACK)
-            nc.vector.tensor_tensor(sums[:, i, cols], offers_sb[b][:, i, cols], pages[s % PAGES][:, cols], ADD)
-
         zt_words = [[held(f"zt_words{u}{c}", [P, 2, P], F32) for c in range(CHUNKS)] for u in range(2)]
 
-        def add_turned(b, u, c):
-            sums = ring_bank()[:].rearrange("t (tt e p) -> t tt e p", tt=2, e=2)
-            blocks = [(e, tt) for e in range(2) for tt in range(2)]
-            for n, (e, tt) in enumerate(blocks):
-                t0 = CHUNK * c + P * tt
-                nc.tensor.matmul(sums[:, tt, e, :], offers_sb[b][:, 2 * u + e, t0 : t0 + P], ident[:],
-                                 start=(n == 0), stop=False, is_transpose=True)
-            for n, (e, tt) in enumerate(blocks):
-                t0 = CHUNK * c + P * tt
-                nc.tensor.matmul(sums[:, tt, e, :], pages[PACK * b + 2 * u + e][:, t0 : t0 + P], ident[:],
-                                 start=False, stop=(n == len(blocks) - 1), is_transpose=True)
+        sums = [bank[:].rearrange("t (tt e p) -> t tt e p", tt=2, e=2) for bank in banks[RING:]]
+
+        def turn_rows(rows, e, start, stop):
+            for c in range(CHUNKS):
+                for tt in range(2):
+                    t0 = CHUNK * c + P * tt
+                    nc.tensor.matmul(sums[c][:, tt, e, :], rows[:, t0 : t0 + P], ident[:],
+                                     start=(start and tt == 0), stop=(stop and tt == 1), is_transpose=True)
+
+        def open_sums(b, u, lanes=2):
+            for e in range(lanes):
+                turn_rows(offers_sb[b, u][:, e, :], e, e == 0, False)
+
+        def round_sums(u, c, lanes):
             nc.scalar.copy(
-                out=zt_words[u][c][:].bitcast(BF16).rearrange("t tt (p e) -> t tt p e", e=2),
-                in_=sums.rearrange("t tt e p -> t tt p e"),
+                out=zt_words[u][c][:].bitcast(BF16).rearrange("t tt (p e) -> t tt p e", e=2)[:, :, :, :lanes],
+                in_=sums[c].rearrange("t tt e p -> t tt p e")[:, :, :, :lanes],
             )
 
-        def turn_back(b, c, pairs):
-            halves = ring_bank()[:, : pairs * CHUNK].rearrange("p (u t) -> p u t", u=pairs)
+        def close_sums(u):
+            for e in range(2):
+                turn_rows(pages[2 * u + e][:], e, False, e == 1)
+            for c in range(CHUNKS):
+                round_sums(u, c, 2)
+
+        def turn_back(b, c, bank, pairs=2):
+            halves = bank[:, : pairs * CHUNK].rearrange("p (u t) -> p u t", u=pairs)
             for u in range(pairs):
                 for tt in range(2):
                     nc.tensor.transpose(halves[:, u, P * tt : P * (tt + 1)], zt_words[u][c][:, tt, :], ident[:])
             nc.scalar.copy(
-                out=z_grouped[b][c].bitcast(F32).rearrange("p (t u) -> p t u", u=2)[:, :, :pairs],
+                out=z_grouped[b][c][:].bitcast(F32).rearrange("p (t u) -> p t u", u=2)[:, :, :pairs],
                 in_=halves.rearrange("p u t -> p t u"),
             )
 
-        def weave_z(c, sums, lanes):
+        def add_page(e, cols):
+            rows = offers_sb[1, 1][:, e, cols]
+            nc.vector.tensor_tensor(rows, rows, pages[2 + e][:, cols], ADD)
+
+        def weave_last(c):
             nc.scalar.copy(
-                out=z_grouped[1][c].rearrange("p (t i) -> p t i", i=PACK)[:, :, lanes],
-                in_=sums[:, lanes, CHUNK * c : CHUNK * (c + 1)].rearrange("p i t -> p t i"),
+                out=z_grouped[1][c][:].rearrange("p (t i) -> p t i", i=PACK)[:, :, 2:],
+                in_=offers_sb[1, 1][:, :, CHUNK * c : CHUNK * (c + 1)].rearrange("p i t -> p t i"),
             )
 
-        def quantize_z(b, c):
-            nc.vector.quantize_mx(out=z_codes[b][c][:].bitcast(FP8X4), scales=z_scales[b][c][:], in_=z_grouped[b][c])
+        def quantize_z(b, c, slot=None):
+            z_codes[b, c] = tenant(slot or f"z_codes{b}{c}", f"z_codes{b}{c}", [P, CHUNK], U32)
+            nc.vector.quantize_mx(out=z_codes[b, c][:].bitcast(FP8X4), scales=z_scales[b][c][:], in_=z_grouped[b][c][:])
 
         w4_codes = held("w4_codes", [P, 2 * N], U32)
         w4_scales = held("w4_scales", [P, 2 * N], U8)
 
-        def quantize_w4(b, grouped):
-            nc.scalar.copy(
-                out=grouped.rearrange("p (c n i) -> p c i n", n=4, i=PACK),
+        def quantize_w4(b, slot, cast):
+            grouped = tenant(slot, f"w4_grouped{b}", [P, PACK * N], BF16)
+            cast(
+                out=grouped[:].rearrange("p (c n i) -> p c i n", n=4, i=PACK),
                 in_=w4_raw[b][:].rearrange("p i (c n) -> p c i n", n=4),
             )
             cols = slice(N * b, N * (b + 1))
-            nc.vector.quantize_mx(out=w4_codes[:, cols].bitcast(FP8X4), scales=w4_scales[:, cols], in_=grouped)
+            nc.vector.quantize_mx(out=w4_codes[:, cols].bitcast(FP8X4), scales=w4_scales[:, cols], in_=grouped[:])
 
         results = [held(f"result{c}", [P, N_TILES, CHUNK], F32) for c in range(CHUNKS)]
 
@@ -306,7 +304,7 @@ def tile_list_bundle_offer_scores_kernel(
                 cols = slice(N * b + P * n, N * b + P * (n + 1))
                 nc.tensor.matmul_mx(
                     out=slots[n], lhsT=w4_codes[:, cols].bitcast(FP8X4), lhsT_scale=w4_scales[:, cols],
-                    rhs=z_codes[b][c][:].bitcast(FP8X4), rhs_scale=z_scales[b][c][:],
+                    rhs=z_codes[b, c][:].bitcast(FP8X4), rhs_scale=z_scales[b][c][:],
                     start=(b == 0 and n != 1), stop=(b == 1 and n != 0),
                 )
             return slots
@@ -329,74 +327,73 @@ def tile_list_bundle_offer_scores_kernel(
                 pass2(b, jt, a, bank)
             times_a2(b, jt, bank)
 
-        cast_w1(0, 0, 0, nc.vector.tensor_copy, "cast0")
-        for first in range(0, J_TILES, 2):
-            for a in range(2):
-                for jt in (first, first + 1):
-                    pass3(0, jt, a, banks[jt])
-            for jt in (first, first + 1):
-                weigh_a3(0, jt, banks[jt])
+        for a in range(2):
+            for jt in range(J_TILES):
+                pass3(0, jt, a, banks[jt])
+        for jt in range(J_TILES):
+            weigh_a3(0, jt, banks[jt])
         for jt in range(J_TILES):
             affinity2(0, jt, banks[RING + jt])
-            if jt == 0:
-                cast_w1(0, 1, 0, nc.vector.tensor_copy, 47)
-        load_w23(1, 47)
-        load_w1(1, 1, 0)
-        feed(0, (banks[0], banks[5]))
-        feed(1, (banks[2], banks[0]))
-        cast_w1(0, 0, 1, nc.scalar.copy, 45)
-        load_w1(1, 0, "weighed02")
+        load_w1(1, 0, 30)
+        cast_w1(0, 0, 0, nc.scalar.copy, 38)
+        cast_w1(0, 1, 0, nc.vector.tensor_copy, 49)
+        turn_a23(0, banks[0])
+        affinity1(0, banks[RING])
+        cast_w1(0, 0, 1, nc.vector.tensor_copy, "weighed03")
         cast_w1(0, 1, 1, nc.scalar.copy, "weighed01")
-        load_offers(0, 16)
-        feed(2, (banks[5], banks[2]))
+        place(0)
+        load_w3(1, landed(17, "w3_w1", [P, 2 * PASS], I32)[:])
+        load_w2(1, landed(15, "w2_w1", [P, PASS], I32)[:])
+        load_w1(1, 1, 21)
+        load_offers(0, 0, 42)
+        load_w4(0, 50)
+        load_w4(1, 62)
+        load_offers(0, 1, 68)
+        affinity1(1, banks[0])
+        turn_a23(1, banks[RING])
+        place(1)
         for jt in range(J_TILES):
             affinity3(1, jt, ring_bank())
             affinity2(1, jt, banks[RING + jt])
-        bias_sb = tenant("weighed03", "bias_sb", [P, N_TILES], F32)
+        feed(2)
+        place(2)
+        cast_w1_both(0, "w1_codes0")
+        feed(3)
+        place(3)
+        cast_w1_both(1, "w1_scales0")
+        load_offers(1, 0, 21)
+        load_offers(1, 1, 30)
+        bias_sb = tenant("weighed12", "bias_sb", [P, N_TILES], F32)
         with nc.allow_non_contiguous_dma(reason="one bias value for each partition and output tile"):
             nc.sync.dma_start(out=bias_sb[:], in_=bias.rearrange("(n p) -> p n", p=P))
-        cast_w1_both(0)
-        for b in range(2):
-            load_w4(b, f"weighed1{b}")
-        feed(3, ring[-2:])
-        load_offers(1, "space_h")
-        add_turned(0, 0, 0)
-        add_turned(0, 0, 1)
-        cast_w1_both(1)
         feed(4)
+        open_sums(0, 0)
+        close_sums(0)
+        place(4)
         feed(5)
-        low_sums = tenant("a1_5", "low_sums", [P, 2, T2], F32)
-        add_page(4, low_sums)
-        add_page(5, low_sums)
-        add_turned(0, 0, 2)
-        add_turned(0, 0, 3)
-        add_turned(0, 1, 0)
-        add_turned(0, 1, 1)
-        feed(6)
-        add_turned(0, 1, 2)
-        add_turned(0, 1, 3)
+        place(5)
         for b in range(2):
-            quantize_w4(b, tenant(f"weighed1{2 + b}", f"w4_grouped{b}", [P, PACK * N], BF16)[:])
-        add_page(6, offers_sb[1])
-        last = SLICES - 1
-        turn_a23(last, ring_bank())
+            quantize_w4(b, f"weighed1{b}", nc.scalar.copy)
+        open_sums(0, 1)
+        feed(6)
+        close_sums(1)
+        place(6)
+        open_sums(1, 0)
         for c in range(CHUNKS):
-            turn_back(0, c, 2)
+            turn_back(0, c, ring_bank())
             quantize_z(0, c)
-            if c == 1:
-                affinity1(last, ring_bank())
-                place(last)
-        late_grouped = tenant("woven1", "z_grouped1", [P, CHUNKS, CHUNK * PACK], BF16)
-        z_grouped.append([late_grouped[:, c, :] for c in range(CHUNKS)])
+        feed(7)
+        add_page(0, slice(0, T2))
+        close_sums(0)
         for c in range(CHUNKS):
-            weave_z(c, low_sums, slice(0, 2))
+            turn_back(1, c, ring_bank(), 1)
+        place(7)
         score_banks = [banks[4:6], banks[6:8], ring[-4:-2], ring[-2:]]
         for c in range(CHUNKS):
+            add_page(1, slice(CHUNK * c, CHUNK * (c + 1)))
             score_pass(0, c, score_banks[c])
         for c in range(CHUNKS):
-            add_page(last, offers_sb[1], slice(CHUNK * c, CHUNK * (c + 1)))
-        for c in range(CHUNKS):
-            weave_z(c, offers_sb[1], slice(2, PACK))
+            weave_last(c)
         for c in range(CHUNKS):
             quantize_z(1, c)
             store_scores(c, score_pass(1, c, score_banks[c]))

@@ -66,15 +66,14 @@ def tile_list_bundle_offer_scores_kernel(
         low_s = held("low_s", [P, S], U8)
         w3_s = held("w3_s", [P, 2 * H], U8)
         w2_s = held("w2_s", [P, 2 * H], U8)
-        pages = [held(f"page{s}", [P, T2], F32) for s in range(PAGES)]
+        pages = [held(f"page{s}", [P, T2], F32) for s in range(2)]
         ident = held("ident", [P, P], F32)
         tab_w, w1_raw, offers_sb, w2_w, w3_w, w4_raw = {}, {}, {}, {}, {}, {}
 
         for plane in (tab_s, w3_s, w2_s, low_s):
             nc.vector.memset(plane[:].bitcast(I32), 0)
         for page in pages:
-            nc.vector.memset(page[:, 1:], 0.0)
-            nc.vector.memset(page[:, :1], 0.0)
+            nc.vector.memset(page[:], 0.0)
 
         def load_scale_rows(queue, plane, first_row, scales):
             for r in range(4):
@@ -115,13 +114,16 @@ def tile_list_bundle_offer_scores_kernel(
         nc.sync.dma_start(picks[:], offs)
         nc.sync.dma_start(cells[:], offs2)
         load_tab(0, 7)
-        load_w3(0, landed(56, "w3_w0", [P, 2 * PASS], I32)[:])
-        load_tab(1, 29)
-        load_scale_rows(nc.scalar, w3_s, W3_ROW, w3_scales)
+        wgs_rows = landed(44, "wgs_rows", [P, P], F32)
+        nc.sync.dma_start(out=wgs_rows[:], in_=wgs[0:P:J_TILES, :].rearrange("m (jt c) -> m jt c", jt=J_TILES))
+        load_tab(1, 83)
+        load_w3(0, landed(22, "w3_w0", [P, 2 * PASS], I32)[:])
+        load_w2(0, landed(42, "w2_w0", [P, PASS], I32)[:])
         for q in range(4):
-            nc.gpsimd.dma_start(out=tab_s[32 * q : 32 * q + 8, :].bitcast(I32),
+            nc.scalar.dma_start(out=tab_s[32 * q : 32 * q + 8, :].bitcast(I32),
                                 in_=tab_scales[:, 4 * q : 4 * q + 4, :].bitcast(I32))
         make_identity(nc, ident[:])
+        load_scale_rows(nc.gpsimd, w3_s, W3_ROW, w3_scales)
         load_scale_rows(nc.gpsimd, w2_s, 0, w2_scales)
 
         got_w = [held("got_w0", [P, S], U32)]
@@ -132,9 +134,6 @@ def tile_list_bundle_offer_scores_kernel(
             nc.vector.tensor_copy(got_w[a][:], tab_w[a][:].bitcast(U32).indirect(picks[:]))
 
         gather_words(0)
-        load_w2(0, landed(8, "w2_w0", [P, PASS], I32)[:])
-        wgs_rows = landed(10, "wgs_rows", [P, P], F32)
-        nc.sync.dma_start(out=wgs_rows[:], in_=wgs[0:P:J_TILES, :].rearrange("m (jt c) -> m jt c", jt=J_TILES))
         load_w1(0, 0, 0)
         load_w1(0, 1, 14)
         nc.vector.tensor_copy(got_both[:], tab_s[:].indirect(picks[:]))
@@ -142,6 +141,9 @@ def tile_list_bundle_offer_scores_kernel(
             nc.scalar.dma_start(out=low_s[r:P:32, :].bitcast(I32), in_=got_both[4 + r : P : 32, :].bitcast(I32))
         got_w.append(tenant("tab_s", "got_w1", [P, S], U32))
         gather_words(1)
+        pages.extend([landed(83, "page2", [P, T2], F32), landed(87, "page3", [P, T2], F32)])
+        for page in pages[2:]:
+            nc.vector.memset(page[:], 0.0)
 
         wgs_cols = held("wgs_cols", [P, GROUPS, J_TILES], F32)
         nc.tensor.transpose(banks[7][:, :P], wgs_rows[:], ident[:])
@@ -155,11 +157,12 @@ def tile_list_bundle_offer_scores_kernel(
             src = w1_raw[b, a][:].rearrange("p j (m i) -> p m j i", i=PACK)[:, :, :, 2 * half : 2 * half + 2]
             cast(out=grouped.rearrange("p (i m j) -> p m j i", i=2, j=PACK), in_=src)
 
-        def cast_w1(b, a, half, cast, slot):
-            grouped = placed(slot, f"w1_grouped{b}{a}{half}", [P, 2 * PASS], BF16)
-            group_w1(b, a, half, cast, grouped[:])
+        def cast_w1(b, a, half, cast, kib, span=2):
+            space = landed(kib, f"w1_grouped{b}{a}{half}", [P, span * PASS], BF16)
+            grouped = space[:, : 2 * PASS]
+            group_w1(b, a, half, cast, grouped)
             nc.vector.quantize_mx(out=w1_codes[2 * b + half][:, a, :].bitcast(FP8X4),
-                                  scales=w1_scales[2 * b + half][:, a, :], in_=grouped[:])
+                                  scales=w1_scales[2 * b + half][:, a, :], in_=grouped)
 
         def cast_w1_both(half, slot):
             grouped = placed(slot, f"w1_grouped1{half}", [P, 2, 2 * PASS], BF16)
@@ -171,8 +174,8 @@ def tile_list_bundle_offer_scores_kernel(
 
         a3_wgs = {}
         a23_t = [held(f"a23_t{b}", [P, J_TILES, PASS], F32) for b in range(2)]
-        a23 = [landed(66, "a23_0", [P, S], F32)] + [held(f"a23_{s}", [P, S], F32) for s in range(1, SLICES)]
-        a1 = [landed(74, "a1_0", [P, S], F32)] + [held(f"a1_{s}", [P, S], F32) for s in range(1, SLICES)]
+        a23 = [landed(68, "a23_0", [P, S], F32)] + [held(f"a23_{s}", [P, S], F32) for s in range(1, SLICES)]
+        a1 = [landed(76, "a1_0", [P, S], F32)] + [held(f"a1_{s}", [P, S], F32) for s in range(1, SLICES)]
 
         def turned_pass(bank, jt, a, table_scales, codes, scales):
             cols = slice(P * jt, P * (jt + 1))
@@ -189,7 +192,7 @@ def tile_list_bundle_offer_scores_kernel(
             turned_pass(bank, jt, a, low_s if a else got_both, w2_w[b][:, a, :].bitcast(FP4X4), w2_s[:, H * a + PASS * b : H * a + PASS * (b + 1)])
 
         def weigh_a3(b, jt, bank):
-            a3_wgs[b, jt] = placed({(0, 0): 37, (0, 2): 49}.get((b, jt), f"weighed{b}{jt}"), f"a3_wgs{b}{jt}", [P, GROUPS, PACK, GROUP_ROWS], F32)
+            a3_wgs[b, jt] = placed({(0, 0): 49}.get((b, jt), f"weighed{b}{jt}"), f"a3_wgs{b}{jt}", [P, GROUPS, PACK, GROUP_ROWS], F32)
             rows = bank[:].rearrange("j (g m i) -> j g i m", g=GROUPS, i=PACK)
             for g in range(GROUPS):
                 nc.scalar.activation(
@@ -270,15 +273,21 @@ def tile_list_bundle_offer_scores_kernel(
                 in_=halves.rearrange("p u t -> p t u"),
             )
 
-        def add_page(e, cols):
-            rows = offers_sb[1, 1][:, e, cols]
-            nc.vector.tensor_tensor(rows, rows, pages[2 + e][:, cols], ADD)
+        def add_page(u, e, cols):
+            rows = offers_sb[1, u][:, e, cols]
+            nc.vector.tensor_tensor(rows, rows, pages[2 * u + e][:, cols], ADD)
 
-        def weave_last(c):
+        def weave(u, c):
             nc.scalar.copy(
-                out=z_grouped[1][c][:].rearrange("p (t i) -> p t i", i=PACK)[:, :, 2:],
-                in_=offers_sb[1, 1][:, :, CHUNK * c : CHUNK * (c + 1)].rearrange("p i t -> p t i"),
+                out=z_grouped[1][c][:].rearrange("p (t i) -> p t i", i=PACK)[:, :, 2 * u : 2 * u + 2],
+                in_=offers_sb[1, u][:, :, CHUNK * c : CHUNK * (c + 1)].rearrange("p i t -> p t i"),
             )
+
+        def add_last(c):
+            cols = slice(CHUNK * c, CHUNK * (c + 1))
+            nc.vector.tensor_tensor(
+                z_grouped[1][c][:].rearrange("p (t i) -> p t i", i=PACK)[:, :, PACK - 1],
+                offers_sb[1, 1][:, 1, cols], pages[PAGES - 1][:, cols], ADD)
 
         def quantize_z(b, c, slot=None):
             z_codes[b, c] = tenant(slot or f"z_codes{b}{c}", f"z_codes{b}{c}", [P, CHUNK], U32)
@@ -311,7 +320,7 @@ def tile_list_bundle_offer_scores_kernel(
 
         def store_scores(c, slots):
             for n in range(N_TILES):
-                if c % 2 == 0 or (c == CHUNKS - 1 and n == N_TILES - 1):
+                if c >= 2 and (c + n) % 2 == 0:
                     nc.vector.tensor_scalar_add(results[c][:, n, :], slots[n], bias_sb[:, n : n + 1])
                 else:
                     nc.scalar.activation(out=results[c][:, n, :], in_=slots[n], func=IDENT, bias=bias_sb[:, n : n + 1])
@@ -332,24 +341,24 @@ def tile_list_bundle_offer_scores_kernel(
                 pass3(0, jt, a, banks[jt])
         for jt in range(J_TILES):
             weigh_a3(0, jt, banks[jt])
+        cast_w1(0, 0, 0, nc.vector.tensor_copy, 37)
+        load_w1(1, 0, 30)
         for jt in range(J_TILES):
             affinity2(0, jt, banks[RING + jt])
-        load_w1(1, 0, 30)
-        cast_w1(0, 0, 0, nc.scalar.copy, 38)
-        cast_w1(0, 1, 0, nc.vector.tensor_copy, 49)
+        cast_w1(0, 1, 0, nc.scalar.copy, 49, 10)
         turn_a23(0, banks[0])
         affinity1(0, banks[RING])
-        cast_w1(0, 0, 1, nc.vector.tensor_copy, "weighed03")
-        cast_w1(0, 1, 1, nc.scalar.copy, "weighed01")
+        load_w3(1, landed(49, "w3_w1", [P, 2 * PASS], I32)[:])
+        load_w2(1, landed(53, "w2_w1", [P, PASS], I32)[:])
+        cast_w1(0, 0, 1, nc.vector.tensor_copy, 55)
+        cast_w1(0, 1, 1, nc.vector.tensor_copy, 57)
         place(0)
-        load_w3(1, landed(17, "w3_w1", [P, 2 * PASS], I32)[:])
-        load_w2(1, landed(15, "w2_w1", [P, PASS], I32)[:])
-        load_w1(1, 1, 21)
-        load_offers(0, 0, 42)
-        load_w4(0, 50)
-        load_w4(1, 62)
-        load_offers(0, 1, 68)
-        affinity1(1, banks[0])
+        load_w1(1, 1, 14)
+        load_offers(0, 0, 55)
+        load_w4(0, 69)
+        load_w4(1, 63)
+        load_offers(0, 1, 75)
+        affinity1(1, banks[RING + 1])
         turn_a23(1, banks[RING])
         place(1)
         for jt in range(J_TILES):
@@ -361,7 +370,7 @@ def tile_list_bundle_offer_scores_kernel(
         feed(3)
         place(3)
         cast_w1_both(1, "w1_scales0")
-        load_offers(1, 0, 21)
+        load_offers(1, 0, 14)
         load_offers(1, 1, 30)
         bias_sb = tenant("weighed12", "bias_sb", [P, N_TILES], F32)
         with nc.allow_non_contiguous_dma(reason="one bias value for each partition and output tile"):
@@ -383,17 +392,17 @@ def tile_list_bundle_offer_scores_kernel(
             turn_back(0, c, ring_bank())
             quantize_z(0, c)
         feed(7)
-        add_page(0, slice(0, T2))
         close_sums(0)
+        open_sums(1, 1, 1)
+        turn_rows(pages[2][:], 0, False, True)
         for c in range(CHUNKS):
-            turn_back(1, c, ring_bank(), 1)
+            round_sums(1, c, 1)
+            turn_back(1, c, ring_bank())
         place(7)
         score_banks = [banks[4:6], banks[6:8], ring[-4:-2], ring[-2:]]
         for c in range(CHUNKS):
-            add_page(1, slice(CHUNK * c, CHUNK * (c + 1)))
             score_pass(0, c, score_banks[c])
         for c in range(CHUNKS):
-            weave_last(c)
-        for c in range(CHUNKS):
+            add_last(c)
             quantize_z(1, c)
             store_scores(c, score_pass(1, c, score_banks[c]))

@@ -174,7 +174,7 @@ def tile_list_bundle_offer_scores_kernel(
 
         a3_wgs = {}
         a23_t = [held(f"a23_t{b}", [P, J_TILES, PASS], F32) for b in range(2)]
-        a23 = [landed(68, "a23_0", [P, S], F32)] + [held(f"a23_{s}", [P, S], F32) for s in range(1, SLICES)]
+        a23 = [landed(68, "a23_0", [P, S], F32)] + [tenant(f"a23_{s}", f"a23_{s}", [P, S], F32) for s in range(1, SLICES)]
         a1 = [landed(76, "a1_0", [P, S], F32)] + [held(f"a1_{s}", [P, S], F32) for s in range(1, SLICES)]
 
         def turned_pass(bank, jt, a, table_scales, codes, scales):
@@ -296,31 +296,36 @@ def tile_list_bundle_offer_scores_kernel(
         w4_codes = held("w4_codes", [P, 2 * N], U32)
         w4_scales = held("w4_scales", [P, 2 * N], U8)
 
-        def quantize_w4(b, slot, cast):
-            grouped = tenant(slot, f"w4_grouped{b}", [P, PACK * N], BF16)
+        w4_grouped = {}
+
+        def cast_w4(b, slot, cast):
+            grouped = placed(slot, f"w4_grouped{b}", [P, PACK * N], BF16)
             cast(
                 out=grouped[:].rearrange("p (c n i) -> p c i n", n=4, i=PACK),
                 in_=w4_raw[b][:].rearrange("p i (c n) -> p c i n", n=4),
             )
+            w4_grouped[b] = grouped
+
+        def quantize_w4(b):
             cols = slice(N * b, N * (b + 1))
-            nc.vector.quantize_mx(out=w4_codes[:, cols].bitcast(FP8X4), scales=w4_scales[:, cols], in_=grouped[:])
+            nc.vector.quantize_mx(out=w4_codes[:, cols].bitcast(FP8X4), scales=w4_scales[:, cols], in_=w4_grouped[b][:])
 
         results = [held(f"result{c}", [P, N_TILES, CHUNK], F32) for c in range(CHUNKS)]
 
-        def score_pass(b, c, pair):
+        def score_pass(b, c, pair, first):
             slots = [pair[0][:, :CHUNK], pair[0][:, CHUNK:], pair[1][:, :CHUNK]]
             for n in range(N_TILES):
                 cols = slice(N * b + P * n, N * b + P * (n + 1))
                 nc.tensor.matmul_mx(
                     out=slots[n], lhsT=w4_codes[:, cols].bitcast(FP8X4), lhsT_scale=w4_scales[:, cols],
                     rhs=z_codes[b, c][:].bitcast(FP8X4), rhs_scale=z_scales[b][c][:],
-                    start=(b == 0 and n != 1), stop=(b == 1 and n != 0),
+                    start=(first and n != 1), stop=(not first and n != 0),
                 )
             return slots
 
         def store_scores(c, slots):
             for n in range(N_TILES):
-                if c >= 2 and (c + n) % 2 == 0:
+                if c == 2 or (c == 3 and n == 2):
                     nc.vector.tensor_scalar_add(results[c][:, n, :], slots[n], bias_sb[:, n : n + 1])
                 else:
                     nc.scalar.activation(out=results[c][:, n, :], in_=slots[n], func=IDENT, bias=bias_sb[:, n : n + 1])
@@ -375,23 +380,27 @@ def tile_list_bundle_offer_scores_kernel(
         bias_sb = tenant("weighed12", "bias_sb", [P, N_TILES], F32)
         with nc.allow_non_contiguous_dma(reason="one bias value for each partition and output tile"):
             nc.sync.dma_start(out=bias_sb[:], in_=bias.rearrange("(n p) -> p n", p=P))
-        feed(4)
         open_sums(0, 0)
         close_sums(0)
+        feed(4)
         place(4)
+        open_sums(0, 1)
         feed(5)
         place(5)
-        for b in range(2):
-            quantize_w4(b, f"weighed1{b}", nc.scalar.copy)
-        open_sums(0, 1)
         feed(6)
         close_sums(1)
         place(6)
-        open_sums(1, 0)
+        affinity1(7, ring_bank())
+        cast_w4(0, 77, nc.scalar.copy)
+        cast_w4(1, 69, nc.vector.tensor_copy)
+        for b in range(2):
+            quantize_w4(b)
         for c in range(CHUNKS):
             turn_back(0, c, ring_bank())
-            quantize_z(0, c)
-        feed(7)
+            if c < 2:
+                quantize_z(0, c)
+        turn_a23(7, ring_bank())
+        open_sums(1, 0)
         close_sums(0)
         open_sums(1, 1, 1)
         turn_rows(pages[2][:], 0, False, True)
@@ -400,9 +409,13 @@ def tile_list_bundle_offer_scores_kernel(
             turn_back(1, c, ring_bank())
         place(7)
         score_banks = [banks[4:6], banks[6:8], ring[-4:-2], ring[-2:]]
-        for c in range(CHUNKS):
-            score_pass(0, c, score_banks[c])
+        for c in range(2):
+            score_pass(0, c, score_banks[c], True)
         for c in range(CHUNKS):
             add_last(c)
             quantize_z(1, c)
-            store_scores(c, score_pass(1, c, score_banks[c]))
+            slots = score_pass(1, c, score_banks[c], False)
+            if c < 2:
+                quantize_z(0, c + 2, f"z_grouped1{c}")
+                score_pass(0, c + 2, score_banks[c + 2], True)
+            store_scores(c, slots)

@@ -73,7 +73,8 @@ def tile_list_bundle_offer_scores_kernel(
         for plane in (tab_s, w3_s, w2_s, low_s):
             nc.vector.memset(plane[:].bitcast(I32), 0)
         for page in pages:
-            nc.vector.memset(page[:], 0.0)
+            nc.vector.memset(page[:, 1:], 0.0)
+            nc.vector.memset(page[:, :1], 0.0)
 
         def load_scale_rows(queue, plane, first_row, scales):
             for r in range(4):
@@ -113,9 +114,9 @@ def tile_list_bundle_offer_scores_kernel(
 
         nc.sync.dma_start(picks[:], offs)
         nc.sync.dma_start(cells[:], offs2)
-        load_tab(0, 7)
         wgs_rows = landed(44, "wgs_rows", [P, P], F32)
         nc.sync.dma_start(out=wgs_rows[:], in_=wgs[0:P:J_TILES, :].rearrange("m (jt c) -> m jt c", jt=J_TILES))
+        load_tab(0, 7)
         load_tab(1, 83)
         load_w3(0, landed(22, "w3_w0", [P, 2 * PASS], I32)[:])
         load_w2(0, landed(42, "w2_w0", [P, PASS], I32)[:])

@@ -258,19 +258,34 @@ def tile_list_bundle_offer_scores_kernel(
                 in_=sums[c].rearrange("t tt e p -> t tt p e")[:, :, :, :lanes],
             )
 
+        def turn_lane(rows, pair, start):
+            for block in range(T2 // P):
+                nc.tensor.matmul(pair[block // 4][:, P * (block % 4) : P * (block % 4 + 1)], rows[:, P * block : P * (block + 1)],
+                                 ident[:], start=(start and block % 4 == 0), stop=(not start and block % 4 == 3),
+                                 is_transpose=True)
+
+        def round_lane(c, pair):
+            nc.scalar.copy(
+                out=zt_words[1][c][:].bitcast(BF16).rearrange("t tt (p e) -> t tt p e", e=2)[:, :, :, 0],
+                in_=pair[c // 2][:, CHUNK * (c % 2) : CHUNK * (c % 2 + 1)].rearrange("t (tt p) -> t tt p", tt=2),
+            )
+
         def close_sums(u):
             for e in range(2):
                 turn_rows(pages[2 * u + e][:], e, False, e == 1)
             for c in range(CHUNKS):
                 round_sums(u, c, 2)
 
-        def turn_back(b, c, bank, pairs=2):
-            halves = bank[:, : pairs * CHUNK].rearrange("p (u t) -> p u t", u=pairs)
-            for u in range(pairs):
+        def turn_back(b, c, bank):
+            halves = bank[:].rearrange("p (u t) -> p u t", u=2)
+            for u in range(2):
                 for tt in range(2):
                     nc.tensor.transpose(halves[:, u, P * tt : P * (tt + 1)], zt_words[u][c][:, tt, :], ident[:])
+            return halves
+
+        def weave_back(b, c, halves):
             nc.scalar.copy(
-                out=z_grouped[b][c][:].bitcast(F32).rearrange("p (t u) -> p t u", u=2)[:, :, :pairs],
+                out=z_grouped[b][c][:].bitcast(F32).rearrange("p (t u) -> p t u", u=2),
                 in_=halves.rearrange("p u t -> p t u"),
             )
 
@@ -388,28 +403,34 @@ def tile_list_bundle_offer_scores_kernel(
         open_sums(0, 1)
         feed(5)
         place(5)
+        cast_w4(0, "w1_codes2", nc.scalar.copy)
         feed(6)
         close_sums(1)
         place(6)
         affinity1(7, ring_bank())
-        cast_w4(0, 77, nc.scalar.copy)
-        cast_w4(1, 69, nc.vector.tensor_copy)
+        cast_w4(1, "w1_codes3", nc.scalar.copy)
         for b in range(2):
             quantize_w4(b)
+        turned = []
         for c in range(CHUNKS):
-            turn_back(0, c, ring_bank())
+            if c == 2:
+                turn_a23(7, ring_bank())
+            turned.append(turn_back(0, c, ring_bank()))
             if c < 2:
+                weave_back(0, c, turned[c])
                 quantize_z(0, c)
-        turn_a23(7, ring_bank())
         open_sums(1, 0)
         close_sums(0)
-        open_sums(1, 1, 1)
-        turn_rows(pages[2][:], 0, False, True)
+        lane_banks = [ring_bank(), ring_bank()]
+        turn_lane(offers_sb[1, 1][:, 0, :], lane_banks, True)
+        turn_lane(pages[2][:], lane_banks, False)
         for c in range(CHUNKS):
-            round_sums(1, c, 1)
-            turn_back(1, c, ring_bank())
+            round_lane(c, lane_banks)
+            weave_back(1, c, turn_back(1, c, banks[RING + c]))
+        for c in range(2, CHUNKS):
+            weave_back(0, c, turned[c])
         place(7)
-        score_banks = [banks[4:6], banks[6:8], ring[-4:-2], ring[-2:]]
+        score_banks = [lane_banks, banks[RING : RING + 2], ring[-4:-2], banks[RING + 2 :]]
         for c in range(2):
             score_pass(0, c, score_banks[c], True)
         for c in range(CHUNKS):

from contextlib import ExitStack

import concourse.mybir as mybir
from concourse.masks import make_identity

K, T, S, T2, H, N = 1024, 2048, 512, 1024, 1024, 384
FLOPS = 3 * 2 * K * H * S + 2 * H * N * T2

F32 = mybir.dt.float32
BF16 = mybir.dt.bfloat16
I32 = mybir.dt.int32
U32 = mybir.dt.uint32
U16 = mybir.dt.uint16
U8 = mybir.dt.uint8
FP8X4 = mybir.dt.float8_e4m3fn_x4
FP4X4 = mybir.dt.float4_e2m1fn_x4
MULT = mybir.AluOpType.mult
ADD = mybir.AluOpType.add
IDENT = mybir.ActivationFunctionType.Identity
COPY = mybir.ActivationFunctionType.Copy

P = 128
PACK = 4
PASS = P * PACK
GROUPS = 8
GROUP_ROWS = P // GROUPS
J_TILES = S // P
CHUNK = 256
CHUNKS = T2 // CHUNK
N_TILES = N // P
SLICES = 2 * PACK
PAGES = 4
RING = 4
TAB_ROWS = (0, 4)
W3_ROW = 12
KIB = 1024


def tile_list_bundle_offer_scores_kernel(
    tc, tab_words, tab_scales, offs, w1, w2_words, w2_scales, w3_words, w3_scales,
    wgs, offs2, offers, w4, bias, out,
):
    nc = tc.nc
    with ExitStack() as ctx:
        keep = ctx.enter_context(tc.tile_pool(name="keep", bufs=1))
        landing = ctx.enter_context(tc.tile_pool(name="landing", bufs=1))
        psum = ctx.enter_context(tc.psum_pool(name="psum", bufs=1))

        def held(name, shape, dtype):
            return keep.tile(shape, dtype, name=name, align_bytes=64)

        def tenant(slot, name, shape, dtype):
            return keep.tile(shape, dtype, name=name, tag=slot, align_bytes=64)

        def landed(kib, name, shape, dtype):
            return landing.tile(shape, dtype, name=name, offset=int(kib * KIB), align_bytes=64)

        def placed(where, name, shape, dtype):
            return (tenant if isinstance(where, str) else landed)(where, name, shape, dtype)

        banks = [psum.tile([P, PASS], F32, name=f"bank{n}") for n in range(8)]

        picks = keep.tile([P, S // 16], U16, name="picks")
        cells = keep.tile([P, S // 16], U16, name="cells")
        tab_s = tenant("tab_s", "tab_s", [P, T], U8)
        low_s = held("low_s", [P, S], U8)
        w3_s = held("w3_s", [P, 2 * H], U8)
        w2_s = held("w2_s", [P, 2 * H], U8)
        pages = [held(f"page{s}", [P, T2], F32) for s in range(2)]
        ident = held("ident", [P, P], F32)
        tab_w, w1_raw, offers_sb, w2_w, w3_w, w4_raw = {}, {}, {}, {}, {}, {}

        for plane in (tab_s, w3_s, w2_s, low_s):
            nc.vector.memset(plane[:].bitcast(I32), 0)
        for page in pages:
            nc.vector.memset(page[:, 1:], 0.0)
            nc.vector.memset(page[:, :1], 0.0)

        def load_scale_rows(queue, plane, first_row, scales):
            for r in range(4):
                rows = scales[:, r:16:4, :].rearrange("a q c -> q a c")
                queue.dma_start(
                    out=plane[first_row + r : P : 32, :].bitcast(I32).rearrange("q (a c) -> q a c", a=2),
                    in_=rows.bitcast(I32))

        def load_tab(a, kib):
            tab_w[a] = landed(kib, f"tab_w{a}", [P, T], I32)
            nc.sync.dma_start(out=tab_w[a][:], in_=tab_words[a].rearrange("p t i -> p (t i)").bitcast(I32))

        def load_w1(b, a, kib):
            rows = w1[PASS * a : PASS * (a + 1), PASS * b : PASS * (b + 1)]
            w1_raw[b, a] = landed(kib, f"w1_raw{b}{a}", [P, PACK, PASS], F32)
            nc.sync.dma_start(out=w1_raw[b, a][:], in_=rows.rearrange("(p j) c -> p j c", j=PACK))

        def load_w3(b, words):
            w3_w[b] = words.rearrange("p (a c) -> p a c", a=2)
            view = w3_words.rearrange("a p c i -> p a (c i)")[:, :, 4 * PASS * b : 4 * PASS * (b + 1)]
            nc.sync.dma_start(out=w3_w[b], in_=view.bitcast(I32))

        def load_w2(b, words):
            w2_w[b] = words.rearrange("p (a c) -> p a c", a=2)
            view = w2_words.rearrange("a p c -> p a c")[:, :, 2 * PASS * b : 2 * PASS * (b + 1)]
            nc.sync.dma_start(out=w2_w[b], in_=view.bitcast(I32))

        def load_offers(b, u, kib):
            rows = offers[PASS * b : PASS * (b + 1), :].rearrange("(p i) t -> p i t", i=PACK)
            offers_sb[b, u] = landed(kib, f"offers{b}{u}", [P, 2, T2], F32)
            nc.sync.dma_start(out=offers_sb[b, u][:], in_=rows[:, 2 * u : 2 * u + 2, :])

        def load_w4(b, kib):
            rows = w4[PASS * b : PASS * (b + 1), :].rearrange("(p i) n -> p i n", i=PACK)
            w4_raw[b] = landed(kib, f"w4_raw{b}", [P, PACK, N], F32)
            nc.sync.dma_start(out=w4_raw[b][:], in_=rows)

        nc.sync.dma_start(picks[:], offs)
        nc.sync.dma_start(cells[:], offs2)
        wgs_rows = landed(44, "wgs_rows", [P, P], F32)
        nc.sync.dma_start(out=wgs_rows[:], in_=wgs[0:P:J_TILES, :].rearrange("m (jt c) -> m jt c", jt=J_TILES))
        load_tab(0, 7)
        load_tab(1, 83)
        load_w3(0, landed(22, "w3_w0", [P, 2 * PASS], I32)[:])
        load_w2(0, landed(42, "w2_w0", [P, PASS], I32)[:])
        for q in range(4):
            nc.scalar.dma_start(out=tab_s[32 * q : 32 * q + 8, :].bitcast(I32),
                                in_=tab_scales[:, 4 * q : 4 * q + 4, :].bitcast(I32))
        make_identity(nc, ident[:])
        load_scale_rows(nc.gpsimd, w3_s, W3_ROW, w3_scales)
        load_scale_rows(nc.gpsimd, w2_s, 0, w2_scales)

        got_w = [held("got_w0", [P, S], U32)]
        got_both = held("got_both", [P, S], U8)
        got_s = [got_both[row:P, :] for row in TAB_ROWS]

        def gather_words(a):
            nc.vector.tensor_copy(got_w[a][:], tab_w[a][:].bitcast(U32).indirect(picks[:]))

        gather_words(0)
        load_w1(0, 0, 0)
        load_w1(0, 1, 14)
        nc.vector.tensor_copy(got_both[:], tab_s[:].indirect(picks[:]))
        for r in range(4):
            nc.scalar.dma_start(out=low_s[r:P:32, :].bitcast(I32), in_=got_both[4 + r : P : 32, :].bitcast(I32))
        got_w.append(tenant("tab_s", "got_w1", [P, S], U32))
        gather_words(1)
        pages.extend([landed(83, "page2", [P, T2], F32), landed(87, "page3", [P, T2], F32)])
        for page in pages[2:]:
            nc.vector.memset(page[:], 0.0)

        wgs_cols = held("wgs_cols", [P, GROUPS, J_TILES], F32)
        nc.tensor.transpose(banks[7][:, :P], wgs_rows[:], ident[:])
        nc.scalar.activation(
            out=wgs_cols[:], in_=banks[7][:, :P].rearrange("j (g m) -> j g m", g=GROUPS)[:, :, :J_TILES], func=COPY)

        w1_codes = [tenant(f"w1_codes{pair}", f"w1_codes{pair}", [P, 2, 2 * P], U32) for pair in range(4)]
        w1_scales = [tenant(f"w1_scales{pair}", f"w1_scales{pair}", [P, 2, 2 * P], U8) for pair in range(4)]

        def group_w1(b, a, half, cast, grouped):
            src = w1_raw[b, a][:].rearrange("p j (m i) -> p m j i", i=PACK)[:, :, :, 2 * half : 2 * half + 2]
            cast(out=grouped.rearrange("p (i m j) -> p m j i", i=2, j=PACK), in_=src)

        def cast_w1(b, a, half, cast, kib, span=2):
            space = landed(kib, f"w1_grouped{b}{a}{half}", [P, span * PASS], BF16)
            grouped = space[:, : 2 * PASS]
            group_w1(b, a, half, cast, grouped)
            nc.vector.quantize_mx(out=w1_codes[2 * b + half][:, a, :].bitcast(FP8X4),
                                  scales=w1_scales[2 * b + half][:, a, :], in_=grouped)

        def cast_w1_both(half, slot):
            grouped = placed(slot, f"w1_grouped1{half}", [P, 2, 2 * PASS], BF16)
            for a in range(2):
                group_w1(1, a, half, nc.scalar.copy, grouped[:, a, :])
            nc.vector.quantize_mx(
                out=w1_codes[2 + half][:].rearrange("p a c -> p (a c)").bitcast(FP8X4),
                scales=w1_scales[2 + half][:].rearrange("p a c -> p (a c)"), in_=grouped[:].rearrange("p a c -> p (a c)"))

        a3_wgs = {}
        a23_t = [held(f"a23_t{b}", [P, J_TILES, PASS], F32) for b in range(2)]
        a23 = [landed(68, "a23_0", [P, S], F32)] + [tenant(f"a23_{s}", f"a23_{s}", [P, S], F32) for s in range(1, SLICES)]
        a1 = [landed(76, "a1_0", [P, S], F32)] + [held(f"a1_{s}", [P, S], F32) for s in range(1, SLICES)]

        def turned_pass(bank, jt, a, table_scales, codes, scales):
            cols = slice(P * jt, P * (jt + 1))
            nc.tensor.matmul_mx(
                out=bank[:], lhsT=got_w[a][:, cols].bitcast(FP8X4), lhsT_scale=table_scales[:, cols],
                rhs=codes, rhs_scale=scales, start=(a == 0), stop=(a == 1),
            )

        def pass3(b, jt, a, bank):
            turned_pass(bank, jt, a, got_s[a], w3_w[b][:, a, :].bitcast(FP8X4),
                        w3_s[W3_ROW:P, H * a + PASS * b : H * a + PASS * (b + 1)])

        def pass2(b, jt, a, bank):
            turned_pass(bank, jt, a, low_s if a else got_both, w2_w[b][:, a, :].bitcast(FP4X4), w2_s[:, H * a + PASS * b : H * a + PASS * (b + 1)])

        def weigh_a3(b, jt, bank):
            a3_wgs[b, jt] = placed({(0, 0): 49}.get((b, jt), f"weighed{b}{jt}"), f"a3_wgs{b}{jt}", [P, GROUPS, PACK, GROUP_ROWS], F32)
            rows = bank[:].rearrange("j (g m i) -> j g i m", g=GROUPS, i=PACK)
            for g in range(GROUPS):
                nc.scalar.activation(
                    out=a3_wgs[b, jt][:, g], in_=rows[:, g], func=COPY, scale=wgs_cols[:, g, jt : jt + 1])

        def times_a2(b, jt, bank):
            nc.vector.tensor_tensor(
                a23_t[b][:, jt, :].rearrange("j (i g m) -> j i g m", i=PACK, g=GROUPS),
                bank[:].rearrange("j (g m i) -> j i g m", g=GROUPS, i=PACK),
                a3_wgs[b, jt][:].rearrange("j g i m -> j i g m"), MULT)

        def turn_a23(s, bank):
            b, i = divmod(s, PACK)
            for jt in range(J_TILES):
                nc.tensor.transpose(bank[:, P * jt : P * (jt + 1)], a23_t[b][:, jt, P * i : P * (i + 1)], ident[:])
            nc.scalar.copy(out=a23[s][:], in_=bank[:])

        def affinity1(s, bank):
            pair, e = divmod(s, 2)
            cols = slice(P * e, P * (e + 1))
            for a in range(2):
                nc.tensor.matmul_mx(
                    out=bank[:], lhsT=w1_codes[pair][:, a, cols].bitcast(FP8X4), lhsT_scale=w1_scales[pair][:, a, cols],
                    rhs=got_w[a][:].bitcast(FP8X4), rhs_scale=got_s[a], start=(a == 0), stop=(a == 1),
                )
            nc.scalar.copy(out=a1[s][:], in_=bank[:])

        def place(s):
            nc.vector.tensor_tensor(pages[s % PAGES][:].indirect(cells[:]), a1[s][:], a23[s][:], MULT)

        ring = []

        def ring_bank():
            ring.append(banks[(len(ring) + 1) % RING])
            return ring[-1]

        def feed(s):
            turn_a23(s, ring_bank())
            affinity1(s, ring_bank())

        z_grouped = [[tenant(f"z_grouped{b}{c}", f"z_grouped{b}{c}", [P, CHUNK * PACK], BF16) for c in range(CHUNKS)] for b in range(2)]
        z_codes = {}
        z_scales = [[held(f"z_scales{b}{c}", [P, CHUNK], U8) for c in range(CHUNKS)] for b in range(2)]
        zt_words = [[held(f"zt_words{u}{c}", [P, 2, P], F32) for c in range(CHUNKS)] for u in range(2)]

        sums = [bank[:].rearrange("t (tt e p) -> t tt e p", tt=2, e=2) for bank in banks[RING:]]

        def turn_rows(rows, e, start, stop):
            for c in range(CHUNKS):
                for tt in range(2):
                    t0 = CHUNK * c + P * tt
                    nc.tensor.matmul(sums[c][:, tt, e, :], rows[:, t0 : t0 + P], ident[:],
                                     start=(start and tt == 0), stop=(stop and tt == 1), is_transpose=True)

        def open_sums(b, u, lanes=2):
            for e in range(lanes):
                turn_rows(offers_sb[b, u][:, e, :], e, e == 0, False)

        def round_sums(u, c, lanes):
            nc.scalar.copy(
                out=zt_words[u][c][:].bitcast(BF16).rearrange("t tt (p e) -> t tt p e", e=2)[:, :, :, :lanes],
                in_=sums[c].rearrange("t tt e p -> t tt p e")[:, :, :, :lanes],
            )

        def turn_lane(rows, pair, start):
            for block in range(T2 // P):
                nc.tensor.matmul(pair[block // 4][:, P * (block % 4) : P * (block % 4 + 1)], rows[:, P * block : P * (block + 1)],
                                 ident[:], start=(start and block % 4 == 0), stop=(not start and block % 4 == 3),
                                 is_transpose=True)

        def round_lane(c, pair):
            nc.scalar.copy(
                out=zt_words[1][c][:].bitcast(BF16).rearrange("t tt (p e) -> t tt p e", e=2)[:, :, :, 0],
                in_=pair[c // 2][:, CHUNK * (c % 2) : CHUNK * (c % 2 + 1)].rearrange("t (tt p) -> t tt p", tt=2),
            )

        def close_sums(u):
            for e in range(2):
                turn_rows(pages[2 * u + e][:], e, False, e == 1)
            for c in range(CHUNKS):
                round_sums(u, c, 2)

        def turn_back(b, c, bank):
            halves = bank[:].rearrange("p (u t) -> p u t", u=2)
            for u in range(2):
                for tt in range(2):
                    nc.tensor.transpose(halves[:, u, P * tt : P * (tt + 1)], zt_words[u][c][:, tt, :], ident[:])
            return halves

        def weave_back(b, c, halves):
            nc.scalar.copy(
                out=z_grouped[b][c][:].bitcast(F32).rearrange("p (t u) -> p t u", u=2),
                in_=halves.rearrange("p u t -> p t u"),
            )

        def add_page(u, e, cols):
            rows = offers_sb[1, u][:, e, cols]
            nc.vector.tensor_tensor(rows, rows, pages[2 * u + e][:, cols], ADD)

        def weave(u, c):
            nc.scalar.copy(
                out=z_grouped[1][c][:].rearrange("p (t i) -> p t i", i=PACK)[:, :, 2 * u : 2 * u + 2],
                in_=offers_sb[1, u][:, :, CHUNK * c : CHUNK * (c + 1)].rearrange("p i t -> p t i"),
            )

        def add_last(c):
            cols = slice(CHUNK * c, CHUNK * (c + 1))
            nc.vector.tensor_tensor(
                z_grouped[1][c][:].rearrange("p (t i) -> p t i", i=PACK)[:, :, PACK - 1],
                offers_sb[1, 1][:, 1, cols], pages[PAGES - 1][:, cols], ADD)

        def quantize_z(b, c, slot=None):
            z_codes[b, c] = tenant(slot or f"z_codes{b}{c}", f"z_codes{b}{c}", [P, CHUNK], U32)
            nc.vector.quantize_mx(out=z_codes[b, c][:].bitcast(FP8X4), scales=z_scales[b][c][:], in_=z_grouped[b][c][:])

        w4_codes = held("w4_codes", [P, 2 * N], U32)
        w4_scales = held("w4_scales", [P, 2 * N], U8)

        w4_grouped = {}

        def cast_w4(b, slot, cast):
            grouped = placed(slot, f"w4_grouped{b}", [P, PACK * N], BF16)
            cast(
                out=grouped[:].rearrange("p (c n i) -> p c i n", n=4, i=PACK),
                in_=w4_raw[b][:].rearrange("p i (c n) -> p c i n", n=4),
            )
            w4_grouped[b] = grouped

        def quantize_w4(b):
            cols = slice(N * b, N * (b + 1))
            nc.vector.quantize_mx(out=w4_codes[:, cols].bitcast(FP8X4), scales=w4_scales[:, cols], in_=w4_grouped[b][:])

        results = [held(f"result{c}", [P, N_TILES, CHUNK], F32) for c in range(CHUNKS)]

        def score_pass(b, c, pair, first):
            slots = [pair[0][:, :CHUNK], pair[0][:, CHUNK:], pair[1][:, :CHUNK]]
            for n in range(N_TILES):
                cols = slice(N * b + P * n, N * b + P * (n + 1))
                nc.tensor.matmul_mx(
                    out=slots[n], lhsT=w4_codes[:, cols].bitcast(FP8X4), lhsT_scale=w4_scales[:, cols],
                    rhs=z_codes[b, c][:].bitcast(FP8X4), rhs_scale=z_scales[b][c][:],
                    start=(first and n != 1), stop=(not first and n != 0),
                )
            return slots

        def store_scores(c, slots):
            for n in range(N_TILES):
                if c == 2 or (c == 3 and n == 2):
                    nc.vector.tensor_scalar_add(results[c][:, n, :], slots[n], bias_sb[:, n : n + 1])
                else:
                    nc.scalar.activation(out=results[c][:, n, :], in_=slots[n], func=IDENT, bias=bias_sb[:, n : n + 1])
                nc.sync.dma_start(out=out[P * n : P * (n + 1), CHUNK * c : CHUNK * (c + 1)], in_=results[c][:, n, :])

        def affinity3(b, jt, bank):
            for a in range(2):
                pass3(b, jt, a, bank)
            weigh_a3(b, jt, bank)

        def affinity2(b, jt, bank):
            for a in range(2):
                pass2(b, jt, a, bank)
            times_a2(b, jt, bank)

        for a in range(2):
            for jt in range(J_TILES):
                pass3(0, jt, a, banks[jt])
        for jt in range(J_TILES):
            weigh_a3(0, jt, banks[jt])
        cast_w1(0, 0, 0, nc.vector.tensor_copy, 37)
        load_w1(1, 0, 30)
        for jt in range(J_TILES):
            affinity2(0, jt, banks[RING + jt])
        cast_w1(0, 1, 0, nc.scalar.copy, 49, 10)
        turn_a23(0, banks[0])
        affinity1(0, banks[RING])
        load_w3(1, landed(49, "w3_w1", [P, 2 * PASS], I32)[:])
        load_w2(1, landed(53, "w2_w1", [P, PASS], I32)[:])
        cast_w1(0, 0, 1, nc.vector.tensor_copy, 55)
        cast_w1(0, 1, 1, nc.vector.tensor_copy, 57)
        place(0)
        load_w1(1, 1, 14)
        load_offers(0, 0, 55)
        load_w4(0, 69)
        load_w4(1, 63)
        load_offers(0, 1, 75)
        affinity1(1, banks[RING + 1])
        turn_a23(1, banks[RING])
        place(1)
        for jt in range(J_TILES):
            affinity3(1, jt, ring_bank())
            affinity2(1, jt, banks[RING + jt])
        feed(2)
        place(2)
        cast_w1_both(0, "w1_codes0")
        feed(3)
        place(3)
        cast_w1_both(1, "w1_scales0")
        load_offers(1, 0, 14)
        load_offers(1, 1, 30)
        bias_sb = tenant("weighed12", "bias_sb", [P, N_TILES], F32)
        with nc.allow_non_contiguous_dma(reason="one bias value for each partition and output tile"):
            nc.sync.dma_start(out=bias_sb[:], in_=bias.rearrange("(n p) -> p n", p=P))
        open_sums(0, 0)
        close_sums(0)
        feed(4)
        place(4)
        open_sums(0, 1)
        feed(5)
        place(5)
        cast_w4(0, "w1_codes2", nc.scalar.copy)
        feed(6)
        close_sums(1)
        place(6)
        affinity1(7, ring_bank())
        cast_w4(1, "w1_codes3", nc.scalar.copy)
        for b in range(2):
            quantize_w4(b)
        turned = []
        for c in range(CHUNKS):
            if c == 2:
                turn_a23(7, ring_bank())
            turned.append(turn_back(0, c, ring_bank()))
            if c < 2:
                weave_back(0, c, turned[c])
                quantize_z(0, c)
        open_sums(1, 0)
        close_sums(0)
        lane_banks = [ring_bank(), ring_bank()]
        turn_lane(offers_sb[1, 1][:, 0, :], lane_banks, True)
        turn_lane(pages[2][:], lane_banks, False)
        for c in range(CHUNKS):
            round_lane(c, lane_banks)
            weave_back(1, c, turn_back(1, c, banks[RING + c]))
        for c in range(2, CHUNKS):
            weave_back(0, c, turned[c])
        place(7)
        score_banks = [lane_banks, banks[RING : RING + 2], ring[-4:-2], banks[RING + 2 :]]
        for c in range(2):
            score_pass(0, c, score_banks[c], True)
        for c in range(CHUNKS):
            add_last(c)
            quantize_z(1, c)
            slots = score_pass(1, c, score_banks[c], False)
            if c < 2:
                quantize_z(0, c + 2, f"z_grouped1{c}")
                score_pass(0, c + 2, score_banks[c + 2], True)
            store_scores(c, slots)
